import numpy as np
import ml_dtypes


def mxq(x, axis, fmt="e4m3"):
    dtype, down = {"e4m3": (ml_dtypes.float8_e4m3fn, 7), "e5m2": (ml_dtypes.float8_e5m2, 14)}[fmt]
    v = np.moveaxis(np.asarray(x, np.float32).astype(ml_dtypes.bfloat16).astype(np.float64), axis, -1)
    blocks = v.reshape(v.shape[:-1] + (-1, 32))
    amax = np.abs(blocks).max(-1, keepdims=True)
    byte = np.maximum(np.where(amax > 0, np.frexp(amax)[1] - 1 + 127, 0) - down, 1)
    scale = np.exp2(byte - 127.0)
    codes = (blocks / scale).astype(np.float32).astype(dtype).astype(np.float64)
    return np.moveaxis((codes * scale).reshape(v.shape), -1, axis)


WIDE = False


def mx_kscale(k):
    if not WIDE:
        return np.ones(k)
    levels = np.array([10, -10, 5, -5, 0])
    if k % 512:
        return np.exp2(np.random.permutation(np.resize(levels, k // 32))).repeat(32)
    a = np.empty((k // 512, 16))
    for p in range(k // 512):
        a[p, :8] = np.random.permutation(np.resize(levels, 8))
        for g in range(8):
            far = levels[np.abs(levels - a[p, g]) >= 10]
            a[p, g + 8] = far[np.random.randint(len(far))]
    return np.exp2(a.ravel()).repeat(32)


def f64(x):
    return np.asarray(x).astype(np.float64)


def striped(idx):
    return np.tile(idx.reshape(-1, 16).T, (8, 1)).astype(np.uint16)


def unstriped(offs):
    return offs[:16].T.reshape(-1).astype(np.int64)


def silu(v):
    return v / (1.0 + np.exp(-np.maximum(v, -700.0)))


K, T, E, C, H, N = 512, 512, 6, 256, 512, 384
TOP = 3


def by_expert(wq, xq):
    return np.concatenate([wq[e].T @ xq[:, e * C:(e + 1) * C] for e in range(E)], axis=1)


def setup_inputs():
    n = np.random.standard_normal
    s = mx_kscale(K)[:, None]
    u = mx_kscale(H)
    deal = np.repeat(np.arange(E), C).reshape(TOP, T)[:, np.random.permutation(T)]
    deal = np.take_along_axis(deal, np.argsort(np.random.rand(TOP, T), axis=0), axis=0)
    for _ in range(8):
        s_, t_ = np.random.permutation(T).reshape(2, -1); r = np.random.randint(TOP, size=T // 2); x, y = deal[r, s_].copy(), deal[r, t_].copy()
        ok = ~((deal[:, s_] == y).any(0) | (deal[:, t_] == x).any(0)); deal[r[ok], s_[ok]] = y[ok]; deal[r[ok], t_[ok]] = x[ok]
    order = np.lexsort((np.random.rand(TOP * T), deal.reshape(-1)))
    slot_token = order % T; pos = np.empty(TOP * T, np.int64); pos[order] = np.arange(TOP * T); pos = pos.reshape(TOP, T)
    g = np.random.uniform(0.5, 1.5, (TOP, T)); g = g / g.sum(0)
    return {
        "xT": (n((K, T)) * s).astype(np.float32),
        "w1": (n((E, K, H)) / np.sqrt(K) / s[None]).astype(np.float32),
        "w3": (n((E, K, H)) / np.sqrt(K) / s[None] * u[None, None, :]).astype(np.float32),
        "w2": (n((E, H, N)) / np.sqrt(H) / u[None, :, None]).astype(np.float32),
        "gate": np.stack([np.tile(r, (N, 1)) for r in g]).astype(np.float32),
        "offs": striped(slot_token),
        "pos1": striped(pos[0]),
        "pos2": striped(pos[1]),
        "pos3": striped(pos[2]),
    }


def reference(xT, w1, w3, w2, gate, offs, pos1, pos2, pos3):
    idx = unstriped(offs)
    xq = mxq(f64(xT)[:, idx], 0, "e4m3")
    h = silu(by_expert(mxq(f64(w1), 1, "e4m3"), xq))
    h = h * by_expert(mxq(f64(w3), 1, "e4m3"), xq)
    y = by_expert(mxq(f64(w2), 1, "e4m3"), mxq(h, 0, "e4m3"))
    return sum(f64(gate[r]) * y[:, unstriped(p)] for r, p in enumerate((pos1, pos2, pos3)))

@@ -1,0 +1,271 @@
+from contextlib import ExitStack
+
+import concourse.mybir as mybir
+
+K, T, E, C, H, N = 512, 512, 6, 256, 512, 384
+TOP = 3
+FLOPS = 2 * TOP * T * (2 * K * H + H * N)
+
+F32 = mybir.dt.float32
+BF16 = mybir.dt.bfloat16
+U32 = mybir.dt.uint32
+U16 = mybir.dt.uint16
+U8 = mybir.dt.uint8
+FP8X4 = mybir.dt.float8_e4m3fn_x4
+MULT = mybir.AluOpType.mult
+ADD = mybir.AluOpType.add
+SILU = mybir.ActivationFunctionType.Silu
+
+P = 128
+BLK = 128
+GATHER = 384
+S = E * C
+
+MS1 = [112, 128, 128, 128, 96, 112]
+MS3 = [128, 80, 32, 64, 48, 128]
+MSX = 32
+MSN = [[32, 32, 0], [8, 0, 32], [8, 16, 8]]
+LOADS = [('a', 0), ('b', 0), ('a', 1), ('b', 1), ('b', 2), ('a', 3), ('a', 2), ('b', 3), ('a', 4), ('b', 4), ('b', 5), ('c', 1), ('c', 0), ('a', 5), ('n', 5), ('c', 3), ('n', 2), ('c', 4), ('m', 5), ('m', 2), ('g', 0), ('g', 1), ('g', 2)]
+GATH = {0: [0, 1], 3: [2], 4: [3]}
+RING = 11
+GB = 3
+XPOS = 0
+ROOM = 'baaaa'
+YV = []
+PAIRS = [(0, 1), (2, 3), (4, 5)]
+HALVES = []
+YROOM = 0
+QA = 0
+ENDORD = 0
+LATE = []
+XH = 1
+
+
+def tile_moe_tk_glu_silu_kernel(tc, xT, w1, w3, w2, gate, offs, pos1, pos2, pos3, out):
+    nc = tc.nc
+    with ExitStack() as ctx:
+        lists = ctx.enter_context(tc.tile_pool(name="lists", bufs=1))
+        keep = ctx.enter_context(tc.tile_pool(name="keep", bufs=1))
+        ring = ctx.enter_context(tc.tile_pool(name="ring", bufs=RING))
+        work = ctx.enter_context(tc.tile_pool(name="work", bufs=2))
+        psum = ctx.enter_context(tc.psum_pool(name="psum", bufs=8))
+
+        offs_sb = lists.tile([P, S // 16], U16, name="offs_sb")
+        pos_sb = [lists.tile([P, T // 16], U16, name=f"pos_sb{r}") for r in range(TOP)]
+
+        xs = keep.tile([P, T], U8, name="xs", align_bytes=64)
+        nc.gpsimd.memset(xs[:], 0)
+        warm = keep.tile([P, 1], F32, name="warm")
+        nc.gpsimd.memset(warm[:], 0.0)
+        warm_out = keep.tile([P, 1], F32, name="warm_out")
+        nc.scalar.activation(warm_out[:], warm[:], SILU)
+
+        x_raw = []
+        raw, gates, pieces = {}, {}, {}
+        for n, (kind, e) in enumerate(LOADS):
+            if n == XPOS:
+                x_all = ring.tile([P, 4, T], F32, name="x_all", tag="raw")
+                for half in range(XH):
+                    xr = x_all[:, :, half * (T // XH) : (half + 1) * (T // XH)]
+                    nc.sync.dma_start(out=xr, in_=xT.rearrange("(p j) t -> p j t", j=4)[:, :, half * (T // XH) : (half + 1) * (T // XH)])
+                    x_raw.append(xr)
+                nc.sync.dma_start(offs_sb[:], offs)
+            if kind in "ab":
+                wr = ring.tile([P, 4, H], F32, name=f"raw_{kind}{e}", tag="raw")
+                src = (w1 if kind == "a" else w3)[e].rearrange("(p j) i -> p j i", j=4)
+                if (kind, e) in HALVES:
+                    nc.sync.dma_start(out=wr[:, :, 0:256], in_=src[:, :, 0:256])
+                    nc.sync.dma_start(out=wr[:, :, 256:512], in_=src[:, :, 256:512])
+                else:
+                    nc.sync.dma_start(out=wr[:], in_=src)
+                raw[kind, e] = wr
+            elif kind == "c":
+                wr = ring.tile([P, 4, N], F32, name=f"raw_c{e}", tag="raw")
+                nc.sync.dma_start(out=wr[:], in_=w2[e].rearrange("(p j) n -> p j n", j=4))
+                for r in range(3):
+                    raw[r, e] = wr[:, :, r * BLK : (r + 1) * BLK]
+            elif kind == "n":
+                pieces[e] = ring.tile([P, 4 * N], F32, name=f"raw_nm{e}", tag="raw")
+                wr = pieces[e][:, 0 : 4 * BLK].rearrange("p (j n) -> p j n", j=4)
+                nc.sync.dma_start(out=wr, in_=w2[e].rearrange("(p j) n -> p j n", j=4)[:, :, 0:BLK])
+                raw[0, e] = wr
+            elif kind == "m":
+                wr = pieces[e][:, 4 * BLK : 4 * N].rearrange("p (j n) -> p j n", j=4)
+                nc.sync.dma_start(out=wr, in_=w2[e].rearrange("(p j) n -> p j n", j=4)[:, :, BLK:N])
+                for r in range(2):
+                    raw[r + 1, e] = wr[:, :, r * BLK : (r + 1) * BLK]
+            else:
+                if e == 0:
+                    for k, src in enumerate((pos1, pos2, pos3)):
+                        nc.sync.dma_start(pos_sb[k][:], src)
+                gt = ring.tile([P, TOP, T], F32, name=f"gate{e}", tag="raw")
+                nc.sync.dma_start(out=gt[:], in_=gate[:, e * BLK : (e + 1) * BLK, :].rearrange("g p t -> p g t"))
+                gates[e] = gt
+
+        def split_copy(dst, src, ms, total):
+            if ms:
+                nc.scalar.copy(dst[:, 0:ms], src[:, 0:ms])
+            if ms < total:
+                nc.vector.tensor_copy(dst[:, ms:total], src[:, ms:total])
+
+        xg = keep.tile([P, T, 4], BF16, name="xg", align_bytes=64)
+        xv = xg[:].rearrange("p (c i) j -> p c j i", i=4)
+        w = T // 4 // XH
+        for half in range(XH):
+            split_copy(xv[:, half * w : (half + 1) * w], x_raw[half].rearrange("p j (c i) -> p c j i", i=4), MSX * w // 64, w)
+        xw = keep.tile([P, T], U32, name="xw", align_bytes=64)
+        nc.vector.quantize_mx(out=xw[:].bitcast(FP8X4), scales=xs[:], in_=xg[:].rearrange("p t j -> p (t j)"))
+
+        gw, gs = {}, {}
+
+        def gather(b):
+            cols = slice(b * GATHER // 16, (b + 1) * GATHER // 16)
+            gw[b] = work.tile([P, GATHER], U32, name=f"gw{b}", tag="gw", align_bytes=64, bufs=GB)
+            nc.vector.tensor_copy(gw[b][:], xw[:].indirect(offs_sb[:, cols]))
+            gs[b] = work.tile([P, GATHER], U8, name=f"gs{b}", tag="gs", align_bytes=64, bufs=GB)
+            nc.vector.tensor_copy(gs[b][:], xs[:].indirect(offs_sb[:, cols]))
+
+        def moving(blk):
+            b, o = divmod(blk * BLK, GATHER)
+            return gw[b][:, o : o + BLK].bitcast(FP8X4), gs[b][:, o : o + BLK]
+
+        grouped, codes, hb, hw, hs = {}, {}, {}, {}, {}
+        w2g, w2w, w2s = {}, {}, {}
+
+        def copy_w13(e, i):
+            kind, ms = (("a", MS1[e]), ("b", MS3[e]))[i]
+            grouped[e, i] = work.tile([P, 4 * H], BF16, name=f"grp_{kind}{e}", tag="grp", align_bytes=64, bufs=4)
+            split_copy(grouped[e, i][:].rearrange("p (t m j) -> p m j t", t=4, j=4), raw[kind, e][:].rearrange("p j (m t) -> p m j t", t=4), ms, 128)
+
+        def quantize_w13(e, i):
+            cw = work.tile([P, H], U32, name=f"cw{e}_{i}", tag="cw", align_bytes=64, bufs=4)
+            cs = work.tile([P, H], U8, name=f"cs{e}_{i}", tag="cs", align_bytes=64, bufs=4)
+            nc.vector.quantize_mx(out=cw[:].bitcast(FP8X4), scales=cs[:], in_=grouped[e, i][:])
+            codes[e, i] = (cw, cs)
+
+        banks = {}
+
+        def hidden(e):
+            for c in range(2):
+                rw, rs = moving(2 * e + c)
+                for i in range(2):
+                    cw, cs = codes[e, i]
+                    bank = psum.tile([P, 4, BLK], F32, name=f"bank_{i}_{e}_{c}", tag="bank")
+                    for t in range(4):
+                        sl = slice(t * BLK, (t + 1) * BLK)
+                        nc.tensor.matmul_mx(out=bank[:, t, :], lhsT=cw[:, sl].bitcast(FP8X4), lhsT_scale=cs[:, sl], rhs=rw, rhs_scale=rs, start=True, stop=True)
+                    banks[e, i, c] = bank
+
+        def activate(e):
+            hb[e] = work.tile([P, C, 4], BF16, name=f"hb{e}", tag="hb", align_bytes=64)
+            if e + 1 < E:
+                room = raw[ROOM[e], e + 1]
+            else:
+                room = work.tile([P, 2, H], F32, name="room", tag="room", align_bytes=64, bufs=1)
+            for c in range(2):
+                sil = room[:, c, :].rearrange("p (c t) -> p c t", t=4)
+                nc.scalar.activation(sil, banks[e, 0, c][:].rearrange("p t c -> p c t"), SILU)
+                nc.vector.tensor_tensor(hb[e][:, c * BLK : (c + 1) * BLK, :], banks[e, 1, c][:].rearrange("p t c -> p c t"), sil, MULT)
+
+        def quantize_h(e):
+            hw[e] = keep.tile([P, C], U32, name=f"hw{e}", align_bytes=64)
+            hs[e] = keep.tile([P, C], U8, name=f"hs{e}", align_bytes=64)
+            nc.vector.quantize_mx(out=hw[e][:].bitcast(FP8X4), scales=hs[e][:], in_=hb[e][:].rearrange("p c t -> p (c t)"))
+
+        late = []
+
+        def copy_w2(r, q):
+            if (r, q) in LATE:
+                if not late:
+                    late.append(work.tile([P, 6, 2, BLK, 4], BF16, name="late", tag="room", align_bytes=64, bufs=1))
+                w2g[r, q] = late[0][:, 3 * (r - 1) + q]
+            else:
+                w2g[r, q] = keep.tile([P, 2, BLK, 4], BF16, name=f"grp2_{r}_{q}", align_bytes=64)[:]
+            for u in range(2):
+                split_copy(w2g[r, q][:, u].rearrange("p (c i) j -> p c j i", i=4), raw[r, PAIRS[q][u]].rearrange("p j (c i) -> p c j i", i=4), MSN[r][q], 32)
+
+        def quantize_w2(r, q):
+            w2w[r, q] = keep.tile([P, 2, BLK], U32, name=f"w2w{r}_{q}", align_bytes=64)
+            w2s[r, q] = keep.tile([P, 2, BLK], U8, name=f"w2s{r}_{q}", align_bytes=64)
+            nc.vector.quantize_mx(out=w2w[r, q][:].rearrange("p u n -> p (u n)").bitcast(FP8X4), scales=w2s[r, q][:].rearrange("p u n -> p (u n)"), in_=w2g[r, q].rearrange("p u n j -> p (u n j)"))
+
+        ys = {}
+
+        def project(r):
+            if r == 0 and YROOM:
+                ys[r] = work.tile([P, S], F32, name=f"y{r}", tag="room", align_bytes=64, bufs=1)
+            else:
+                ys[r] = keep.tile([P, S], F32, name=f"y{r}")
+            for q in range(3):
+                bank = psum.tile([P, 2, C], F32, name=f"bank_y{r}_{q}", tag="bank")
+                for u in range(2):
+                    e = PAIRS[q][u]
+                    nc.tensor.matmul_mx(out=bank[:, u, :], lhsT=w2w[r, q][:, u].bitcast(FP8X4), lhsT_scale=w2s[r, q][:, u], rhs=hw[e][:].bitcast(FP8X4), rhs_scale=hs[e][:], start=True, stop=True)
+                e0, e1 = PAIRS[q]
+                dst = ys[r][:].rearrange("p (e c) -> p e c", c=C)[:, e0 : e1 + 1 : e1 - e0]
+                if (r, q) in YV:
+                    nc.vector.tensor_copy(dst, bank[:])
+                else:
+                    nc.scalar.copy(dst, bank[:])
+
+        prods, sums, outs = {}, {}, {}
+
+        def fetch(r, k, t0=0, t1=T):
+            if (r, k) not in prods:
+                prods[r, k] = work.tile([P, T], F32, name=f"prod{r}_{k}", tag=f"prod{k}")
+            nc.vector.tensor_tensor(prods[r, k][:, t0:t1], ys[r][:].indirect(pos_sb[k][:, t0 // 16 : t1 // 16]), gates[r][:, k, t0:t1], MULT)
+
+        def add01(r):
+            sums[r] = work.tile([P, T], F32, name=f"sum{r}", tag="sum")
+            nc.vector.tensor_tensor(sums[r][:], prods[r, 0][:], prods[r, 1][:], ADD)
+
+        def add2(r, t0=0, t1=T):
+            if r not in outs:
+                outs[r] = work.tile([P, T], F32, name=f"o{r}", tag="o")
+            nc.vector.tensor_tensor(outs[r][:, t0:t1], sums[r][:, t0:t1], prods[r, 2][:, t0:t1], ADD)
+            nc.sync.dma_start(out=out[r * BLK : (r + 1) * BLK, t0:t1], in_=outs[r][:, t0:t1])
+
+        for e in range(E):
+            for b in GATH.get(e, []):
+                gather(b)
+            copy_w13(e, 0)
+            if not QA:
+                quantize_w13(e, 0)
+            if e > 0 and ROOM[e - 1] == "a":
+                activate(e - 1)
+                quantize_h(e - 1)
+            if QA:
+                quantize_w13(e, 0)
+            copy_w13(e, 1)
+            quantize_w13(e, 1)
+            if e > 0 and ROOM[e - 1] == "b":
+                activate(e - 1)
+                quantize_h(e - 1)
+            hidden(e)
+        activate(E - 1)
+        quantize_h(E - 1)
+        for r, q in [(r, q) for q in range(3) for r in range(3)] if ENDORD == 0 else [(r, q) for r in range(3) for q in range(3)]:
+            copy_w2(r, q)
+            quantize_w2(r, q)
+            if ENDORD == 2 and q == 2:
+                project(r)
+        if ENDORD < 2:
+            for r in range(3):
+                project(r)
+        fetch(0, 0)
+        fetch(0, 1)
+        fetch(0, 2)
+        add01(0)
+        fetch(1, 0)
+        add2(0)
+        fetch(1, 1)
+        fetch(1, 2)
+        add01(1)
+        fetch(2, 0)
+        add2(1)
+        fetch(2, 1)
+        fetch(2, 2, 0, 256)
+        add01(2)
+        fetch(2, 2, 256, 512)
+        add2(2, 0, 256)
+        add2(2, 256, 512)

@@ -18,27 +18,14 @@ SILU = mybir.ActivationFunctionType.Silu
 
 P = 128
 BLK = 128
-GATHER = 384
 S = E * C
-
-MS1 = [112, 128, 128, 128, 96, 112]
-MS3 = [128, 80, 32, 64, 48, 128]
-MSX = 32
-MSN = [[32, 32, 0], [8, 0, 32], [8, 16, 8]]
-LOADS = [('a', 0), ('b', 0), ('a', 1), ('b', 1), ('b', 2), ('a', 3), ('a', 2), ('b', 3), ('a', 4), ('b', 4), ('b', 5), ('c', 1), ('c', 0), ('a', 5), ('n', 5), ('c', 3), ('n', 2), ('c', 4), ('m', 5), ('m', 2), ('g', 0), ('g', 1), ('g', 2)]
-GATH = {0: [0, 1], 3: [2], 4: [3]}
-RING = 11
-GB = 3
-XPOS = 0
-ROOM = 'baaaa'
-YV = []
-PAIRS = [(0, 1), (2, 3), (4, 5)]
-HALVES = []
-YROOM = 0
-QA = 0
-ENDORD = 0
-LATE = []
-XH = 1
+ROWS = N // BLK
+PAIRS = E // 2
+PAIR_BYTES = 2 * 4 * BLK * 4
+SPAN = 4 * PAIR_BYTES
+WINDOW = 2 * T
+X_SCALAR = 22
+W3_SCALAR = 48
 
 
 def tile_moe_tk_glu_silu_kernel(tc, xT, w1, w3, w2, gate, offs, pos1, pos2, pos3, out):
@@ -46,226 +33,170 @@ def tile_moe_tk_glu_silu_kernel(tc, xT, w1, w3, w2, gate, offs, pos1, pos2, pos3
     with ExitStack() as ctx:
         lists = ctx.enter_context(tc.tile_pool(name="lists", bufs=1))
         keep = ctx.enter_context(tc.tile_pool(name="keep", bufs=1))
-        ring = ctx.enter_context(tc.tile_pool(name="ring", bufs=RING))
+        ring = ctx.enter_context(tc.tile_pool(name="ring", bufs=2 * E + 1))
         work = ctx.enter_context(tc.tile_pool(name="work", bufs=2))
+        tail = ctx.enter_context(tc.tile_pool(name="tail", bufs=1))
         psum = ctx.enter_context(tc.psum_pool(name="psum", bufs=8))
 
         offs_sb = lists.tile([P, S // 16], U16, name="offs_sb")
-        pos_sb = [lists.tile([P, T // 16], U16, name=f"pos_sb{r}") for r in range(TOP)]
+        pos_sb = [lists.tile([P, T // 16], U16, name=f"pos_sb{k}") for k in range(TOP)]
 
-        xs = keep.tile([P, T], U8, name="xs", align_bytes=64)
+        xs = keep.tile([P, WINDOW], U8, name="xs", align_bytes=64)
         nc.gpsimd.memset(xs[:], 0)
+        xw = keep.tile([P, WINDOW], U32, name="xw", align_bytes=64)
+        nc.gpsimd.memset(xw[:, T:], 0)
         warm = keep.tile([P, 1], F32, name="warm")
         nc.gpsimd.memset(warm[:], 0.0)
         warm_out = keep.tile([P, 1], F32, name="warm_out")
         nc.scalar.activation(warm_out[:], warm[:], SILU)
 
-        x_raw = []
-        raw, gates, pieces = {}, {}, {}
-        for n, (kind, e) in enumerate(LOADS):
-            if n == XPOS:
-                x_all = ring.tile([P, 4, T], F32, name="x_all", tag="raw")
-                for half in range(XH):
-                    xr = x_all[:, :, half * (T // XH) : (half + 1) * (T // XH)]
-                    nc.sync.dma_start(out=xr, in_=xT.rearrange("(p j) t -> p j t", j=4)[:, :, half * (T // XH) : (half + 1) * (T // XH)])
-                    x_raw.append(xr)
-                nc.sync.dma_start(offs_sb[:], offs)
-            if kind in "ab":
-                wr = ring.tile([P, 4, H], F32, name=f"raw_{kind}{e}", tag="raw")
-                src = (w1 if kind == "a" else w3)[e].rearrange("(p j) i -> p j i", j=4)
-                if (kind, e) in HALVES:
-                    nc.sync.dma_start(out=wr[:, :, 0:256], in_=src[:, :, 0:256])
-                    nc.sync.dma_start(out=wr[:, :, 256:512], in_=src[:, :, 256:512])
-                else:
-                    nc.sync.dma_start(out=wr[:], in_=src)
-                raw[kind, e] = wr
-            elif kind == "c":
-                wr = ring.tile([P, 4, N], F32, name=f"raw_c{e}", tag="raw")
-                nc.sync.dma_start(out=wr[:], in_=w2[e].rearrange("(p j) n -> p j n", j=4))
-                for r in range(3):
-                    raw[r, e] = wr[:, :, r * BLK : (r + 1) * BLK]
-            elif kind == "n":
-                pieces[e] = ring.tile([P, 4 * N], F32, name=f"raw_nm{e}", tag="raw")
-                wr = pieces[e][:, 0 : 4 * BLK].rearrange("p (j n) -> p j n", j=4)
-                nc.sync.dma_start(out=wr, in_=w2[e].rearrange("(p j) n -> p j n", j=4)[:, :, 0:BLK])
-                raw[0, e] = wr
-            elif kind == "m":
-                wr = pieces[e][:, 4 * BLK : 4 * N].rearrange("p (j n) -> p j n", j=4)
-                nc.sync.dma_start(out=wr, in_=w2[e].rearrange("(p j) n -> p j n", j=4)[:, :, BLK:N])
-                for r in range(2):
-                    raw[r + 1, e] = wr[:, :, r * BLK : (r + 1) * BLK]
-            else:
-                if e == 0:
-                    for k, src in enumerate((pos1, pos2, pos3)):
-                        nc.sync.dma_start(pos_sb[k][:], src)
-                gt = ring.tile([P, TOP, T], F32, name=f"gate{e}", tag="raw")
-                nc.sync.dma_start(out=gt[:], in_=gate[:, e * BLK : (e + 1) * BLK, :].rearrange("g p t -> p g t"))
-                gates[e] = gt
+        x_raw = ring.tile([P, 2, 4, T // 2], F32, name="x_raw", tag="raw")
+        for h in range(2):
+            nc.sync.dma_start(out=x_raw[:, h], in_=xT.rearrange("(p j) (h t) -> h p j t", j=4, h=2)[h])
+        nc.sync.dma_start(offs_sb[:], offs)
+        raw = {}
+        for e in range(E):
+            for i, w in enumerate((w1, w3)):
+                raw[e, i] = ring.tile([P, 4, H], F32, name=f"raw{e}_{i}", tag="raw")
+                nc.sync.dma_start(out=raw[e, i][:], in_=w[e].rearrange("(p j) i -> p j i", j=4))
+        raw2, gates = {}, {}
 
-        def split_copy(dst, src, ms, total):
-            if ms:
-                nc.scalar.copy(dst[:, 0:ms], src[:, 0:ms])
-            if ms < total:
-                nc.vector.tensor_copy(dst[:, ms:total], src[:, ms:total])
+        def load_w2(r):
+            for q in range(PAIRS):
+                raw2[r, q] = tail.tile([P, 2, 4, BLK], F32, name=f"raw2_{r}_{q}", offset=r * SPAN + q * PAIR_BYTES)
+                for u in range(2):
+                    nc.sync.dma_start(out=raw2[r, q][:, u], in_=w2[2 * q + u].rearrange("(p j) n -> p j n", j=4)[:, :, r * BLK : (r + 1) * BLK])
+
+        load_w2(0)
+        for k, src in enumerate((pos1, pos2, pos3)):
+            nc.sync.dma_start(pos_sb[k][:], src)
+            gates[k] = keep.tile([P, T], F32, name=f"gate{k}")
+            nc.sync.dma_start(out=gates[k][:], in_=gate[k, 0:P, :])
+        load_w2(1)
+        load_w2(2)
 
         xg = keep.tile([P, T, 4], BF16, name="xg", align_bytes=64)
-        xv = xg[:].rearrange("p (c i) j -> p c j i", i=4)
-        w = T // 4 // XH
-        for half in range(XH):
-            split_copy(xv[:, half * w : (half + 1) * w], x_raw[half].rearrange("p j (c i) -> p c j i", i=4), MSX * w // 64, w)
-        xw = keep.tile([P, T], U32, name="xw", align_bytes=64)
-        nc.vector.quantize_mx(out=xw[:].bitcast(FP8X4), scales=xs[:], in_=xg[:].rearrange("p t j -> p (t j)"))
+        xv = xg[:].rearrange("p (h c i) j -> p h c j i", h=2, i=4)
+        xr = x_raw[:].rearrange("p h j (c i) -> p h c j i", i=4)
+        nc.scalar.copy(xv[:, 0], xr[:, 0])
+        nc.scalar.copy(xv[:, 1, 0:X_SCALAR], xr[:, 1, 0:X_SCALAR])
+        nc.vector.tensor_copy(xv[:, 1, X_SCALAR:], xr[:, 1, X_SCALAR:])
+        for h in range(2):
+            toks = slice(h * T // 2, (h + 1) * T // 2)
+            nc.vector.quantize_mx(out=xw[:, toks].bitcast(FP8X4), scales=xs[:, toks], in_=xg[:, toks].rearrange("p t j -> p (t j)"))
 
-        gw, gs = {}, {}
+        gw = keep.tile([P, S], U32, name="gw", align_bytes=64)
+        gs = keep.tile([P, S], U8, name="gs", align_bytes=64)
+        for h in range(2):
+            nc.vector.tensor_copy(gw[:, h * S // 2 : (h + 1) * S // 2], xw[:].indirect(offs_sb[:, h * S // 32 : (h + 1) * S // 32]))
+            nc.vector.tensor_copy(gs[:, h * S // 2 : (h + 1) * S // 2], xs[:].indirect(offs_sb[:, h * S // 32 : (h + 1) * S // 32]))
 
-        def gather(b):
-            cols = slice(b * GATHER // 16, (b + 1) * GATHER // 16)
-            gw[b] = work.tile([P, GATHER], U32, name=f"gw{b}", tag="gw", align_bytes=64, bufs=GB)
-            nc.vector.tensor_copy(gw[b][:], xw[:].indirect(offs_sb[:, cols]))
-            gs[b] = work.tile([P, GATHER], U8, name=f"gs{b}", tag="gs", align_bytes=64, bufs=GB)
-            nc.vector.tensor_copy(gs[b][:], xs[:].indirect(offs_sb[:, cols]))
+        grouped, banks, sil, hb, hw, hs = {}, {}, {}, {}, {}, {}
 
-        def moving(blk):
-            b, o = divmod(blk * BLK, GATHER)
-            return gw[b][:, o : o + BLK].bitcast(FP8X4), gs[b][:, o : o + BLK]
+        def group(e, i):
+            grouped[e, i] = work.tile([P, 4 * H], BF16, name=f"grp{e}_{i}", tag="grp", align_bytes=64, bufs=4)
+            dst = grouped[e, i][:].rearrange("p (t m j) -> p m j t", t=4, j=4)
+            src = raw[e, i][:].rearrange("p j (m t) -> p m j t", t=4)
+            if i == 0 or e == 0:
+                nc.scalar.copy(dst, src)
+            else:
+                nc.scalar.copy(dst[:, 0:W3_SCALAR], src[:, 0:W3_SCALAR])
+                nc.vector.tensor_copy(dst[:, W3_SCALAR:], src[:, W3_SCALAR:])
 
-        grouped, codes, hb, hw, hs = {}, {}, {}, {}, {}
-        w2g, w2w, w2s = {}, {}, {}
-
-        def copy_w13(e, i):
-            kind, ms = (("a", MS1[e]), ("b", MS3[e]))[i]
-            grouped[e, i] = work.tile([P, 4 * H], BF16, name=f"grp_{kind}{e}", tag="grp", align_bytes=64, bufs=4)
-            split_copy(grouped[e, i][:].rearrange("p (t m j) -> p m j t", t=4, j=4), raw[kind, e][:].rearrange("p j (m t) -> p m j t", t=4), ms, 128)
-
-        def quantize_w13(e, i):
-            cw = work.tile([P, H], U32, name=f"cw{e}_{i}", tag="cw", align_bytes=64, bufs=4)
-            cs = work.tile([P, H], U8, name=f"cs{e}_{i}", tag="cs", align_bytes=64, bufs=4)
+        def first_layer(e, i):
+            cw = work.tile([P, H], U32, name=f"cw{e}_{i}", tag="cw", align_bytes=64, bufs=3)
+            cs = work.tile([P, H], U8, name=f"cs{e}_{i}", tag="cs", align_bytes=64, bufs=3)
             nc.vector.quantize_mx(out=cw[:].bitcast(FP8X4), scales=cs[:], in_=grouped[e, i][:])
-            codes[e, i] = (cw, cs)
-
-        banks = {}
-
-        def hidden(e):
             for c in range(2):
-                rw, rs = moving(2 * e + c)
-                for i in range(2):
-                    cw, cs = codes[e, i]
-                    bank = psum.tile([P, 4, BLK], F32, name=f"bank_{i}_{e}_{c}", tag="bank")
-                    for t in range(4):
-                        sl = slice(t * BLK, (t + 1) * BLK)
-                        nc.tensor.matmul_mx(out=bank[:, t, :], lhsT=cw[:, sl].bitcast(FP8X4), lhsT_scale=cs[:, sl], rhs=rw, rhs_scale=rs, start=True, stop=True)
-                    banks[e, i, c] = bank
+                slots = slice(e * C + c * BLK, e * C + (c + 1) * BLK)
+                banks[e, i, c] = psum.tile([P, 4, BLK], F32, name=f"bank{e}_{i}_{c}", tag="bank")
+                for t in range(4):
+                    cols = slice(t * BLK, (t + 1) * BLK)
+                    nc.tensor.matmul_mx(out=banks[e, i, c][:, t, :], lhsT=cw[:, cols].bitcast(FP8X4), lhsT_scale=cs[:, cols], rhs=gw[:, slots].bitcast(FP8X4), rhs_scale=gs[:, slots], start=True, stop=True)
 
         def activate(e):
-            hb[e] = work.tile([P, C, 4], BF16, name=f"hb{e}", tag="hb", align_bytes=64)
-            if e + 1 < E:
-                room = raw[ROOM[e], e + 1]
-            else:
-                room = work.tile([P, 2, H], F32, name="room", tag="room", align_bytes=64, bufs=1)
+            room = raw[e + 1, 0] if e + 1 < E else ring.tile([P, 4, H], F32, name="room", tag="raw")
             for c in range(2):
-                sil = room[:, c, :].rearrange("p (c t) -> p c t", t=4)
-                nc.scalar.activation(sil, banks[e, 0, c][:].rearrange("p t c -> p c t"), SILU)
-                nc.vector.tensor_tensor(hb[e][:, c * BLK : (c + 1) * BLK, :], banks[e, 1, c][:].rearrange("p t c -> p c t"), sil, MULT)
+                sil[e, c] = room[:, c, :].rearrange("p (c t) -> p c t", t=4)
+                nc.scalar.activation(sil[e, c], banks[e, 0, c][:].rearrange("p t c -> p c t"), SILU)
+
+        def hidden(e):
+            hb[e] = work.tile([P, C, 4], BF16, name=f"hb{e}", tag="hb", align_bytes=64)
+            for c in range(2):
+                nc.vector.tensor_tensor(hb[e][:, c * BLK : (c + 1) * BLK, :], banks[e, 1, c][:].rearrange("p t c -> p c t"), sil[e, c], MULT)
 
         def quantize_h(e):
             hw[e] = keep.tile([P, C], U32, name=f"hw{e}", align_bytes=64)
             hs[e] = keep.tile([P, C], U8, name=f"hs{e}", align_bytes=64)
             nc.vector.quantize_mx(out=hw[e][:].bitcast(FP8X4), scales=hs[e][:], in_=hb[e][:].rearrange("p c t -> p (c t)"))
 
-        late = []
+        ys, w2g = {}, {}
 
-        def copy_w2(r, q):
-            if (r, q) in LATE:
-                if not late:
-                    late.append(work.tile([P, 6, 2, BLK, 4], BF16, name="late", tag="room", align_bytes=64, bufs=1))
-                w2g[r, q] = late[0][:, 3 * (r - 1) + q]
-            else:
-                w2g[r, q] = keep.tile([P, 2, BLK, 4], BF16, name=f"grp2_{r}_{q}", align_bytes=64)[:]
+        def group_w2(r, q):
+            w2g[r, q] = work.tile([P, 2, BLK, 4], BF16, name=f"grp2_{r}_{q}", tag="grp2", align_bytes=64, bufs=3)
+            nc.scalar.copy(w2g[r, q][:].rearrange("p u (c i) j -> p u c j i", i=4), raw2[r, q][:].rearrange("p u j (c i) -> p u c j i", i=4))
+
+        def second_layer(r, q):
+            cw = work.tile([P, 2, BLK], U32, name=f"w2w{r}_{q}", tag="w2w", align_bytes=64, bufs=3)
+            cs = work.tile([P, 2, BLK], U8, name=f"w2s{r}_{q}", tag="w2s", align_bytes=64, bufs=3)
+            nc.vector.quantize_mx(out=cw[:].rearrange("p u n -> p (u n)").bitcast(FP8X4), scales=cs[:].rearrange("p u n -> p (u n)"), in_=w2g[r, q][:].rearrange("p u n j -> p (u n j)"))
+            if q == 0:
+                ys[r] = tail.tile([P, S], F32, name=f"y{r}", offset=r * SPAN + 2 * PAIR_BYTES + PAIR_BYTES // 2)
+            bank = psum.tile([P, 2, C], F32, name=f"bank_y{r}_{q}", tag="bank")
             for u in range(2):
-                split_copy(w2g[r, q][:, u].rearrange("p (c i) j -> p c j i", i=4), raw[r, PAIRS[q][u]].rearrange("p j (c i) -> p c j i", i=4), MSN[r][q], 32)
+                e = 2 * q + u
+                nc.tensor.matmul_mx(out=bank[:, u, :], lhsT=cw[:, u].bitcast(FP8X4), lhsT_scale=cs[:, u], rhs=hw[e][:].bitcast(FP8X4), rhs_scale=hs[e][:], start=True, stop=True)
+            nc.scalar.copy(ys[r][:, 2 * q * C : 2 * (q + 1) * C], bank[:].rearrange("p u c -> p (u c)"))
 
-        def quantize_w2(r, q):
-            w2w[r, q] = keep.tile([P, 2, BLK], U32, name=f"w2w{r}_{q}", align_bytes=64)
-            w2s[r, q] = keep.tile([P, 2, BLK], U8, name=f"w2s{r}_{q}", align_bytes=64)
-            nc.vector.quantize_mx(out=w2w[r, q][:].rearrange("p u n -> p (u n)").bitcast(FP8X4), scales=w2s[r, q][:].rearrange("p u n -> p (u n)"), in_=w2g[r, q].rearrange("p u n j -> p (u n j)"))
-
-        ys = {}
-
-        def project(r):
-            if r == 0 and YROOM:
-                ys[r] = work.tile([P, S], F32, name=f"y{r}", tag="room", align_bytes=64, bufs=1)
-            else:
-                ys[r] = keep.tile([P, S], F32, name=f"y{r}")
-            for q in range(3):
-                bank = psum.tile([P, 2, C], F32, name=f"bank_y{r}_{q}", tag="bank")
-                for u in range(2):
-                    e = PAIRS[q][u]
-                    nc.tensor.matmul_mx(out=bank[:, u, :], lhsT=w2w[r, q][:, u].bitcast(FP8X4), lhsT_scale=w2s[r, q][:, u], rhs=hw[e][:].bitcast(FP8X4), rhs_scale=hs[e][:], start=True, stop=True)
-                e0, e1 = PAIRS[q]
-                dst = ys[r][:].rearrange("p (e c) -> p e c", c=C)[:, e0 : e1 + 1 : e1 - e0]
-                if (r, q) in YV:
-                    nc.vector.tensor_copy(dst, bank[:])
-                else:
-                    nc.scalar.copy(dst, bank[:])
-
-        prods, sums, outs = {}, {}, {}
+        prods = {}
 
         def fetch(r, k, t0=0, t1=T):
             if (r, k) not in prods:
-                prods[r, k] = work.tile([P, T], F32, name=f"prod{r}_{k}", tag=f"prod{k}")
-            nc.vector.tensor_tensor(prods[r, k][:, t0:t1], ys[r][:].indirect(pos_sb[k][:, t0 // 16 : t1 // 16]), gates[r][:, k, t0:t1], MULT)
-
-        def add01(r):
-            sums[r] = work.tile([P, T], F32, name=f"sum{r}", tag="sum")
-            nc.vector.tensor_tensor(sums[r][:], prods[r, 0][:], prods[r, 1][:], ADD)
-
-        def add2(r, t0=0, t1=T):
-            if r not in outs:
-                outs[r] = work.tile([P, T], F32, name=f"o{r}", tag="o")
-            nc.vector.tensor_tensor(outs[r][:, t0:t1], sums[r][:, t0:t1], prods[r, 2][:, t0:t1], ADD)
-            nc.sync.dma_start(out=out[r * BLK : (r + 1) * BLK, t0:t1], in_=outs[r][:, t0:t1])
+                if k > 0 and r + 1 < ROWS:
+                    prods[r, k] = tail.tile([P, T], F32, name=f"prod{r}_{k}", offset=(r + 1) * SPAN + (k - 1) * 2 * PAIR_BYTES)
+                else:
+                    prods[r, k] = work.tile([P, T], F32, name=f"prod{r}_{k}", tag=f"prod{k}", bufs=1 if k else 2)
+            nc.vector.tensor_tensor(prods[r, k][:, t0:t1], ys[r][:].indirect(pos_sb[k][:, t0 // 16 : t1 // 16]), gates[k][:, t0:t1], MULT)
 
         for e in range(E):
-            for b in GATH.get(e, []):
-                gather(b)
-            copy_w13(e, 0)
-            if not QA:
-                quantize_w13(e, 0)
-            if e > 0 and ROOM[e - 1] == "a":
+            group(e, 0)
+            first_layer(e, 0)
+            if e > 0:
                 activate(e - 1)
+                hidden(e - 1)
+            group(e, 1)
+            if e > 0:
                 quantize_h(e - 1)
-            if QA:
-                quantize_w13(e, 0)
-            copy_w13(e, 1)
-            quantize_w13(e, 1)
-            if e > 0 and ROOM[e - 1] == "b":
-                activate(e - 1)
-                quantize_h(e - 1)
-            hidden(e)
+            first_layer(e, 1)
         activate(E - 1)
+        hidden(E - 1)
         quantize_h(E - 1)
-        for r, q in [(r, q) for q in range(3) for r in range(3)] if ENDORD == 0 else [(r, q) for r in range(3) for q in range(3)]:
-            copy_w2(r, q)
-            quantize_w2(r, q)
-            if ENDORD == 2 and q == 2:
-                project(r)
-        if ENDORD < 2:
-            for r in range(3):
-                project(r)
-        fetch(0, 0)
-        fetch(0, 1)
-        fetch(0, 2)
-        add01(0)
-        fetch(1, 0)
-        add2(0)
-        fetch(1, 1)
-        fetch(1, 2)
-        add01(1)
-        fetch(2, 0)
-        add2(1)
-        fetch(2, 1)
-        fetch(2, 2, 0, 256)
-        add01(2)
-        fetch(2, 2, 256, 512)
-        add2(2, 0, 256)
-        add2(2, 256, 512)
+
+        for q in range(PAIRS):
+            group_w2(0, q)
+            second_layer(0, q)
+        for r in range(ROWS):
+            part = work.tile([P, T], F32, name=f"part{r}", tag="part")
+            res = work.tile([P, T], F32, name=f"res{r}", tag="res")
+            last = r + 1 == ROWS
+            if not last:
+                for q in range(PAIRS):
+                    group_w2(r + 1, q)
+            fetch(r, 0)
+            if not last:
+                second_layer(r + 1, 0)
+            fetch(r, 1)
+            if not last:
+                second_layer(r + 1, 1)
+                nc.vector.tensor_tensor(part[:], prods[r, 0][:], prods[r, 1][:], ADD)
+                second_layer(r + 1, 2)
+                fetch(r, 2)
+            else:
+                fetch(r, 2, 0, T // 2)
+                nc.vector.tensor_tensor(part[:], prods[r, 0][:], prods[r, 1][:], ADD)
+                fetch(r, 2, T // 2, T)
+            halves = 2 if r + 1 == ROWS else 1
+            for h in range(halves):
+                cols = slice(h * T // halves, (h + 1) * T // halves)
+                nc.vector.tensor_tensor(res[:, cols], part[:, cols], prods[r, 2][:, cols], ADD)
+                nc.sync.dma_start(out=out[r * BLK : (r + 1) * BLK, cols], in_=res[:, cols])

@@ -1,6 +1,7 @@
 from contextlib import ExitStack
 
 import concourse.mybir as mybir
+from concourse.masks import make_identity
 
 K, T, E, C, H, N = 512, 512, 6, 256, 512, 384
 TOP = 3
@@ -21,11 +22,19 @@ BLK = 128
 S = E * C
 ROWS = N // BLK
 PAIRS = E // 2
+RAW_BYTES = 4 * H * 4
+BANK_BYTES = 2048
+GROUP_BYTES = 4 * H * 2
 PAIR_BYTES = 2 * 4 * BLK * 4
-SPAN = 4 * PAIR_BYTES
+ROW_BYTES = T * 4
+Y_BYTES = S * 4
+LAP = 64
+SPAN = Y_BYTES - LAP + PAIRS * PAIR_BYTES
 WINDOW = 2 * T
+FIRST_AFTER = (3, 5, 5)
+LAST_SCALAR = 64
 X_SCALAR = 22
-W3_SCALAR = 48
+W3_SCALAR = 44
 
 
 def tile_moe_tk_glu_silu_kernel(tc, xT, w1, w3, w2, gate, offs, pos1, pos2, pos3, out):
@@ -33,10 +42,11 @@ def tile_moe_tk_glu_silu_kernel(tc, xT, w1, w3, w2, gate, offs, pos1, pos2, pos3
     with ExitStack() as ctx:
         lists = ctx.enter_context(tc.tile_pool(name="lists", bufs=1))
         keep = ctx.enter_context(tc.tile_pool(name="keep", bufs=1))
-        ring = ctx.enter_context(tc.tile_pool(name="ring", bufs=2 * E + 1))
+        ring = ctx.enter_context(tc.tile_pool(name="ring", bufs=1))
         work = ctx.enter_context(tc.tile_pool(name="work", bufs=2))
         tail = ctx.enter_context(tc.tile_pool(name="tail", bufs=1))
-        psum = ctx.enter_context(tc.psum_pool(name="psum", bufs=8))
+        lane = ctx.enter_context(tc.tile_pool(name="lane", bufs=1))
+        psum = ctx.enter_context(tc.psum_pool(name="psum", bufs=1))
 
         offs_sb = lists.tile([P, S // 16], U16, name="offs_sb")
         pos_sb = [lists.tile([P, T // 16], U16, name=f"pos_sb{k}") for k in range(TOP)]
@@ -45,37 +55,44 @@ def tile_moe_tk_glu_silu_kernel(tc, xT, w1, w3, w2, gate, offs, pos1, pos2, pos3
         nc.gpsimd.memset(xs[:], 0)
         xw = keep.tile([P, WINDOW], U32, name="xw", align_bytes=64)
         nc.gpsimd.memset(xw[:, T:], 0)
+        ident = keep.tile([P, P], F32, name="ident")
+        make_identity(nc, ident[:])
         warm = keep.tile([P, 1], F32, name="warm")
         nc.gpsimd.memset(warm[:], 0.0)
         warm_out = keep.tile([P, 1], F32, name="warm_out")
         nc.scalar.activation(warm_out[:], warm[:], SILU)
 
-        x_raw = ring.tile([P, 2, 4, T // 2], F32, name="x_raw", tag="raw")
+        x_raw = ring.tile([P, 2, 4, T // 2], F32, name="x_raw", offset=0)
         for h in range(2):
             nc.sync.dma_start(out=x_raw[:, h], in_=xT.rearrange("(p j) (h t) -> h p j t", j=4, h=2)[h])
         nc.sync.dma_start(offs_sb[:], offs)
-        raw = {}
+        raw, first, raw2, gates = {}, {}, {}, {}
         for e in range(E):
             for i, w in enumerate((w1, w3)):
-                raw[e, i] = ring.tile([P, 4, H], F32, name=f"raw{e}_{i}", tag="raw")
+                raw[e, i] = ring.tile([P, 4, H], F32, name=f"raw{e}_{i}", offset=((2 * e + i + 1) % (2 * E)) * RAW_BYTES)
                 nc.sync.dma_start(out=raw[e, i][:], in_=w[e].rearrange("(p j) i -> p j i", j=4))
-        raw2, gates = {}, {}
+            for q in [q for q in range(PAIRS) if FIRST_AFTER[q] == e]:
+                first[q] = keep.tile([P, 2, 4, BLK], F32, name=f"first{q}")
+                for u in range(2):
+                    nc.sync.dma_start(out=first[q][:, u], in_=w2[2 * q + u].rearrange("(p j) n -> p j n", j=4)[:, :, 0:BLK])
 
-        def load_w2(r):
-            for q in range(PAIRS):
-                raw2[r, q] = tail.tile([P, 2, 4, BLK], F32, name=f"raw2_{r}_{q}", offset=r * SPAN + q * PAIR_BYTES)
+        def pair_at(r, q):
+            return (r - 1) * SPAN + Y_BYTES - LAP + q * PAIR_BYTES
+
+        def load_w2(r, pairs):
+            for q in pairs:
+                raw2[r, q] = tail.tile([P, 2, 4, BLK], F32, name=f"raw2_{r}_{q}", offset=pair_at(r, q))
                 for u in range(2):
                     nc.sync.dma_start(out=raw2[r, q][:, u], in_=w2[2 * q + u].rearrange("(p j) n -> p j n", j=4)[:, :, r * BLK : (r + 1) * BLK])
 
-        load_w2(0)
         for k, src in enumerate((pos1, pos2, pos3)):
+            load_w2(1, [k])
             nc.sync.dma_start(pos_sb[k][:], src)
             gates[k] = keep.tile([P, T], F32, name=f"gate{k}")
             nc.sync.dma_start(out=gates[k][:], in_=gate[k, 0:P, :])
-        load_w2(1)
-        load_w2(2)
+        load_w2(2, range(PAIRS))
 
-        xg = keep.tile([P, T, 4], BF16, name="xg", align_bytes=64)
+        xg = lane.tile([P, T, 4], BF16, name="xg", align_bytes=64, offset=(E - 1) * GROUP_BYTES)
         xv = xg[:].rearrange("p (h c i) j -> p h c j i", h=2, i=4)
         xr = x_raw[:].rearrange("p h j (c i) -> p h c j i", i=4)
         nc.scalar.copy(xv[:, 0], xr[:, 0])
@@ -94,14 +111,18 @@ def tile_moe_tk_glu_silu_kernel(tc, xT, w1, w3, w2, gate, offs, pos1, pos2, pos3
         grouped, banks, sil, hb, hw, hs = {}, {}, {}, {}, {}, {}
 
         def group(e, i):
-            grouped[e, i] = work.tile([P, 4 * H], BF16, name=f"grp{e}_{i}", tag="grp", align_bytes=64, bufs=4)
+            if i == 0 or e + 1 == E:
+                grouped[e, i] = lane.tile([P, 4 * H], BF16, name=f"grp{e}_{i}", align_bytes=64, offset=(e if i == 0 else 0) * GROUP_BYTES)
+            else:
+                grouped[e, i] = work.tile([P, 4 * H], BF16, name=f"grp{e}_{i}", tag="grp", align_bytes=64)
             dst = grouped[e, i][:].rearrange("p (t m j) -> p m j t", t=4, j=4)
             src = raw[e, i][:].rearrange("p j (m t) -> p m j t", t=4)
             if i == 0 or e == 0:
                 nc.scalar.copy(dst, src)
             else:
-                nc.scalar.copy(dst[:, 0:W3_SCALAR], src[:, 0:W3_SCALAR])
-                nc.vector.tensor_copy(dst[:, W3_SCALAR:], src[:, W3_SCALAR:])
+                cut = W3_SCALAR if e + 1 < E else LAST_SCALAR
+                nc.scalar.copy(dst[:, 0:cut], src[:, 0:cut])
+                nc.vector.tensor_copy(dst[:, cut:], src[:, cut:])
 
         def first_layer(e, i):
             cw = work.tile([P, H], U32, name=f"cw{e}_{i}", tag="cw", align_bytes=64, bufs=3)
@@ -109,13 +130,13 @@ def tile_moe_tk_glu_silu_kernel(tc, xT, w1, w3, w2, gate, offs, pos1, pos2, pos3
             nc.vector.quantize_mx(out=cw[:].bitcast(FP8X4), scales=cs[:], in_=grouped[e, i][:])
             for c in range(2):
                 slots = slice(e * C + c * BLK, e * C + (c + 1) * BLK)
-                banks[e, i, c] = psum.tile([P, 4, BLK], F32, name=f"bank{e}_{i}_{c}", tag="bank")
+                banks[e, i, c] = psum.tile([P, 4, BLK], F32, name=f"bank{e}_{i}_{c}", offset=(4 * (e % 2) + 2 * i + c) * BANK_BYTES)
                 for t in range(4):
                     cols = slice(t * BLK, (t + 1) * BLK)
                     nc.tensor.matmul_mx(out=banks[e, i, c][:, t, :], lhsT=cw[:, cols].bitcast(FP8X4), lhsT_scale=cs[:, cols], rhs=gw[:, slots].bitcast(FP8X4), rhs_scale=gs[:, slots], start=True, stop=True)
 
         def activate(e):
-            room = raw[e + 1, 0] if e + 1 < E else ring.tile([P, 4, H], F32, name="room", tag="raw")
+            room = raw[e + 1, (e + 1) // (E - 1)] if e + 1 < E else ring.tile([P, 4, H], F32, name="room", offset=RAW_BYTES)
             for c in range(2):
                 sil[e, c] = room[:, c, :].rearrange("p (c t) -> p c t", t=4)
                 nc.scalar.activation(sil[e, c], banks[e, 0, c][:].rearrange("p t c -> p c t"), SILU)
@@ -136,67 +157,111 @@ def tile_moe_tk_glu_silu_kernel(tc, xT, w1, w3, w2, gate, offs, pos1, pos2, pos3
             w2g[r, q] = work.tile([P, 2, BLK, 4], BF16, name=f"grp2_{r}_{q}", tag="grp2", align_bytes=64, bufs=3)
             nc.scalar.copy(w2g[r, q][:].rearrange("p u (c i) j -> p u c j i", i=4), raw2[r, q][:].rearrange("p u j (c i) -> p u c j i", i=4))
 
-        def second_layer(r, q):
-            cw = work.tile([P, 2, BLK], U32, name=f"w2w{r}_{q}", tag="w2w", align_bytes=64, bufs=3)
-            cs = work.tile([P, 2, BLK], U8, name=f"w2s{r}_{q}", tag="w2s", align_bytes=64, bufs=3)
-            nc.vector.quantize_mx(out=cw[:].rearrange("p u n -> p (u n)").bitcast(FP8X4), scales=cs[:].rearrange("p u n -> p (u n)"), in_=w2g[r, q][:].rearrange("p u n j -> p (u n j)"))
+        codes = {}
+
+        def first_rows(q):
+            w2g[0, q] = lane.tile([P, 2, BLK, 4], BF16, name=f"first_grp{q}", align_bytes=64, offset=((FIRST_AFTER[q] + 1) % E) * GROUP_BYTES + (q % 2) * GROUP_BYTES // 2)
+            nc.gpsimd.tensor_scalar(w2g[0, q][:], first[q][:].rearrange("p u j n -> p u n j"), 1.0, 0.0, MULT, ADD)
+
+        def quantize_w2(r, q):
+            if r >= 0:
+                cw = work.tile([P, 2, BLK], U32, name=f"w2w{r}_{q}", tag="w2w", align_bytes=64, bufs=5)
+                cs = work.tile([P, 2, BLK], U8, name=f"w2s{r}_{q}", tag="w2s", align_bytes=64, bufs=5)
+                nc.vector.quantize_mx(out=cw[:].rearrange("p u n -> p (u n)").bitcast(FP8X4), scales=cs[:].rearrange("p u n -> p (u n)"), in_=w2g[r, q][:].rearrange("p u n j -> p (u n j)"))
+                for u in range(2):
+                    codes[r, 2 * q + u] = (cw[:, u], cs[:, u])
+
+        def project(r, q):
             if q == 0:
-                ys[r] = tail.tile([P, S], F32, name=f"y{r}", offset=r * SPAN + 2 * PAIR_BYTES + PAIR_BYTES // 2)
-            bank = psum.tile([P, 2, C], F32, name=f"bank_y{r}_{q}", tag="bank")
+                ys[r] = tail.tile([P, S], F32, name=f"y{r}", offset=r * SPAN if r + 1 < ROWS else pair_at(r, 2) + ROW_BYTES + LAP)
+            bank = psum.tile([P, 2, C], F32, name=f"bank_y{r}_{q}", offset=((0, 1, 4), (2, 3, 5), (6, 7, 0))[r][q] * BANK_BYTES)
             for u in range(2):
                 e = 2 * q + u
-                nc.tensor.matmul_mx(out=bank[:, u, :], lhsT=cw[:, u].bitcast(FP8X4), lhsT_scale=cs[:, u], rhs=hw[e][:].bitcast(FP8X4), rhs_scale=hs[e][:], start=True, stop=True)
+                nc.tensor.matmul_mx(out=bank[:, u, :], lhsT=codes[r, e][0].bitcast(FP8X4), lhsT_scale=codes[r, e][1], rhs=hw[e][:].bitcast(FP8X4), rhs_scale=hs[e][:], start=True, stop=True)
             nc.scalar.copy(ys[r][:, 2 * q * C : 2 * (q + 1) * C], bank[:].rearrange("p u c -> p (u c)"))
 
-        prods = {}
+        prods, turned = {}, {}
+        scratch = [ring.tile([P, 4, T], F32, name=f"scratch{r}", offset=(3 + r) * RAW_BYTES) for r in range(ROWS)]
 
         def fetch(r, k, t0=0, t1=T):
             if (r, k) not in prods:
                 if k > 0 and r + 1 < ROWS:
-                    prods[r, k] = tail.tile([P, T], F32, name=f"prod{r}_{k}", offset=(r + 1) * SPAN + (k - 1) * 2 * PAIR_BYTES)
+                    prods[r, k] = tail.tile([P, T], F32, name=f"prod{r}_{k}", offset=pair_at(r + 1, k) - (k - 1) * (ROW_BYTES - LAP))
                 else:
-                    prods[r, k] = work.tile([P, T], F32, name=f"prod{r}_{k}", tag=f"prod{k}", bufs=1 if k else 2)
+                    prods[r, k] = scratch[r][:, k]
             nc.vector.tensor_tensor(prods[r, k][:, t0:t1], ys[r][:].indirect(pos_sb[k][:, t0 // 16 : t1 // 16]), gates[k][:, t0:t1], MULT)
 
-        for e in range(E):
+        def add_turned(r):
+            bank = psum.tile([P, 4, BLK], F32, name=f"bank_sum{r}", offset=(1 + r) * BANK_BYTES)
+            for b in range(4):
+                for k in range(TOP):
+                    nc.tensor.matmul(bank[:, b, :], prods[r, k][:, b * BLK : (b + 1) * BLK], ident[:], start=k == 0, stop=k + 1 == TOP, is_transpose=True)
+            turned[r] = tail.tile([P, 4, BLK], F32, name="turned0", offset=pair_at(2, 2) + LAP)[:] if r == 0 else scratch[r][:, 1].rearrange("p (b n) -> p b n", b=4)
+            nc.scalar.copy(turned[r], bank[:])
+
+        def turn_back(r):
+            bank = psum.tile([P, 4, BLK], F32, name=f"bank_back{r}", offset=(7, 3)[r] * BANK_BYTES)
+            for b in range(4):
+                nc.tensor.transpose(bank[:, b, :], turned[r][:, b, :], ident[:])
+            nc.scalar.copy(scratch[r][:, 3], bank[:].rearrange("p b t -> p (b t)"))
+            nc.sync.dma_start(out=out[r * BLK : (r + 1) * BLK, :], in_=scratch[r][:, 3])
+
+        for e in range(E - 1):
             group(e, 0)
             first_layer(e, 0)
             if e > 0:
                 activate(e - 1)
                 hidden(e - 1)
+            if e - 1 in FIRST_AFTER:
+                first_rows(FIRST_AFTER.index(e - 1))
             group(e, 1)
             if e > 0:
                 quantize_h(e - 1)
             first_layer(e, 1)
-        activate(E - 1)
-        hidden(E - 1)
-        quantize_h(E - 1)
-
-        for q in range(PAIRS):
-            group_w2(0, q)
-            second_layer(0, q)
-        for r in range(ROWS):
-            part = work.tile([P, T], F32, name=f"part{r}", tag="part")
-            res = work.tile([P, T], F32, name=f"res{r}", tag="res")
-            last = r + 1 == ROWS
-            if not last:
-                for q in range(PAIRS):
-                    group_w2(r + 1, q)
+            if e - 1 in FIRST_AFTER:
+                quantize_w2(0, FIRST_AFTER.index(e - 1))
+        for i in range(2):
+            group(E - 1, i)
+            first_layer(E - 1, i)
+        first_rows(1)
+        first_rows(2)
+        for e in (E - 2, E - 1):
+            activate(e)
+            hidden(e)
+        quantize_w2(0, 1)
+        quantize_w2(0, 2)
+        for e in (E - 2, E - 1):
+            quantize_h(e)
+        group_w2(1, 0)
+        quantize_w2(1, 0)
+        for r in range(ROWS - 1):
+            for q in range(PAIRS):
+                project(r, q)
+            for q in (1, 2):
+                group_w2(r + 1, q)
+            if r > 0:
+                add_turned(r - 1)
             fetch(r, 0)
-            if not last:
-                second_layer(r + 1, 0)
-            fetch(r, 1)
-            if not last:
-                second_layer(r + 1, 1)
-                nc.vector.tensor_tensor(part[:], prods[r, 0][:], prods[r, 1][:], ADD)
-                second_layer(r + 1, 2)
-                fetch(r, 2)
-            else:
-                fetch(r, 2, 0, T // 2)
-                nc.vector.tensor_tensor(part[:], prods[r, 0][:], prods[r, 1][:], ADD)
-                fetch(r, 2, T // 2, T)
-            halves = 2 if r + 1 == ROWS else 1
-            for h in range(halves):
-                cols = slice(h * T // halves, (h + 1) * T // halves)
-                nc.vector.tensor_tensor(res[:, cols], part[:, cols], prods[r, 2][:, cols], ADD)
-                nc.sync.dma_start(out=out[r * BLK : (r + 1) * BLK, cols], in_=res[:, cols])
+            for q in (1, 2):
+                quantize_w2(r + 1, q)
+                fetch(r, q)
+            if r + 2 < ROWS:
+                group_w2(r + 2, 0)
+                quantize_w2(r + 2, 0)
+        r = ROWS - 1
+        for q in range(PAIRS):
+            project(r, q)
+        turn_back(r - 2)
+        add_turned(r - 1)
+        turn_back(r - 1)
+        part = scratch[r][:, 3]
+        res = work.tile([P, T], F32, name="res", bufs=1)
+        fetch(r, 0)
+        fetch(r, 1)
+        fetch(r, 2, 0, T // 2)
+        nc.vector.tensor_tensor(part, prods[r, 0], prods[r, 1], ADD)
+        fetch(r, 2, T // 2, T)
+        for h in range(2):
+            cols = slice(h * T // 2, (h + 1) * T // 2)
+            nc.vector.tensor_tensor(res[:, cols], part[:, cols], prods[r, 2][:, cols], ADD)
+            nc.sync.dma_start(out=out[r * BLK : (r + 1) * BLK, cols], in_=res[:, cols])

@@ -9,6 +9,7 @@ FLOPS = 2 * TOP * T * (2 * K * H + H * N)
 
 F32 = mybir.dt.float32
 BF16 = mybir.dt.bfloat16
+I32 = mybir.dt.int32
 U32 = mybir.dt.uint32
 U16 = mybir.dt.uint16
 U8 = mybir.dt.uint8
@@ -33,8 +34,8 @@ SPAN = Y_BYTES - LAP + PAIRS * PAIR_BYTES
 WINDOW = 2 * T
 FIRST_AFTER = (3, 5, 5)
 LAST_SCALAR = 64
-X_SCALAR = 22
-W3_SCALAR = 44
+X_SCALAR = 28
+W3_SCALAR = 42
 
 
 def tile_moe_tk_glu_silu_kernel(tc, xT, w1, w3, w2, gate, offs, pos1, pos2, pos3, out):
@@ -45,36 +46,34 @@ def tile_moe_tk_glu_silu_kernel(tc, xT, w1, w3, w2, gate, offs, pos1, pos2, pos3
         ring = ctx.enter_context(tc.tile_pool(name="ring", bufs=1))
         work = ctx.enter_context(tc.tile_pool(name="work", bufs=2))
         tail = ctx.enter_context(tc.tile_pool(name="tail", bufs=1))
-        lane = ctx.enter_context(tc.tile_pool(name="lane", bufs=1))
         psum = ctx.enter_context(tc.psum_pool(name="psum", bufs=1))
 
         offs_sb = lists.tile([P, S // 16], U16, name="offs_sb")
         pos_sb = [lists.tile([P, T // 16], U16, name=f"pos_sb{k}") for k in range(TOP)]
 
-        xs = keep.tile([P, WINDOW], U8, name="xs", align_bytes=64)
-        nc.gpsimd.memset(xs[:], 0)
-        xw = keep.tile([P, WINDOW], U32, name="xw", align_bytes=64)
-        nc.gpsimd.memset(xw[:, T:], 0)
+        warm = keep.tile([P, 2], F32, name="warm")
+        nc.vector.memset(warm[:, 0:1], 0.0)
+        nc.scalar.activation(warm[:, 1:2], warm[:, 0:1], SILU)
         ident = keep.tile([P, P], F32, name="ident")
         make_identity(nc, ident[:])
-        warm = keep.tile([P, 1], F32, name="warm")
-        nc.gpsimd.memset(warm[:], 0.0)
-        warm_out = keep.tile([P, 1], F32, name="warm_out")
-        nc.scalar.activation(warm_out[:], warm[:], SILU)
+        xs = keep.tile([P, WINDOW], U8, name="xs", align_bytes=64)
+        nc.vector.memset(xs[:].bitcast(I32), 0)
+        xw = keep.tile([P, WINDOW], U32, name="xw", align_bytes=64)
+        nc.vector.memset(xw[:, T:].bitcast(I32), 0)
 
         x_raw = ring.tile([P, 2, 4, T // 2], F32, name="x_raw", offset=0)
         for h in range(2):
             nc.sync.dma_start(out=x_raw[:, h], in_=xT.rearrange("(p j) (h t) -> h p j t", j=4, h=2)[h])
         nc.sync.dma_start(offs_sb[:], offs)
-        raw, first, raw2, gates = {}, {}, {}, {}
+        raw, raw2, gates = {}, {}, {}
         for e in range(E):
             for i, w in enumerate((w1, w3)):
                 raw[e, i] = ring.tile([P, 4, H], F32, name=f"raw{e}_{i}", offset=((2 * e + i + 1) % (2 * E)) * RAW_BYTES)
                 nc.sync.dma_start(out=raw[e, i][:], in_=w[e].rearrange("(p j) i -> p j i", j=4))
             for q in [q for q in range(PAIRS) if FIRST_AFTER[q] == e]:
-                first[q] = keep.tile([P, 2, 4, BLK], F32, name=f"first{q}")
+                raw2[0, q] = keep.tile([P, 2, 4, BLK], F32, name=f"first{q}")
                 for u in range(2):
-                    nc.sync.dma_start(out=first[q][:, u], in_=w2[2 * q + u].rearrange("(p j) n -> p j n", j=4)[:, :, 0:BLK])
+                    nc.sync.dma_start(out=raw2[0, q][:, u], in_=w2[2 * q + u].rearrange("(p j) n -> p j n", j=4)[:, :, 0:BLK])
 
         def pair_at(r, q):
             return (r - 1) * SPAN + Y_BYTES - LAP + q * PAIR_BYTES
@@ -92,29 +91,34 @@ def tile_moe_tk_glu_silu_kernel(tc, xT, w1, w3, w2, gate, offs, pos1, pos2, pos3
             nc.sync.dma_start(out=gates[k][:], in_=gate[k, 0:P, :])
         load_w2(2, range(PAIRS))
 
-        xg = lane.tile([P, T, 4], BF16, name="xg", align_bytes=64, offset=(E - 1) * GROUP_BYTES)
+        xg = keep.tile([P, T, 4], BF16, name="xg", align_bytes=64)
         xv = xg[:].rearrange("p (h c i) j -> p h c j i", h=2, i=4)
         xr = x_raw[:].rearrange("p h j (c i) -> p h c j i", i=4)
-        nc.scalar.copy(xv[:, 0], xr[:, 0])
+        nc.vector.tensor_copy(xv[:, 0], xr[:, 0])
         nc.scalar.copy(xv[:, 1, 0:X_SCALAR], xr[:, 1, 0:X_SCALAR])
         nc.vector.tensor_copy(xv[:, 1, X_SCALAR:], xr[:, 1, X_SCALAR:])
         for h in range(2):
             toks = slice(h * T // 2, (h + 1) * T // 2)
             nc.vector.quantize_mx(out=xw[:, toks].bitcast(FP8X4), scales=xs[:, toks], in_=xg[:, toks].rearrange("p t j -> p (t j)"))
 
-        gw = keep.tile([P, S], U32, name="gw", align_bytes=64)
-        gs = keep.tile([P, S], U8, name="gs", align_bytes=64)
-        for h in range(2):
-            nc.vector.tensor_copy(gw[:, h * S // 2 : (h + 1) * S // 2], xw[:].indirect(offs_sb[:, h * S // 32 : (h + 1) * S // 32]))
-            nc.vector.tensor_copy(gs[:, h * S // 2 : (h + 1) * S // 2], xs[:].indirect(offs_sb[:, h * S // 32 : (h + 1) * S // 32]))
+        gw, gs = {}, {}
+
+        def gather(h):
+            pool, at = (keep, None) if h == 0 else (ring, 2 * E * RAW_BYTES)
+            gw[h] = pool.tile([P, S // 2], U32, name=f"gw{h}", align_bytes=64, offset=at)
+            gs[h] = pool.tile([P, S // 2], U8, name=f"gs{h}", align_bytes=64, offset=at and at + 2 * S)
+            nc.vector.tensor_copy(gw[h][:], xw[:].indirect(offs_sb[:, h * S // 32 : (h + 1) * S // 32]))
+            nc.vector.tensor_copy(gs[h][:], xs[:].indirect(offs_sb[:, h * S // 32 : (h + 1) * S // 32]))
+
+        gather(0)
 
         grouped, banks, sil, hb, hw, hs = {}, {}, {}, {}, {}, {}
 
         def group(e, i):
-            if i == 0 or e + 1 == E:
-                grouped[e, i] = lane.tile([P, 4 * H], BF16, name=f"grp{e}_{i}", align_bytes=64, offset=(e if i == 0 else 0) * GROUP_BYTES)
+            if e + i == 0:
+                grouped[e, i] = ring.tile([P, 4 * H], BF16, name="grp_first", align_bytes=64, offset=2 * E * RAW_BYTES)
             else:
-                grouped[e, i] = work.tile([P, 4 * H], BF16, name=f"grp{e}_{i}", tag="grp", align_bytes=64)
+                grouped[e, i] = work.tile([P, 4 * H], BF16, name=f"grp{e}_{i}", tag="grp", align_bytes=64, bufs=4)
             dst = grouped[e, i][:].rearrange("p (t m j) -> p m j t", t=4, j=4)
             src = raw[e, i][:].rearrange("p j (m t) -> p m j t", t=4)
             if i == 0 or e == 0:
@@ -129,47 +133,46 @@ def tile_moe_tk_glu_silu_kernel(tc, xT, w1, w3, w2, gate, offs, pos1, pos2, pos3
             cs = work.tile([P, H], U8, name=f"cs{e}_{i}", tag="cs", align_bytes=64, bufs=3)
             nc.vector.quantize_mx(out=cw[:].bitcast(FP8X4), scales=cs[:], in_=grouped[e, i][:])
             for c in range(2):
-                slots = slice(e * C + c * BLK, e * C + (c + 1) * BLK)
+                h, at = divmod(e * C + c * BLK, S // 2)
+                slots = slice(at, at + BLK)
                 banks[e, i, c] = psum.tile([P, 4, BLK], F32, name=f"bank{e}_{i}_{c}", offset=(4 * (e % 2) + 2 * i + c) * BANK_BYTES)
                 for t in range(4):
                     cols = slice(t * BLK, (t + 1) * BLK)
-                    nc.tensor.matmul_mx(out=banks[e, i, c][:, t, :], lhsT=cw[:, cols].bitcast(FP8X4), lhsT_scale=cs[:, cols], rhs=gw[:, slots].bitcast(FP8X4), rhs_scale=gs[:, slots], start=True, stop=True)
+                    nc.tensor.matmul_mx(out=banks[e, i, c][:, t, :], lhsT=cw[:, cols].bitcast(FP8X4), lhsT_scale=cs[:, cols], rhs=gw[h][:, slots].bitcast(FP8X4), rhs_scale=gs[h][:, slots], start=True, stop=True)
 
         def activate(e):
-            room = raw[e + 1, (e + 1) // (E - 1)] if e + 1 < E else ring.tile([P, 4, H], F32, name="room", offset=RAW_BYTES)
+            room = raw[e + 1, (e + 1) // (E - 1)] if e + 1 < E else ring.tile([P, 4, H], F32, name="room", offset=2 * RAW_BYTES)
             for c in range(2):
                 sil[e, c] = room[:, c, :].rearrange("p (c t) -> p c t", t=4)
                 nc.scalar.activation(sil[e, c], banks[e, 0, c][:].rearrange("p t c -> p c t"), SILU)
 
         def hidden(e):
-            hb[e] = work.tile([P, C, 4], BF16, name=f"hb{e}", tag="hb", align_bytes=64)
+            q, u = divmod(e, 2)
+            if u == 0:
+                hb[q] = work.tile([P, 2 * C, 4], BF16, name=f"hb{q}", tag="hb", align_bytes=64)
             for c in range(2):
-                nc.vector.tensor_tensor(hb[e][:, c * BLK : (c + 1) * BLK, :], banks[e, 1, c][:].rearrange("p t c -> p c t"), sil[e, c], MULT)
+                nc.vector.tensor_tensor(hb[q][:, u * C + c * BLK : u * C + (c + 1) * BLK, :], banks[e, 1, c][:].rearrange("p t c -> p c t"), sil[e, c], MULT)
 
-        def quantize_h(e):
-            hw[e] = keep.tile([P, C], U32, name=f"hw{e}", align_bytes=64)
-            hs[e] = keep.tile([P, C], U8, name=f"hs{e}", align_bytes=64)
-            nc.vector.quantize_mx(out=hw[e][:].bitcast(FP8X4), scales=hs[e][:], in_=hb[e][:].rearrange("p c t -> p (c t)"))
+        def quantize_h(q):
+            hw[q] = keep.tile([P, 2 * C], U32, name=f"hw{q}", align_bytes=64)
+            hs[q] = keep.tile([P, 2 * C], U8, name=f"hs{q}", align_bytes=64)
+            nc.vector.quantize_mx(out=hw[q][:].bitcast(FP8X4), scales=hs[q][:], in_=hb[q][:].rearrange("p c t -> p (c t)"))
 
         ys, w2g = {}, {}
 
         def group_w2(r, q):
             w2g[r, q] = work.tile([P, 2, BLK, 4], BF16, name=f"grp2_{r}_{q}", tag="grp2", align_bytes=64, bufs=3)
-            nc.scalar.copy(w2g[r, q][:].rearrange("p u (c i) j -> p u c j i", i=4), raw2[r, q][:].rearrange("p u j (c i) -> p u c j i", i=4))
+            copy = nc.vector.tensor_copy if q == 1 else nc.scalar.copy
+            copy(w2g[r, q][:].rearrange("p u (c i) j -> p u c j i", i=4), raw2[r, q][:].rearrange("p u j (c i) -> p u c j i", i=4))
 
         codes = {}
 
-        def first_rows(q):
-            w2g[0, q] = lane.tile([P, 2, BLK, 4], BF16, name=f"first_grp{q}", align_bytes=64, offset=((FIRST_AFTER[q] + 1) % E) * GROUP_BYTES + (q % 2) * GROUP_BYTES // 2)
-            nc.gpsimd.tensor_scalar(w2g[0, q][:], first[q][:].rearrange("p u j n -> p u n j"), 1.0, 0.0, MULT, ADD)
-
         def quantize_w2(r, q):
-            if r >= 0:
-                cw = work.tile([P, 2, BLK], U32, name=f"w2w{r}_{q}", tag="w2w", align_bytes=64, bufs=5)
-                cs = work.tile([P, 2, BLK], U8, name=f"w2s{r}_{q}", tag="w2s", align_bytes=64, bufs=5)
-                nc.vector.quantize_mx(out=cw[:].rearrange("p u n -> p (u n)").bitcast(FP8X4), scales=cs[:].rearrange("p u n -> p (u n)"), in_=w2g[r, q][:].rearrange("p u n j -> p (u n j)"))
-                for u in range(2):
-                    codes[r, 2 * q + u] = (cw[:, u], cs[:, u])
+            cw = work.tile([P, 2, BLK], U32, name=f"w2w{r}_{q}", tag="w2w", align_bytes=64, bufs=5)
+            cs = work.tile([P, 2, BLK], U8, name=f"w2s{r}_{q}", tag="w2s", align_bytes=64, bufs=5)
+            nc.vector.quantize_mx(out=cw[:].rearrange("p u n -> p (u n)").bitcast(FP8X4), scales=cs[:].rearrange("p u n -> p (u n)"), in_=w2g[r, q][:].rearrange("p u n j -> p (u n j)"))
+            for u in range(2):
+                codes[r, 2 * q + u] = (cw[:, u], cs[:, u])
 
         def project(r, q):
             if q == 0:
@@ -177,7 +180,7 @@ def tile_moe_tk_glu_silu_kernel(tc, xT, w1, w3, w2, gate, offs, pos1, pos2, pos3
             bank = psum.tile([P, 2, C], F32, name=f"bank_y{r}_{q}", offset=((0, 1, 4), (2, 3, 5), (6, 7, 0))[r][q] * BANK_BYTES)
             for u in range(2):
                 e = 2 * q + u
-                nc.tensor.matmul_mx(out=bank[:, u, :], lhsT=codes[r, e][0].bitcast(FP8X4), lhsT_scale=codes[r, e][1], rhs=hw[e][:].bitcast(FP8X4), rhs_scale=hs[e][:], start=True, stop=True)
+                nc.tensor.matmul_mx(out=bank[:, u, :], lhsT=codes[r, e][0].bitcast(FP8X4), lhsT_scale=codes[r, e][1], rhs=hw[q][:, u * C : (u + 1) * C].bitcast(FP8X4), rhs_scale=hs[q][:, u * C : (u + 1) * C], start=True, stop=True)
             nc.scalar.copy(ys[r][:, 2 * q * C : 2 * (q + 1) * C], bank[:].rearrange("p u c -> p (u c)"))
 
         prods, turned = {}, {}
@@ -185,8 +188,10 @@ def tile_moe_tk_glu_silu_kernel(tc, xT, w1, w3, w2, gate, offs, pos1, pos2, pos3
 
         def fetch(r, k, t0=0, t1=T):
             if (r, k) not in prods:
-                if k > 0 and r + 1 < ROWS:
-                    prods[r, k] = tail.tile([P, T], F32, name=f"prod{r}_{k}", offset=pair_at(r + 1, k) - (k - 1) * (ROW_BYTES - LAP))
+                if k == 1 and r + 1 < ROWS:
+                    prods[r, k] = tail.tile([P, T], F32, name=f"prod{r}_{k}", offset=pair_at(r + 1, 2) - (ROW_BYTES - LAP))
+                elif k == 2 and r + 2 < ROWS:
+                    prods[r, k] = tail.tile([P, T], F32, name=f"prod{r}_{k}", offset=pair_at(r + 2, 0) + LAP)
                 else:
                     prods[r, k] = scratch[r][:, k]
             nc.vector.tensor_tensor(prods[r, k][:, t0:t1], ys[r][:].indirect(pos_sb[k][:, t0 // 16 : t1 // 16]), gates[k][:, t0:t1], MULT)
@@ -209,44 +214,47 @@ def tile_moe_tk_glu_silu_kernel(tc, xT, w1, w3, w2, gate, offs, pos1, pos2, pos3
         for e in range(E - 1):
             group(e, 0)
             first_layer(e, 0)
+            if e == 0:
+                gather(1)
             if e > 0:
                 activate(e - 1)
                 hidden(e - 1)
             if e - 1 in FIRST_AFTER:
-                first_rows(FIRST_AFTER.index(e - 1))
+                group_w2(0, FIRST_AFTER.index(e - 1))
             group(e, 1)
-            if e > 0:
-                quantize_h(e - 1)
+            if e > 0 and e % 2 == 0:
+                quantize_h(e // 2 - 1)
             first_layer(e, 1)
             if e - 1 in FIRST_AFTER:
                 quantize_w2(0, FIRST_AFTER.index(e - 1))
         for i in range(2):
             group(E - 1, i)
             first_layer(E - 1, i)
-        first_rows(1)
-        first_rows(2)
         for e in (E - 2, E - 1):
             activate(e)
             hidden(e)
+        for q in (1, 2):
+            group_w2(0, q)
         quantize_w2(0, 1)
+        quantize_h(PAIRS - 1)
         quantize_w2(0, 2)
-        for e in (E - 2, E - 1):
-            quantize_h(e)
         group_w2(1, 0)
         quantize_w2(1, 0)
         for r in range(ROWS - 1):
             for q in range(PAIRS):
                 project(r, q)
+            fetch(r, 0)
             for q in (1, 2):
                 group_w2(r + 1, q)
             if r > 0:
                 add_turned(r - 1)
-            fetch(r, 0)
             for q in (1, 2):
                 quantize_w2(r + 1, q)
-                fetch(r, q)
+            fetch(r, 1)
             if r + 2 < ROWS:
                 group_w2(r + 2, 0)
+            fetch(r, 2)
+            if r + 2 < ROWS:
                 quantize_w2(r + 2, 0)
         r = ROWS - 1
         for q in range(PAIRS):

@@ -30,12 +30,12 @@ PAIR_BYTES = 2 * 4 * BLK * 4
 ROW_BYTES = T * 4
 Y_BYTES = S * 4
 LAP = 64
-SPAN = Y_BYTES - LAP + PAIRS * PAIR_BYTES
+WHOLE_BYTES = ROWS * PAIR_BYTES
+SPAN = PAIR_BYTES + ROW_BYTES + LAP + Y_BYTES
 WINDOW = 2 * T
-FIRST_AFTER = (3, 5, 5)
-LAST_SCALAR = 64
-X_SCALAR = 28
-W3_SCALAR = 42
+LAST_SCALAR = 40
+X_SCALAR = 44
+W3_SCALAR = 8
 
 
 def tile_moe_tk_glu_silu_kernel(tc, xT, w1, w3, w2, gate, offs, pos1, pos2, pos3, out):
@@ -61,45 +61,40 @@ def tile_moe_tk_glu_silu_kernel(tc, xT, w1, w3, w2, gate, offs, pos1, pos2, pos3
         xw = keep.tile([P, WINDOW], U32, name="xw", align_bytes=64)
         nc.vector.memset(xw[:, T:].bitcast(I32), 0)
 
-        x_raw = ring.tile([P, 2, 4, T // 2], F32, name="x_raw", offset=0)
-        for h in range(2):
-            nc.sync.dma_start(out=x_raw[:, h], in_=xT.rearrange("(p j) (h t) -> h p j t", j=4, h=2)[h])
+        x_raw = ring.tile([P, 4, T], F32, name="x_raw", offset=0)
+        nc.sync.dma_start(out=x_raw[:], in_=xT.rearrange("(p j) t -> p j t", j=4))
         nc.sync.dma_start(offs_sb[:], offs)
         raw, raw2, gates = {}, {}, {}
         for e in range(E):
             for i, w in enumerate((w1, w3)):
                 raw[e, i] = ring.tile([P, 4, H], F32, name=f"raw{e}_{i}", offset=((2 * e + i + 1) % (2 * E)) * RAW_BYTES)
                 nc.sync.dma_start(out=raw[e, i][:], in_=w[e].rearrange("(p j) i -> p j i", j=4))
-            for q in [q for q in range(PAIRS) if FIRST_AFTER[q] == e]:
-                raw2[0, q] = keep.tile([P, 2, 4, BLK], F32, name=f"first{q}")
-                for u in range(2):
-                    nc.sync.dma_start(out=raw2[0, q][:, u], in_=w2[2 * q + u].rearrange("(p j) n -> p j n", j=4)[:, :, 0:BLK])
+            if e == 0:
+                gate_cols = keep.tile([P, TOP, 4], F32, name="gate_cols")
+                nc.sync.dma_start(out=gate_cols[:], in_=gate[:, 0, :].rearrange("k (p b) -> p k b", b=4))
 
         def pair_at(r, q):
-            return (r - 1) * SPAN + Y_BYTES - LAP + q * PAIR_BYTES
+            return WHOLE_BYTES + r * SPAN + (q - 1) * PAIR_BYTES
 
-        def load_w2(r, pairs):
-            for q in pairs:
-                raw2[r, q] = tail.tile([P, 2, 4, BLK], F32, name=f"raw2_{r}_{q}", offset=pair_at(r, q))
+        whole = tail.tile([P, 2, 4, N], F32, name="whole", offset=0)
+        for u in range(2):
+            nc.sync.dma_start(out=whole[:, u], in_=w2[u].rearrange("(p j) n -> p j n", j=4))
+        for r in range(ROWS):
+            raw2[r, 0] = whole[:, :, :, r * BLK : (r + 1) * BLK]
+            for q in range(1, PAIRS):
+                raw2[r, q] = tail.tile([P, 2, 4, BLK], F32, name=f"raw2_{r}_{q}", offset=pair_at(r, q))[:]
                 for u in range(2):
                     nc.sync.dma_start(out=raw2[r, q][:, u], in_=w2[2 * q + u].rearrange("(p j) n -> p j n", j=4)[:, :, r * BLK : (r + 1) * BLK])
-
-        for k, src in enumerate((pos1, pos2, pos3)):
-            load_w2(1, [k])
-            nc.sync.dma_start(pos_sb[k][:], src)
-            gates[k] = keep.tile([P, T], F32, name=f"gate{k}")
-            nc.sync.dma_start(out=gates[k][:], in_=gate[k, 0:P, :])
-        load_w2(2, range(PAIRS))
+            if r == 0:
+                for k, src in enumerate((pos1, pos2, pos3)):
+                    nc.sync.dma_start(pos_sb[k][:], src)
 
         xg = keep.tile([P, T, 4], BF16, name="xg", align_bytes=64)
-        xv = xg[:].rearrange("p (h c i) j -> p h c j i", h=2, i=4)
-        xr = x_raw[:].rearrange("p h j (c i) -> p h c j i", i=4)
-        nc.vector.tensor_copy(xv[:, 0], xr[:, 0])
-        nc.scalar.copy(xv[:, 1, 0:X_SCALAR], xr[:, 1, 0:X_SCALAR])
-        nc.vector.tensor_copy(xv[:, 1, X_SCALAR:], xr[:, 1, X_SCALAR:])
-        for h in range(2):
-            toks = slice(h * T // 2, (h + 1) * T // 2)
-            nc.vector.quantize_mx(out=xw[:, toks].bitcast(FP8X4), scales=xs[:, toks], in_=xg[:, toks].rearrange("p t j -> p (t j)"))
+        xv = xg[:].rearrange("p (c i) j -> p c j i", i=4)
+        xr = x_raw[:].rearrange("p j (c i) -> p c j i", i=4)
+        nc.scalar.copy(xv[:, 0:X_SCALAR], xr[:, 0:X_SCALAR])
+        nc.vector.tensor_copy(xv[:, X_SCALAR:], xr[:, X_SCALAR:])
+        nc.vector.quantize_mx(out=xw[:, 0:T].bitcast(FP8X4), scales=xs[:, 0:T], in_=xg[:].rearrange("p t j -> p (t j)"))
 
         gw, gs = {}, {}
 
@@ -146,6 +141,19 @@ def tile_moe_tk_glu_silu_kernel(tc, xT, w1, w3, w2, gate, offs, pos1, pos2, pos3
                 sil[e, c] = room[:, c, :].rearrange("p (c t) -> p c t", t=4)
                 nc.scalar.activation(sil[e, c], banks[e, 0, c][:].rearrange("p t c -> p c t"), SILU)
 
+        gate_banks = {}
+
+        def spread_gate(k):
+            bank = psum.tile([P, 4, BLK], F32, name=f"bank_gate{k}", offset=4 * (k % 2) * BANK_BYTES)
+            for b in range(4):
+                nc.tensor.transpose(bank[:, b, :], gate_cols[:, k, b : b + 1].to_broadcast([P, P]), ident[:])
+            gate_banks[k] = bank
+
+        def keep_gate(k):
+            bank = gate_banks[k]
+            gates[k] = raw[k + 2, 0][:, 3, :]
+            nc.scalar.copy(gates[k].rearrange("p (c b) -> p c b", b=4), bank[:].rearrange("p b c -> p c b"))
+
         def hidden(e):
             q, u = divmod(e, 2)
             if u == 0:
@@ -161,22 +169,22 @@ def tile_moe_tk_glu_silu_kernel(tc, xT, w1, w3, w2, gate, offs, pos1, pos2, pos3
         ys, w2g = {}, {}
 
         def group_w2(r, q):
-            w2g[r, q] = work.tile([P, 2, BLK, 4], BF16, name=f"grp2_{r}_{q}", tag="grp2", align_bytes=64, bufs=3)
-            copy = nc.vector.tensor_copy if q == 1 else nc.scalar.copy
-            copy(w2g[r, q][:].rearrange("p u (c i) j -> p u c j i", i=4), raw2[r, q][:].rearrange("p u j (c i) -> p u c j i", i=4))
+            w2g[r, q] = work.tile([P, 2, BLK, 4], BF16, name=f"grp2_{r}_{q}", tag="grp2", align_bytes=64, bufs=4)
+            copy = nc.vector.tensor_copy if (r, q) in ((1, 0), (0, 2)) else nc.scalar.copy
+            copy(w2g[r, q][:].rearrange("p u (c i) j -> p u c j i", i=4), raw2[r, q].rearrange("p u j (c i) -> p u c j i", i=4))
 
         codes = {}
 
         def quantize_w2(r, q):
-            cw = work.tile([P, 2, BLK], U32, name=f"w2w{r}_{q}", tag="w2w", align_bytes=64, bufs=5)
-            cs = work.tile([P, 2, BLK], U8, name=f"w2s{r}_{q}", tag="w2s", align_bytes=64, bufs=5)
+            cw = work.tile([P, 2, BLK], U32, name=f"w2w{r}_{q}", tag="w2w", align_bytes=64, bufs=7)
+            cs = work.tile([P, 2, BLK], U8, name=f"w2s{r}_{q}", tag="w2s", align_bytes=64, bufs=7)
             nc.vector.quantize_mx(out=cw[:].rearrange("p u n -> p (u n)").bitcast(FP8X4), scales=cs[:].rearrange("p u n -> p (u n)"), in_=w2g[r, q][:].rearrange("p u n j -> p (u n j)"))
             for u in range(2):
                 codes[r, 2 * q + u] = (cw[:, u], cs[:, u])
 
         def project(r, q):
             if q == 0:
-                ys[r] = tail.tile([P, S], F32, name=f"y{r}", offset=r * SPAN if r + 1 < ROWS else pair_at(r, 2) + ROW_BYTES + LAP)
+                ys[r] = tail.tile([P, S], F32, name=f"y{r}", offset=pair_at(r, 2) + ROW_BYTES + LAP if r else pair_at(0, 1) - Y_BYTES + LAP)
             bank = psum.tile([P, 2, C], F32, name=f"bank_y{r}_{q}", offset=((0, 1, 4), (2, 3, 5), (6, 7, 0))[r][q] * BANK_BYTES)
             for u in range(2):
                 e = 2 * q + u
@@ -184,14 +192,14 @@ def tile_moe_tk_glu_silu_kernel(tc, xT, w1, w3, w2, gate, offs, pos1, pos2, pos3
             nc.scalar.copy(ys[r][:, 2 * q * C : 2 * (q + 1) * C], bank[:].rearrange("p u c -> p (u c)"))
 
         prods, turned = {}, {}
-        scratch = [ring.tile([P, 4, T], F32, name=f"scratch{r}", offset=(3 + r) * RAW_BYTES) for r in range(ROWS)]
+        scratch = [ring.tile([P, 4, T], F32, name=f"scratch{r}", offset=(3, 4, 6)[r] * RAW_BYTES) for r in range(ROWS)]
 
         def fetch(r, k, t0=0, t1=T):
             if (r, k) not in prods:
-                if k == 1 and r + 1 < ROWS:
+                if k == 2 and r + 1 < ROWS:
                     prods[r, k] = tail.tile([P, T], F32, name=f"prod{r}_{k}", offset=pair_at(r + 1, 2) - (ROW_BYTES - LAP))
-                elif k == 2 and r + 2 < ROWS:
-                    prods[r, k] = tail.tile([P, T], F32, name=f"prod{r}_{k}", offset=pair_at(r + 2, 0) + LAP)
+                elif k == 1 and r + 1 < ROWS:
+                    prods[r, k] = tail.tile([P, T], F32, name=f"prod{r}_{k}", offset=pair_at(r + 1, 1))
                 else:
                     prods[r, k] = scratch[r][:, k]
             nc.vector.tensor_tensor(prods[r, k][:, t0:t1], ys[r][:].indirect(pos_sb[k][:, t0 // 16 : t1 // 16]), gates[k][:, t0:t1], MULT)
@@ -213,55 +221,45 @@ def tile_moe_tk_glu_silu_kernel(tc, xT, w1, w3, w2, gate, offs, pos1, pos2, pos3
 
         for e in range(E - 1):
             group(e, 0)
+            if e >= 2:
+                keep_gate(e - 2)
             first_layer(e, 0)
             if e == 0:
                 gather(1)
             if e > 0:
                 activate(e - 1)
                 hidden(e - 1)
-            if e - 1 in FIRST_AFTER:
-                group_w2(0, FIRST_AFTER.index(e - 1))
+            if 0 < e <= TOP:
+                spread_gate(e - 1)
             group(e, 1)
             if e > 0 and e % 2 == 0:
                 quantize_h(e // 2 - 1)
             first_layer(e, 1)
-            if e - 1 in FIRST_AFTER:
-                quantize_w2(0, FIRST_AFTER.index(e - 1))
         for i in range(2):
             group(E - 1, i)
             first_layer(E - 1, i)
         for e in (E - 2, E - 1):
             activate(e)
             hidden(e)
-        for q in (1, 2):
-            group_w2(0, q)
-        quantize_w2(0, 1)
         quantize_h(PAIRS - 1)
-        quantize_w2(0, 2)
-        group_w2(1, 0)
-        quantize_w2(1, 0)
+        for r, q in [(r, 0) for r in range(ROWS)] + [(0, 1), (0, 2)]:
+            group_w2(r, q)
+            quantize_w2(r, q)
         for r in range(ROWS - 1):
             for q in range(PAIRS):
                 project(r, q)
             fetch(r, 0)
             for q in (1, 2):
                 group_w2(r + 1, q)
-            if r > 0:
-                add_turned(r - 1)
-            for q in (1, 2):
                 quantize_w2(r + 1, q)
-            fetch(r, 1)
-            if r + 2 < ROWS:
-                group_w2(r + 2, 0)
-            fetch(r, 2)
-            if r + 2 < ROWS:
-                quantize_w2(r + 2, 0)
+                fetch(r, q)
         r = ROWS - 1
         for q in range(PAIRS):
             project(r, q)
-        turn_back(r - 2)
-        add_turned(r - 1)
-        turn_back(r - 1)
+        add_turned(0)
+        add_turned(1)
+        turn_back(0)
+        turn_back(1)
         part = scratch[r][:, 3]
         res = work.tile([P, T], F32, name="res", bufs=1)
         fetch(r, 0)

@@ -23,19 +23,26 @@ BLK = 128
 S = E * C
 ROWS = N // BLK
 PAIRS = E // 2
+WINDOW = 2 * T
+
+X_SCALAR = 44
+W3_SCALAR = 24
+LAST_SCALAR = 64
+EARLY_AFTER = 1
+
 RAW_BYTES = 4 * H * 4
-BANK_BYTES = 2048
-GROUP_BYTES = 4 * H * 2
 PAIR_BYTES = 2 * 4 * BLK * 4
 ROW_BYTES = T * 4
 Y_BYTES = S * 4
-LAP = 64
-WHOLE_BYTES = ROWS * PAIR_BYTES
-SPAN = PAIR_BYTES + ROW_BYTES + LAP + Y_BYTES
-WINDOW = 2 * T
-LAST_SCALAR = 40
-X_SCALAR = 44
-W3_SCALAR = 8
+BANK_BYTES = 2048
+
+AT_01, AT_02, AT_11, AT_21, AT_10 = (n * PAIR_BYTES for n in range(5))
+AT_JOINT = AT_10 + Y_BYTES
+AT_20 = AT_JOINT + 2 * PAIR_BYTES
+
+Y_BANKS = ((0, 1, 4), (2, 3, 5), (6, 7, 0))
+SUM_BANKS = (1, 2)
+BACK_BANKS = (7, 3)
 
 
 def tile_moe_tk_glu_silu_kernel(tc, xT, w1, w3, w2, gate, offs, pos1, pos2, pos3, out):
@@ -43,7 +50,7 @@ def tile_moe_tk_glu_silu_kernel(tc, xT, w1, w3, w2, gate, offs, pos1, pos2, pos3
     with ExitStack() as ctx:
         lists = ctx.enter_context(tc.tile_pool(name="lists", bufs=1))
         keep = ctx.enter_context(tc.tile_pool(name="keep", bufs=1))
-        ring = ctx.enter_context(tc.tile_pool(name="ring", bufs=1))
+        slab = ctx.enter_context(tc.tile_pool(name="slab", bufs=1))
         work = ctx.enter_context(tc.tile_pool(name="work", bufs=2))
         tail = ctx.enter_context(tc.tile_pool(name="tail", bufs=1))
         psum = ctx.enter_context(tc.psum_pool(name="psum", bufs=1))
@@ -61,33 +68,45 @@ def tile_moe_tk_glu_silu_kernel(tc, xT, w1, w3, w2, gate, offs, pos1, pos2, pos3
         xw = keep.tile([P, WINDOW], U32, name="xw", align_bytes=64)
         nc.vector.memset(xw[:, T:].bitcast(I32), 0)
 
-        x_raw = ring.tile([P, 4, T], F32, name="x_raw", offset=0)
+        x_raw = slab.tile([P, 4, T], F32, name="x_raw", offset=0)
         nc.sync.dma_start(out=x_raw[:], in_=xT.rearrange("(p j) t -> p j t", j=4))
         nc.sync.dma_start(offs_sb[:], offs)
         raw, raw2, gates = {}, {}, {}
+
+        def load_pair(dst, q, n0, n1):
+            for u in range(2):
+                nc.sync.dma_start(out=dst[:, u], in_=w2[2 * q + u].rearrange("(p j) n -> p j n", j=4)[:, :, n0:n1])
+
         for e in range(E):
             for i, w in enumerate((w1, w3)):
-                raw[e, i] = ring.tile([P, 4, H], F32, name=f"raw{e}_{i}", offset=((2 * e + i + 1) % (2 * E)) * RAW_BYTES)
+                raw[e, i] = slab.tile([P, 4, H], F32, name=f"raw{e}_{i}", offset=((2 * e + i + 1) % (2 * E)) * RAW_BYTES)
                 nc.sync.dma_start(out=raw[e, i][:], in_=w[e].rearrange("(p j) i -> p j i", j=4))
-            if e == 0:
-                gate_cols = keep.tile([P, TOP, 4], F32, name="gate_cols")
-                nc.sync.dma_start(out=gate_cols[:], in_=gate[:, 0, :].rearrange("k (p b) -> p k b", b=4))
+            if e == EARLY_AFTER:
+                raw2[0, 0] = keep.tile([P, 2, 4, BLK], F32, name="raw2_0_0")[:]
+                load_pair(raw2[0, 0], 0, 0, BLK)
 
-        def pair_at(r, q):
-            return WHOLE_BYTES + r * SPAN + (q - 1) * PAIR_BYTES
+        def load_rows(r, q, at):
+            raw2[r, q] = tail.tile([P, 2, 4, BLK], F32, name=f"raw2_{r}_{q}", offset=at)[:]
+            load_pair(raw2[r, q], q, r * BLK, (r + 1) * BLK)
 
-        whole = tail.tile([P, 2, 4, N], F32, name="whole", offset=0)
-        for u in range(2):
-            nc.sync.dma_start(out=whole[:, u], in_=w2[u].rearrange("(p j) n -> p j n", j=4))
-        for r in range(ROWS):
-            raw2[r, 0] = whole[:, :, :, r * BLK : (r + 1) * BLK]
-            for q in range(1, PAIRS):
-                raw2[r, q] = tail.tile([P, 2, 4, BLK], F32, name=f"raw2_{r}_{q}", offset=pair_at(r, q))[:]
-                for u in range(2):
-                    nc.sync.dma_start(out=raw2[r, q][:, u], in_=w2[2 * q + u].rearrange("(p j) n -> p j n", j=4)[:, :, r * BLK : (r + 1) * BLK])
-            if r == 0:
-                for k, src in enumerate((pos1, pos2, pos3)):
-                    nc.sync.dma_start(pos_sb[k][:], src)
+        def load_gate(k):
+            nc.sync.dma_start(pos_sb[k][:], (pos1, pos2, pos3)[k])
+            gates[k] = keep.tile([P, T], F32, name=f"gate{k}")
+            nc.sync.dma_start(out=gates[k][:], in_=gate[k, 0:P, :])
+
+        load_rows(0, 1, AT_01)
+        load_rows(0, 2, AT_02)
+        load_rows(1, 0, AT_10)
+        load_gate(0)
+        load_rows(1, 1, AT_11)
+        load_gate(1)
+        joint = tail.tile([P, 2, 4, N - BLK], F32, name="joint", offset=AT_JOINT)
+        load_pair(joint[:], PAIRS - 1, BLK, N)
+        for r in range(1, ROWS):
+            raw2[r, PAIRS - 1] = joint[:, :, :, (r - 1) * BLK : r * BLK]
+        load_gate(2)
+        load_rows(2, 0, AT_20)
+        load_rows(2, 1, AT_21)
 
         xg = keep.tile([P, T, 4], BF16, name="xg", align_bytes=64)
         xv = xg[:].rearrange("p (c i) j -> p c j i", i=4)
@@ -98,12 +117,13 @@ def tile_moe_tk_glu_silu_kernel(tc, xT, w1, w3, w2, gate, offs, pos1, pos2, pos3
 
         gw, gs = {}, {}
 
-        def gather(h):
-            pool, at = (keep, None) if h == 0 else (ring, 2 * E * RAW_BYTES)
-            gw[h] = pool.tile([P, S // 2], U32, name=f"gw{h}", align_bytes=64, offset=at)
-            gs[h] = pool.tile([P, S // 2], U8, name=f"gs{h}", align_bytes=64, offset=at and at + 2 * S)
-            nc.vector.tensor_copy(gw[h][:], xw[:].indirect(offs_sb[:, h * S // 32 : (h + 1) * S // 32]))
-            nc.vector.tensor_copy(gs[h][:], xs[:].indirect(offs_sb[:, h * S // 32 : (h + 1) * S // 32]))
+        def gather(half):
+            pool, at = (keep, None) if half == 0 else (slab, 2 * E * RAW_BYTES)
+            gw[half] = pool.tile([P, S // 2], U32, name=f"gw{half}", align_bytes=64, offset=at)
+            gs[half] = pool.tile([P, S // 2], U8, name=f"gs{half}", align_bytes=64, offset=at and at + 2 * S)
+            entries = offs_sb[:, half * S // 32 : (half + 1) * S // 32]
+            nc.vector.tensor_copy(gw[half][:], xw[:].indirect(entries))
+            nc.vector.tensor_copy(gs[half][:], xs[:].indirect(entries))
 
         gather(0)
 
@@ -111,7 +131,7 @@ def tile_moe_tk_glu_silu_kernel(tc, xT, w1, w3, w2, gate, offs, pos1, pos2, pos3
 
         def group(e, i):
             if e + i == 0:
-                grouped[e, i] = ring.tile([P, 4 * H], BF16, name="grp_first", align_bytes=64, offset=2 * E * RAW_BYTES)
+                grouped[e, i] = slab.tile([P, 4 * H], BF16, name="grp_first", align_bytes=64, offset=2 * E * RAW_BYTES)
             else:
                 grouped[e, i] = work.tile([P, 4 * H], BF16, name=f"grp{e}_{i}", tag="grp", align_bytes=64, bufs=4)
             dst = grouped[e, i][:].rearrange("p (t m j) -> p m j t", t=4, j=4)
@@ -128,92 +148,75 @@ def tile_moe_tk_glu_silu_kernel(tc, xT, w1, w3, w2, gate, offs, pos1, pos2, pos3
             cs = work.tile([P, H], U8, name=f"cs{e}_{i}", tag="cs", align_bytes=64, bufs=3)
             nc.vector.quantize_mx(out=cw[:].bitcast(FP8X4), scales=cs[:], in_=grouped[e, i][:])
             for c in range(2):
-                h, at = divmod(e * C + c * BLK, S // 2)
+                half, at = divmod(e * C + c * BLK, S // 2)
                 slots = slice(at, at + BLK)
                 banks[e, i, c] = psum.tile([P, 4, BLK], F32, name=f"bank{e}_{i}_{c}", offset=(4 * (e % 2) + 2 * i + c) * BANK_BYTES)
                 for t in range(4):
                     cols = slice(t * BLK, (t + 1) * BLK)
-                    nc.tensor.matmul_mx(out=banks[e, i, c][:, t, :], lhsT=cw[:, cols].bitcast(FP8X4), lhsT_scale=cs[:, cols], rhs=gw[h][:, slots].bitcast(FP8X4), rhs_scale=gs[h][:, slots], start=True, stop=True)
+                    nc.tensor.matmul_mx(out=banks[e, i, c][:, t, :], lhsT=cw[:, cols].bitcast(FP8X4), lhsT_scale=cs[:, cols], rhs=gw[half][:, slots].bitcast(FP8X4), rhs_scale=gs[half][:, slots], start=True, stop=True)
 
         def activate(e):
-            room = raw[e + 1, (e + 1) // (E - 1)] if e + 1 < E else ring.tile([P, 4, H], F32, name="room", offset=2 * RAW_BYTES)
+            room = raw[e + 1, (e + 1) // (E - 1)] if e + 1 < E else slab.tile([P, 4, H], F32, name="room", offset=2 * RAW_BYTES)
             for c in range(2):
-                sil[e, c] = room[:, c, :].rearrange("p (c t) -> p c t", t=4)
-                nc.scalar.activation(sil[e, c], banks[e, 0, c][:].rearrange("p t c -> p c t"), SILU)
-
-        gate_banks = {}
-
-        def spread_gate(k):
-            bank = psum.tile([P, 4, BLK], F32, name=f"bank_gate{k}", offset=4 * (k % 2) * BANK_BYTES)
-            for b in range(4):
-                nc.tensor.transpose(bank[:, b, :], gate_cols[:, k, b : b + 1].to_broadcast([P, P]), ident[:])
-            gate_banks[k] = bank
-
-        def keep_gate(k):
-            bank = gate_banks[k]
-            gates[k] = raw[k + 2, 0][:, 3, :]
-            nc.scalar.copy(gates[k].rearrange("p (c b) -> p c b", b=4), bank[:].rearrange("p b c -> p c b"))
+                sil[e, c] = room[:, c, :].rearrange("p (s t) -> p s t", t=4)
+                nc.scalar.activation(sil[e, c], banks[e, 0, c][:].rearrange("p t s -> p s t"), SILU)
 
         def hidden(e):
             q, u = divmod(e, 2)
             if u == 0:
                 hb[q] = work.tile([P, 2 * C, 4], BF16, name=f"hb{q}", tag="hb", align_bytes=64)
             for c in range(2):
-                nc.vector.tensor_tensor(hb[q][:, u * C + c * BLK : u * C + (c + 1) * BLK, :], banks[e, 1, c][:].rearrange("p t c -> p c t"), sil[e, c], MULT)
+                nc.vector.tensor_tensor(hb[q][:, u * C + c * BLK : u * C + (c + 1) * BLK, :], banks[e, 1, c][:].rearrange("p t s -> p s t"), sil[e, c], MULT)
 
         def quantize_h(q):
             hw[q] = keep.tile([P, 2 * C], U32, name=f"hw{q}", align_bytes=64)
             hs[q] = keep.tile([P, 2 * C], U8, name=f"hs{q}", align_bytes=64)
-            nc.vector.quantize_mx(out=hw[q][:].bitcast(FP8X4), scales=hs[q][:], in_=hb[q][:].rearrange("p c t -> p (c t)"))
+            nc.vector.quantize_mx(out=hw[q][:].bitcast(FP8X4), scales=hs[q][:], in_=hb[q][:].rearrange("p s t -> p (s t)"))
 
-        ys, w2g = {}, {}
+        ys, w2g, codes = {}, {}, {}
 
         def group_w2(r, q):
-            w2g[r, q] = work.tile([P, 2, BLK, 4], BF16, name=f"grp2_{r}_{q}", tag="grp2", align_bytes=64, bufs=4)
-            copy = nc.vector.tensor_copy if (r, q) in ((1, 0), (0, 2)) else nc.scalar.copy
+            w2g[r, q] = work.tile([P, 2, BLK, 4], BF16, name=f"grp2_{r}_{q}", tag="grp2", align_bytes=64, bufs=3)
+            copy = nc.vector.tensor_copy if q == 1 else nc.scalar.copy
             copy(w2g[r, q][:].rearrange("p u (c i) j -> p u c j i", i=4), raw2[r, q].rearrange("p u j (c i) -> p u c j i", i=4))
-
-        codes = {}
 
         def quantize_w2(r, q):
             cw = work.tile([P, 2, BLK], U32, name=f"w2w{r}_{q}", tag="w2w", align_bytes=64, bufs=7)
             cs = work.tile([P, 2, BLK], U8, name=f"w2s{r}_{q}", tag="w2s", align_bytes=64, bufs=7)
             nc.vector.quantize_mx(out=cw[:].rearrange("p u n -> p (u n)").bitcast(FP8X4), scales=cs[:].rearrange("p u n -> p (u n)"), in_=w2g[r, q][:].rearrange("p u n j -> p (u n j)"))
-            for u in range(2):
-                codes[r, 2 * q + u] = (cw[:, u], cs[:, u])
+            codes[r, q] = (cw, cs)
 
         def project(r, q):
-            if q == 0:
-                ys[r] = tail.tile([P, S], F32, name=f"y{r}", offset=pair_at(r, 2) + ROW_BYTES + LAP if r else pair_at(0, 1) - Y_BYTES + LAP)
-            bank = psum.tile([P, 2, C], F32, name=f"bank_y{r}_{q}", offset=((0, 1, 4), (2, 3, 5), (6, 7, 0))[r][q] * BANK_BYTES)
+            if r not in ys:
+                ys[r] = tail.tile([P, S], F32, name=f"y{r}", offset=(AT_10, AT_JOINT + ROW_BYTES, AT_20 + ROW_BYTES)[r])
+            bank = psum.tile([P, 2, C], F32, name=f"bank_y{r}_{q}", offset=Y_BANKS[r][q] * BANK_BYTES)
+            cw, cs = codes[r, q]
             for u in range(2):
-                e = 2 * q + u
-                nc.tensor.matmul_mx(out=bank[:, u, :], lhsT=codes[r, e][0].bitcast(FP8X4), lhsT_scale=codes[r, e][1], rhs=hw[q][:, u * C : (u + 1) * C].bitcast(FP8X4), rhs_scale=hs[q][:, u * C : (u + 1) * C], start=True, stop=True)
-            nc.scalar.copy(ys[r][:, 2 * q * C : 2 * (q + 1) * C], bank[:].rearrange("p u c -> p (u c)"))
+                slots = slice(u * C, (u + 1) * C)
+                nc.tensor.matmul_mx(out=bank[:, u, :], lhsT=cw[:, u].bitcast(FP8X4), lhsT_scale=cs[:, u], rhs=hw[q][:, slots].bitcast(FP8X4), rhs_scale=hs[q][:, slots], start=True, stop=True)
+            nc.scalar.copy(ys[r][:, 2 * q * C : 2 * (q + 1) * C], bank[:].rearrange("p u s -> p (u s)"))
 
         prods, turned = {}, {}
-        scratch = [ring.tile([P, 4, T], F32, name=f"scratch{r}", offset=(3, 4, 6)[r] * RAW_BYTES) for r in range(ROWS)]
+        scratch = [slab.tile([P, 4, T], F32, name=f"scratch{r}", offset=(3, 4, 6)[r] * RAW_BYTES) for r in range(ROWS)]
 
         def fetch(r, k, t0=0, t1=T):
             if (r, k) not in prods:
-                if k == 2 and r + 1 < ROWS:
-                    prods[r, k] = tail.tile([P, T], F32, name=f"prod{r}_{k}", offset=pair_at(r + 1, 2) - (ROW_BYTES - LAP))
-                elif k == 1 and r + 1 < ROWS:
-                    prods[r, k] = tail.tile([P, T], F32, name=f"prod{r}_{k}", offset=pair_at(r + 1, 1))
+                if k == 1 and r + 1 < ROWS:
+                    prods[r, k] = tail.tile([P, T], F32, name=f"prod{r}_{k}", offset=(AT_JOINT, AT_21)[r])
                 else:
                     prods[r, k] = scratch[r][:, k]
             nc.vector.tensor_tensor(prods[r, k][:, t0:t1], ys[r][:].indirect(pos_sb[k][:, t0 // 16 : t1 // 16]), gates[k][:, t0:t1], MULT)
 
         def add_turned(r):
-            bank = psum.tile([P, 4, BLK], F32, name=f"bank_sum{r}", offset=(1 + r) * BANK_BYTES)
+            bank = psum.tile([P, 4, BLK], F32, name=f"bank_sum{r}", offset=SUM_BANKS[r] * BANK_BYTES)
             for b in range(4):
                 for k in range(TOP):
                     nc.tensor.matmul(bank[:, b, :], prods[r, k][:, b * BLK : (b + 1) * BLK], ident[:], start=k == 0, stop=k + 1 == TOP, is_transpose=True)
-            turned[r] = tail.tile([P, 4, BLK], F32, name="turned0", offset=pair_at(2, 2) + LAP)[:] if r == 0 else scratch[r][:, 1].rearrange("p (b n) -> p b n", b=4)
+            turned[r] = tail.tile([P, 4, BLK], F32, name="turned0", offset=AT_20)[:] if r == 0 else scratch[r][:, 1].rearrange("p (b n) -> p b n", b=4)
             nc.scalar.copy(turned[r], bank[:])
 
         def turn_back(r):
-            bank = psum.tile([P, 4, BLK], F32, name=f"bank_back{r}", offset=(7, 3)[r] * BANK_BYTES)
+            bank = psum.tile([P, 4, BLK], F32, name=f"bank_back{r}", offset=BACK_BANKS[r] * BANK_BYTES)
             for b in range(4):
                 nc.tensor.transpose(bank[:, b, :], turned[r][:, b, :], ident[:])
             nc.scalar.copy(scratch[r][:, 3], bank[:].rearrange("p b t -> p (b t)"))
@@ -221,53 +224,68 @@ def tile_moe_tk_glu_silu_kernel(tc, xT, w1, w3, w2, gate, offs, pos1, pos2, pos3
 
         for e in range(E - 1):
             group(e, 0)
-            if e >= 2:
-                keep_gate(e - 2)
             first_layer(e, 0)
             if e == 0:
                 gather(1)
             if e > 0:
                 activate(e - 1)
                 hidden(e - 1)
-            if 0 < e <= TOP:
-                spread_gate(e - 1)
             group(e, 1)
             if e > 0 and e % 2 == 0:
                 quantize_h(e // 2 - 1)
             first_layer(e, 1)
+            if e == EARLY_AFTER:
+                group_w2(0, 0)
+                quantize_w2(0, 0)
         for i in range(2):
             group(E - 1, i)
             first_layer(E - 1, i)
         for e in (E - 2, E - 1):
             activate(e)
             hidden(e)
+        for q in (1, 2):
+            group_w2(0, q)
+        quantize_w2(0, 1)
         quantize_h(PAIRS - 1)
-        for r, q in [(r, 0) for r in range(ROWS)] + [(0, 1), (0, 2)]:
-            group_w2(r, q)
-            quantize_w2(r, q)
-        for r in range(ROWS - 1):
-            for q in range(PAIRS):
-                project(r, q)
-            fetch(r, 0)
-            for q in (1, 2):
-                group_w2(r + 1, q)
-                quantize_w2(r + 1, q)
-                fetch(r, q)
-        r = ROWS - 1
+        quantize_w2(0, 2)
+        group_w2(1, 0)
+        quantize_w2(1, 0)
+
         for q in range(PAIRS):
-            project(r, q)
+            project(0, q)
+        fetch(0, 0)
+        for r, q in ((1, 1), (1, 2), (2, 2)):
+            group_w2(r, q)
+        for q in (1, 2):
+            quantize_w2(1, q)
+        fetch(0, 1)
+        fetch(0, 2)
+        quantize_w2(2, 2)
+
+        for q in range(PAIRS):
+            project(1, q)
+        fetch(1, 0)
+        for q in (0, 1):
+            group_w2(2, q)
+            quantize_w2(2, q)
+        fetch(1, 1)
+        fetch(1, 2)
+
+        last = ROWS - 1
+        for q in (2, 0, 1):
+            project(last, q)
         add_turned(0)
         add_turned(1)
         turn_back(0)
         turn_back(1)
-        part = scratch[r][:, 3]
+        part = scratch[last][:, 3]
         res = work.tile([P, T], F32, name="res", bufs=1)
-        fetch(r, 0)
-        fetch(r, 1)
-        fetch(r, 2, 0, T // 2)
-        nc.vector.tensor_tensor(part, prods[r, 0], prods[r, 1], ADD)
-        fetch(r, 2, T // 2, T)
-        for h in range(2):
-            cols = slice(h * T // 2, (h + 1) * T // 2)
-            nc.vector.tensor_tensor(res[:, cols], part[:, cols], prods[r, 2][:, cols], ADD)
-            nc.sync.dma_start(out=out[r * BLK : (r + 1) * BLK, cols], in_=res[:, cols])
+        fetch(last, 0)
+        fetch(last, 1)
+        fetch(last, 2, 0, T // 2)
+        nc.vector.tensor_tensor(part, prods[last, 0], prods[last, 1], ADD)
+        fetch(last, 2, T // 2, T)
+        for half in range(2):
+            cols = slice(half * T // 2, (half + 1) * T // 2)
+            nc.vector.tensor_tensor(res[:, cols], part[:, cols], prods[last, 2][:, cols], ADD)
+            nc.sync.dma_start(out=out[last * BLK : (last + 1) * BLK, cols], in_=res[:, cols])

@@ -26,9 +26,8 @@ PAIRS = E // 2
 WINDOW = 2 * T
 
 X_SCALAR = 44
-W3_SCALAR = 24
+W3_SCALAR = 36
 LAST_SCALAR = 64
-EARLY_AFTER = 1
 
 RAW_BYTES = 4 * H * 4
 PAIR_BYTES = 2 * 4 * BLK * 4
@@ -36,9 +35,8 @@ ROW_BYTES = T * 4
 Y_BYTES = S * 4
 BANK_BYTES = 2048
 
-AT_01, AT_02, AT_11, AT_21, AT_10 = (n * PAIR_BYTES for n in range(5))
-AT_JOINT = AT_10 + Y_BYTES
-AT_20 = AT_JOINT + 2 * PAIR_BYTES
+LAP = 64
+SPAN = PAIR_BYTES + ROW_BYTES + LAP + Y_BYTES
 
 Y_BANKS = ((0, 1, 4), (2, 3, 5), (6, 7, 0))
 SUM_BANKS = (1, 2)
@@ -73,40 +71,38 @@ def tile_moe_tk_glu_silu_kernel(tc, xT, w1, w3, w2, gate, offs, pos1, pos2, pos3
         nc.sync.dma_start(offs_sb[:], offs)
         raw, raw2, gates = {}, {}, {}
 
-        def load_pair(dst, q, n0, n1):
-            for u in range(2):
-                nc.sync.dma_start(out=dst[:, u], in_=w2[2 * q + u].rearrange("(p j) n -> p j n", j=4)[:, :, n0:n1])
-
         for e in range(E):
             for i, w in enumerate((w1, w3)):
                 raw[e, i] = slab.tile([P, 4, H], F32, name=f"raw{e}_{i}", offset=((2 * e + i + 1) % (2 * E)) * RAW_BYTES)
                 nc.sync.dma_start(out=raw[e, i][:], in_=w[e].rearrange("(p j) i -> p j i", j=4))
-            if e == EARLY_AFTER:
-                raw2[0, 0] = keep.tile([P, 2, 4, BLK], F32, name="raw2_0_0")[:]
-                load_pair(raw2[0, 0], 0, 0, BLK)
 
-        def load_rows(r, q, at):
-            raw2[r, q] = tail.tile([P, 2, 4, BLK], F32, name=f"raw2_{r}_{q}", offset=at)[:]
-            load_pair(raw2[r, q], q, r * BLK, (r + 1) * BLK)
+        def pair_at(r, q):
+            return r * SPAN + (q - 1) * PAIR_BYTES
+
+        def load_pair(dst, q, n0, n1):
+            for u in range(2):
+                nc.sync.dma_start(out=dst[:, u], in_=w2[2 * q + u].rearrange("(p j) n -> p j n", j=4)[:, :, n0:n1])
+
+        def load_rows(r):
+            for q in range(1, PAIRS):
+                raw2[r, q] = tail.tile([P, 2, 4, BLK], F32, name=f"raw2_{r}_{q}", offset=pair_at(r, q))[:]
+                load_pair(raw2[r, q], q, r * BLK, (r + 1) * BLK)
 
         def load_gate(k):
             nc.sync.dma_start(pos_sb[k][:], (pos1, pos2, pos3)[k])
             gates[k] = keep.tile([P, T], F32, name=f"gate{k}")
             nc.sync.dma_start(out=gates[k][:], in_=gate[k, 0:P, :])
 
-        load_rows(0, 1, AT_01)
-        load_rows(0, 2, AT_02)
-        load_rows(1, 0, AT_10)
+        whole = keep.tile([P, 2, 4, N], F32, name="whole")
+        load_pair(whole[:], 0, 0, N)
+        for r in range(ROWS):
+            raw2[r, 0] = whole[:, :, :, r * BLK : (r + 1) * BLK]
+        load_rows(0)
         load_gate(0)
-        load_rows(1, 1, AT_11)
+        load_rows(1)
         load_gate(1)
-        joint = tail.tile([P, 2, 4, N - BLK], F32, name="joint", offset=AT_JOINT)
-        load_pair(joint[:], PAIRS - 1, BLK, N)
-        for r in range(1, ROWS):
-            raw2[r, PAIRS - 1] = joint[:, :, :, (r - 1) * BLK : r * BLK]
         load_gate(2)
-        load_rows(2, 0, AT_20)
-        load_rows(2, 1, AT_21)
+        load_rows(2)
 
         xg = keep.tile([P, T, 4], BF16, name="xg", align_bytes=64)
         xv = xg[:].rearrange("p (c i) j -> p c j i", i=4)
@@ -176,19 +172,25 @@ def tile_moe_tk_glu_silu_kernel(tc, xT, w1, w3, w2, gate, offs, pos1, pos2, pos3
         ys, w2g, codes = {}, {}, {}
 
         def group_w2(r, q):
-            w2g[r, q] = work.tile([P, 2, BLK, 4], BF16, name=f"grp2_{r}_{q}", tag="grp2", align_bytes=64, bufs=3)
-            copy = nc.vector.tensor_copy if q == 1 else nc.scalar.copy
+            if q == 0 and r > 0:
+                w2g[r, q] = tail.tile([P, 2, BLK, 4], BF16, name=f"grp2_{r}_{q}", align_bytes=64, offset=(pair_at(0, 2) - (ROW_BYTES - LAP), pair_at(0, 1))[r - 1])
+            else:
+                w2g[r, q] = work.tile([P, 2, BLK, 4], BF16, name=f"grp2_{r}_{q}", tag="grp2", align_bytes=64, bufs=3)
+            copy = nc.vector.tensor_copy if (r, q) in ((0, 2), (1, 0)) else nc.scalar.copy
             copy(w2g[r, q][:].rearrange("p u (c i) j -> p u c j i", i=4), raw2[r, q].rearrange("p u j (c i) -> p u c j i", i=4))
 
         def quantize_w2(r, q):
-            cw = work.tile([P, 2, BLK], U32, name=f"w2w{r}_{q}", tag="w2w", align_bytes=64, bufs=7)
+            if (r, q) == (2, 0):
+                cw = tail.tile([P, 2, BLK], U32, name="w2w2_0", align_bytes=64, offset=pair_at(0, 2) + LAP)
+            else:
+                cw = work.tile([P, 2, BLK], U32, name=f"w2w{r}_{q}", tag="w2w", align_bytes=64, bufs=7)
             cs = work.tile([P, 2, BLK], U8, name=f"w2s{r}_{q}", tag="w2s", align_bytes=64, bufs=7)
             nc.vector.quantize_mx(out=cw[:].rearrange("p u n -> p (u n)").bitcast(FP8X4), scales=cs[:].rearrange("p u n -> p (u n)"), in_=w2g[r, q][:].rearrange("p u n j -> p (u n j)"))
             codes[r, q] = (cw, cs)
 
         def project(r, q):
-            if r not in ys:
-                ys[r] = tail.tile([P, S], F32, name=f"y{r}", offset=(AT_10, AT_JOINT + ROW_BYTES, AT_20 + ROW_BYTES)[r])
+            if q == 0:
+                ys[r] = tail.tile([P, S], F32, name=f"y{r}", offset=pair_at(r, 2) + ROW_BYTES + LAP)
             bank = psum.tile([P, 2, C], F32, name=f"bank_y{r}_{q}", offset=Y_BANKS[r][q] * BANK_BYTES)
             cw, cs = codes[r, q]
             for u in range(2):
@@ -201,8 +203,8 @@ def tile_moe_tk_glu_silu_kernel(tc, xT, w1, w3, w2, gate, offs, pos1, pos2, pos3
 
         def fetch(r, k, t0=0, t1=T):
             if (r, k) not in prods:
-                if k == 1 and r + 1 < ROWS:
-                    prods[r, k] = tail.tile([P, T], F32, name=f"prod{r}_{k}", offset=(AT_JOINT, AT_21)[r])
+                if k > 0 and r + 1 < ROWS:
+                    prods[r, k] = tail.tile([P, T], F32, name=f"prod{r}_{k}", offset=pair_at(r + 1, k) - (k - 1) * (ROW_BYTES - LAP))
                 else:
                     prods[r, k] = scratch[r][:, k]
             nc.vector.tensor_tensor(prods[r, k][:, t0:t1], ys[r][:].indirect(pos_sb[k][:, t0 // 16 : t1 // 16]), gates[k][:, t0:t1], MULT)
@@ -212,7 +214,7 @@ def tile_moe_tk_glu_silu_kernel(tc, xT, w1, w3, w2, gate, offs, pos1, pos2, pos3
             for b in range(4):
                 for k in range(TOP):
                     nc.tensor.matmul(bank[:, b, :], prods[r, k][:, b * BLK : (b + 1) * BLK], ident[:], start=k == 0, stop=k + 1 == TOP, is_transpose=True)
-            turned[r] = tail.tile([P, 4, BLK], F32, name="turned0", offset=AT_20)[:] if r == 0 else scratch[r][:, 1].rearrange("p (b n) -> p b n", b=4)
+            turned[r] = tail.tile([P, 4, BLK], F32, name="turned0", offset=pair_at(2, 2) + LAP)[:] if r == 0 else scratch[r][:, 1].rearrange("p (b n) -> p b n", b=4)
             nc.scalar.copy(turned[r], bank[:])
 
         def turn_back(r):
@@ -234,45 +236,32 @@ def tile_moe_tk_glu_silu_kernel(tc, xT, w1, w3, w2, gate, offs, pos1, pos2, pos3
             if e > 0 and e % 2 == 0:
                 quantize_h(e // 2 - 1)
             first_layer(e, 1)
-            if e == EARLY_AFTER:
-                group_w2(0, 0)
-                quantize_w2(0, 0)
         for i in range(2):
             group(E - 1, i)
             first_layer(E - 1, i)
         for e in (E - 2, E - 1):
             activate(e)
             hidden(e)
-        for q in (1, 2):
-            group_w2(0, q)
-        quantize_w2(0, 1)
         quantize_h(PAIRS - 1)
-        quantize_w2(0, 2)
-        group_w2(1, 0)
-        quantize_w2(1, 0)
-
         for q in range(PAIRS):
-            project(0, q)
-        fetch(0, 0)
-        for r, q in ((1, 1), (1, 2), (2, 2)):
-            group_w2(r, q)
-        for q in (1, 2):
-            quantize_w2(1, q)
-        fetch(0, 1)
-        fetch(0, 2)
-        quantize_w2(2, 2)
+            group_w2(0, q)
+            quantize_w2(0, q)
 
-        for q in range(PAIRS):
-            project(1, q)
-        fetch(1, 0)
-        for q in (0, 1):
-            group_w2(2, q)
-            quantize_w2(2, q)
-        fetch(1, 1)
-        fetch(1, 2)
+        for r in range(ROWS - 1):
+            for q in range(PAIRS):
+                project(r, q)
+            if r == 0:
+                for later in range(1, ROWS):
+                    group_w2(later, 0)
+                    quantize_w2(later, 0)
+            fetch(r, 0)
+            for q in (1, 2):
+                group_w2(r + 1, q)
+                quantize_w2(r + 1, q)
+                fetch(r, q)
 
         last = ROWS - 1
-        for q in (2, 0, 1):
+        for q in range(PAIRS):
             project(last, q)
         add_turned(0)
         add_turned(1)

@@ -130,8 +130,8 @@ def tile_moe_tk_glu_silu_kernel(tc, xT, w1, w3, w2, gate, offs, pos1, pos2, pos3
                 grouped[e, i] = slab.tile([P, 4 * H], BF16, name="grp_first", align_bytes=64, offset=2 * E * RAW_BYTES)
             else:
                 grouped[e, i] = work.tile([P, 4 * H], BF16, name=f"grp{e}_{i}", tag="grp", align_bytes=64, bufs=4)
-            dst = grouped[e, i][:].rearrange("p (t m j) -> p m j t", t=4, j=4)
-            src = raw[e, i][:].rearrange("p j (m t) -> p m j t", t=4)
+            dst = grouped[e, i][:].rearrange("p (t m g j) -> p m g t j", t=4, g=2, j=2)
+            src = raw[e, i][:].rearrange("p (g j) (m t) -> p m g t j", t=4, j=2)
             if i == 0 or e == 0:
                 nc.scalar.copy(dst, src)
             else:

@@ -25,22 +25,27 @@ ROWS = N // BLK
 PAIRS = E // 2
 WINDOW = 2 * T
 
+WHOLE = 3
+LATE = range(WHOLE, E)
+
 X_SCALAR = 44
-W3_SCALAR = 36
-LAST_SCALAR = 64
+W1_SCALAR = (128, 128, 32, 32, 16, 16)
+W3_SCALAR = (128, 64, 128, 128, 128, 80)
+W2_SCALAR = (96, 0, 96)
+ROWS0_SCALAR = (32, 0, 0)
+TIED = (0,)
 
 RAW_BYTES = 4 * H * 4
-PAIR_BYTES = 2 * 4 * BLK * 4
 ROW_BYTES = T * 4
 Y_BYTES = S * 4
 BANK_BYTES = 2048
-
 LAP = 64
-SPAN = PAIR_BYTES + ROW_BYTES + LAP + Y_BYTES
+SPAN = len(LATE) * (ROW_BYTES + LAP) + 12 * BLK + Y_BYTES
 
-Y_BANKS = ((0, 1, 4), (2, 3, 5), (6, 7, 0))
-SUM_BANKS = (1, 2)
-BACK_BANKS = (7, 3)
+GROUPS = ((0, 1), (2, 3), (4,), (5,))
+Y_BANKS = ((0, 1, 2, 3), (4, 5, 6, 7), (0, 1, 2, 3))
+SUM_BANKS = (4, 6)
+BACK_BANKS = (5, 7)
 
 
 def tile_moe_tk_glu_silu_kernel(tc, xT, w1, w3, w2, gate, offs, pos1, pos2, pos3, out):
@@ -71,38 +76,45 @@ def tile_moe_tk_glu_silu_kernel(tc, xT, w1, w3, w2, gate, offs, pos1, pos2, pos3
         nc.sync.dma_start(offs_sb[:], offs)
         raw, raw2, gates = {}, {}, {}
 
-        for e in range(E):
-            for i, w in enumerate((w1, w3)):
-                raw[e, i] = slab.tile([P, 4, H], F32, name=f"raw{e}_{i}", offset=((2 * e + i + 1) % (2 * E)) * RAW_BYTES)
-                nc.sync.dma_start(out=raw[e, i][:], in_=w[e].rearrange("(p j) i -> p j i", j=4))
+        def place(e, i):
+            return ((2 * e + i + 1) % (2 * E)) * RAW_BYTES
 
-        def pair_at(r, q):
-            return r * SPAN + (q - 1) * PAIR_BYTES
+        def load_first(e, i):
+            raw[e, i] = slab.tile([P, 4, H], F32, name=f"raw{e}_{i}", align_bytes=64, offset=place(e, i))
+            nc.sync.dma_start(out=raw[e, i][:], in_=(w1, w3)[i][e].rearrange("(p j) i -> p j i", j=4))
 
-        def load_pair(dst, q, n0, n1):
-            for u in range(2):
-                nc.sync.dma_start(out=dst[:, u], in_=w2[2 * q + u].rearrange("(p j) n -> p j n", j=4)[:, :, n0:n1])
+        def load_whole(e):
+            raw2[e] = tail.tile([P, 4, N], F32, name=f"whole{e}", offset=ROWS * SPAN + e * Y_BYTES)
+            nc.sync.dma_start(out=raw2[e][:], in_=w2[e].rearrange("(p j) n -> p j n", j=4))
 
-        def load_rows(r):
-            for q in range(1, PAIRS):
-                raw2[r, q] = tail.tile([P, 2, 4, BLK], F32, name=f"raw2_{r}_{q}", offset=pair_at(r, q))[:]
-                load_pair(raw2[r, q], q, r * BLK, (r + 1) * BLK)
+        def rows_at(r, e):
+            return r * SPAN + 12 * BLK + (e - WHOLE) * (ROW_BYTES + LAP)
+
+        def load_rows(r, e):
+            raw2[r, e] = tail.tile([P, 4, BLK], F32, name=f"raw2_{r}_{e}", offset=rows_at(r, e))
+            nc.sync.dma_start(out=raw2[r, e][:], in_=w2[e].rearrange("(p j) n -> p j n", j=4)[:, :, r * BLK : (r + 1) * BLK])
 
         def load_gate(k):
             nc.sync.dma_start(pos_sb[k][:], (pos1, pos2, pos3)[k])
             gates[k] = keep.tile([P, T], F32, name=f"gate{k}")
             nc.sync.dma_start(out=gates[k][:], in_=gate[k, 0:P, :])
 
-        whole = keep.tile([P, 2, 4, N], F32, name="whole")
-        load_pair(whole[:], 0, 0, N)
-        for r in range(ROWS):
-            raw2[r, 0] = whole[:, :, :, r * BLK : (r + 1) * BLK]
-        load_rows(0)
+        for e in range(E):
+            for i in range(2):
+                load_first(e, i)
+
+        for e in range(WHOLE):
+            load_whole(e)
+        for e in LATE:
+            load_rows(0, e)
         load_gate(0)
-        load_rows(1)
+        load_rows(1, 3)
         load_gate(1)
+        load_rows(1, 4)
+        load_rows(1, 5)
         load_gate(2)
-        load_rows(2)
+        for e in LATE:
+            load_rows(2, e)
 
         xg = keep.tile([P, T, 4], BF16, name="xg", align_bytes=64)
         xv = xg[:].rearrange("p (c i) j -> p c j i", i=4)
@@ -123,6 +135,16 @@ def tile_moe_tk_glu_silu_kernel(tc, xT, w1, w3, w2, gate, offs, pos1, pos2, pos3
 
         gather(0)
 
+        def shared_copy(dst, src, share):
+            cut = dst.shape[1] - share
+            if share > 0:
+                nc.scalar.copy(dst[:, cut:], src[:, cut:])
+            if cut > BLK // 2:
+                nc.vector.tensor_copy(dst[:, 0 : BLK // 2], src[:, 0 : BLK // 2])
+                nc.vector.tensor_copy(dst[:, BLK // 2 : cut], src[:, BLK // 2 : cut])
+            elif cut > 0:
+                nc.vector.tensor_copy(dst[:, 0:cut], src[:, 0:cut])
+
         grouped, banks, sil, hb, hw, hs = {}, {}, {}, {}, {}, {}
 
         def group(e, i):
@@ -132,12 +154,7 @@ def tile_moe_tk_glu_silu_kernel(tc, xT, w1, w3, w2, gate, offs, pos1, pos2, pos3
                 grouped[e, i] = work.tile([P, 4 * H], BF16, name=f"grp{e}_{i}", tag="grp", align_bytes=64, bufs=4)
             dst = grouped[e, i][:].rearrange("p (t m g j) -> p m g t j", t=4, g=2, j=2)
             src = raw[e, i][:].rearrange("p (g j) (m t) -> p m g t j", t=4, j=2)
-            if i == 0 or e == 0:
-                nc.scalar.copy(dst, src)
-            else:
-                cut = W3_SCALAR if e + 1 < E else LAST_SCALAR
-                nc.scalar.copy(dst[:, 0:cut], src[:, 0:cut])
-                nc.vector.tensor_copy(dst[:, cut:], src[:, cut:])
+            shared_copy(dst, src, (W1_SCALAR, W3_SCALAR)[i][e])
 
         def first_layer(e, i):
             cw = work.tile([P, H], U32, name=f"cw{e}_{i}", tag="cw", align_bytes=64, bufs=3)
@@ -152,59 +169,90 @@ def tile_moe_tk_glu_silu_kernel(tc, xT, w1, w3, w2, gate, offs, pos1, pos2, pos3
                     nc.tensor.matmul_mx(out=banks[e, i, c][:, t, :], lhsT=cw[:, cols].bitcast(FP8X4), lhsT_scale=cs[:, cols], rhs=gw[half][:, slots].bitcast(FP8X4), rhs_scale=gs[half][:, slots], start=True, stop=True)
 
         def activate(e):
-            room = raw[e + 1, (e + 1) // (E - 1)] if e + 1 < E else slab.tile([P, 4, H], F32, name="room", offset=2 * RAW_BYTES)
+            room = slab.tile([P, 2, BLK, 4], F32, name=f"sil{e}", offset=place(e + 1, 0) if e in TIED else place(e, 1))
             for c in range(2):
-                sil[e, c] = room[:, c, :].rearrange("p (s t) -> p s t", t=4)
+                sil[e, c] = room[:, c]
                 nc.scalar.activation(sil[e, c], banks[e, 0, c][:].rearrange("p t s -> p s t"), SILU)
 
-        def hidden(e):
-            q, u = divmod(e, 2)
-            if u == 0:
-                hb[q] = work.tile([P, 2 * C, 4], BF16, name=f"hb{q}", tag="hb", align_bytes=64)
-            for c in range(2):
-                nc.vector.tensor_tensor(hb[q][:, u * C + c * BLK : u * C + (c + 1) * BLK, :], banks[e, 1, c][:].rearrange("p t s -> p s t"), sil[e, c], MULT)
+        def hidden_last_chunk(e):
+            late = slab.tile([P, BLK, 4], BF16, name="hb_late", align_bytes=64, offset=place(e + 1, 1) + RAW_BYTES - 8 * BLK)
+            nc.vector.tensor_tensor(late[:], banks[e, 1, 1][:].rearrange("p t s -> p s t"), sil[e, 1], MULT)
+            nc.vector.quantize_mx(out=hw[e][:, BLK:C].bitcast(FP8X4), scales=hs[e][:, BLK:C], in_=late[:].rearrange("p s t -> p (s t)"))
 
-        def quantize_h(q):
-            hw[q] = keep.tile([P, 2 * C], U32, name=f"hw{q}", align_bytes=64)
-            hs[q] = keep.tile([P, 2 * C], U8, name=f"hs{q}", align_bytes=64)
-            nc.vector.quantize_mx(out=hw[q][:].bitcast(FP8X4), scales=hs[q][:], in_=hb[q][:].rearrange("p s t -> p (s t)"))
-
-        ys, w2g, codes = {}, {}, {}
-
-        def group_w2(r, q):
-            if q == 0 and r > 0:
-                w2g[r, q] = tail.tile([P, 2, BLK, 4], BF16, name=f"grp2_{r}_{q}", align_bytes=64, offset=(pair_at(0, 2) - (ROW_BYTES - LAP), pair_at(0, 1))[r - 1])
+        def hidden(e, cs=(0, 1)):
+            if e in hb:
+                pass
+            elif 0 < e < E - 1:
+                hb[e] = raw[e + 1, 0][:, 0, :].bitcast(BF16).rearrange("p (s t) -> p s t", t=4)
             else:
-                w2g[r, q] = work.tile([P, 2, BLK, 4], BF16, name=f"grp2_{r}_{q}", tag="grp2", align_bytes=64, bufs=3)
-            copy = nc.vector.tensor_copy if (r, q) in ((0, 2), (1, 0)) else nc.scalar.copy
-            copy(w2g[r, q][:].rearrange("p u (c i) j -> p u c j i", i=4), raw2[r, q].rearrange("p u j (c i) -> p u c j i", i=4))
+                hb[e] = work.tile([P, C, 4], BF16, name=f"hb{e}", tag="hb", align_bytes=64)
+            for c in cs:
+                nc.vector.tensor_tensor(hb[e][:, c * BLK : (c + 1) * BLK, :], banks[e, 1, c][:].rearrange("p t s -> p s t"), sil[e, c], MULT)
 
-        def quantize_w2(r, q):
-            if (r, q) == (2, 0):
-                cw = tail.tile([P, 2, BLK], U32, name="w2w2_0", align_bytes=64, offset=pair_at(0, 2) + LAP)
+        def quantize_h(e, n=C):
+            at = place(max(e, 1), 1) + RAW_BYTES // 2 + (e == 0) * 5 * C
+            hw[e] = slab.tile([P, C], U32, name=f"hw{e}", align_bytes=64, offset=at)
+            hs[e] = slab.tile([P, C], U8, name=f"hs{e}", align_bytes=64, offset=at + 4 * C)
+            nc.vector.quantize_mx(out=hw[e][:, 0:n].bitcast(FP8X4), scales=hs[e][:, 0:n], in_=hb[e][:, 0:n].rearrange("p s t -> p (s t)"))
+
+        ys, codes = {}, {}
+
+        def last_codes_at(r):
+            return r * SPAN + 8 * BLK - LAP
+
+        def group_w2(name, src, n, cut, at=None):
+            if at is None:
+                g = work.tile([P, n, 4], BF16, name=f"grp2_{name}", tag=f"grp2_{n}", align_bytes=64, bufs=3)
             else:
-                cw = work.tile([P, 2, BLK], U32, name=f"w2w{r}_{q}", tag="w2w", align_bytes=64, bufs=7)
-            cs = work.tile([P, 2, BLK], U8, name=f"w2s{r}_{q}", tag="w2s", align_bytes=64, bufs=7)
-            nc.vector.quantize_mx(out=cw[:].rearrange("p u n -> p (u n)").bitcast(FP8X4), scales=cs[:].rearrange("p u n -> p (u n)"), in_=w2g[r, q][:].rearrange("p u n j -> p (u n j)"))
-            codes[r, q] = (cw, cs)
+                g = tail.tile([P, n, 4], BF16, name=f"grp2_{name}", align_bytes=64, offset=at)
+            shared_copy(g[:].rearrange("p (c i) j -> p c j i", i=4), src.rearrange("p j (c i) -> p c j i", i=4), cut)
+            return g
 
-        def project(r, q):
-            if q == 0:
-                ys[r] = tail.tile([P, S], F32, name=f"y{r}", offset=pair_at(r, 2) + ROW_BYTES + LAP)
-            bank = psum.tile([P, 2, C], F32, name=f"bank_y{r}_{q}", offset=Y_BANKS[r][q] * BANK_BYTES)
-            cw, cs = codes[r, q]
-            for u in range(2):
-                slots = slice(u * C, (u + 1) * C)
-                nc.tensor.matmul_mx(out=bank[:, u, :], lhsT=cw[:, u].bitcast(FP8X4), lhsT_scale=cs[:, u], rhs=hw[q][:, slots].bitcast(FP8X4), rhs_scale=hs[q][:, slots], start=True, stop=True)
-            nc.scalar.copy(ys[r][:, 2 * q * C : 2 * (q + 1) * C], bank[:].rearrange("p u s -> p (u s)"))
+        def quantize_w2(name, g, at=None):
+            n = g.shape[1]
+            pool = keep if at is None else tail
+            cw = pool.tile([P, n], U32, name=f"w2w{name}", align_bytes=64, offset=at)
+            cs = keep.tile([P, n], U8, name=f"w2s{name}", align_bytes=64)
+            nc.vector.quantize_mx(out=cw[:].bitcast(FP8X4), scales=cs[:], in_=g.rearrange("p n j -> p (n j)"))
+            return cw, cs
+
+        whole_g = {}
+
+        def pack_whole(e):
+            whole_g[e] = group_w2(f"{e}", raw2[e][:], N, W2_SCALAR[e])
+            cw, cs = quantize_w2(f"0_{e}", whole_g[e][:, 0:BLK])
+            codes[0, e] = (cw[:], cs[:])
+
+        def pack_later(e):
+            cw, cs = quantize_w2(f"later{e}", whole_g[e][:, BLK:N], rows_at(0, WHOLE + e))
+            for r in range(1, ROWS):
+                codes[r, e] = (cw[:, (r - 1) * BLK : r * BLK], cs[:, (r - 1) * BLK : r * BLK])
+
+        def pack_rows(r, e):
+            g = group_w2(f"{r}_{e}", raw2[r, e][:], BLK, ROWS0_SCALAR[e - WHOLE] if r == 0 else BLK // 4, (r - 1) * SPAN if r > 0 and e == WHOLE else None)
+            cw, cs = quantize_w2(f"{r}_{e}", g[:], last_codes_at(r) if e == E - 1 else None)
+            codes[r, e] = (cw[:], cs[:])
+
+        def project(r, j):
+            experts = GROUPS[j]
+            if j == 0:
+                if r == 0:
+                    ys[r] = tail.tile([P, S], F32, name="y0", offset=ROWS * SPAN + (WHOLE - 1) * Y_BYTES)
+                else:
+                    ys[r] = tail.tile([P, S], F32, name=f"y{r}", offset=rows_at(r, E - 1) + ROW_BYTES - LAP)
+            bank = psum.tile([P, len(experts), C], F32, name=f"bank_y{r}_{j}", offset=Y_BANKS[r][j] * BANK_BYTES)
+            for u, e in enumerate(experts):
+                cw, cs = codes[r, e]
+                nc.tensor.matmul_mx(out=bank[:, u, :], lhsT=cw.bitcast(FP8X4), lhsT_scale=cs, rhs=hw[e][:].bitcast(FP8X4), rhs_scale=hs[e][:], start=True, stop=True)
+            nc.scalar.copy(ys[r][:, experts[0] * C : (experts[-1] + 1) * C], bank[:].rearrange("p u s -> p (u s)"))
 
         prods, turned = {}, {}
-        scratch = [slab.tile([P, 4, T], F32, name=f"scratch{r}", offset=(3, 4, 6)[r] * RAW_BYTES) for r in range(ROWS)]
+        scratch = [slab.tile([P, 4, T], F32, name=f"scratch{r}", offset=(3, 5, 7)[r] * RAW_BYTES) for r in range(ROWS)]
 
         def fetch(r, k, t0=0, t1=T):
             if (r, k) not in prods:
                 if k > 0 and r + 1 < ROWS:
-                    prods[r, k] = tail.tile([P, T], F32, name=f"prod{r}_{k}", offset=pair_at(r + 1, k) - (k - 1) * (ROW_BYTES - LAP))
+                    prods[r, k] = tail.tile([P, T], F32, name=f"prod{r}_{k}", offset=rows_at(r + 1, (E - 3, E - 1)[k - 1]) - LAP)
                 else:
                     prods[r, k] = scratch[r][:, k]
             nc.vector.tensor_tensor(prods[r, k][:, t0:t1], ys[r][:].indirect(pos_sb[k][:, t0 // 16 : t1 // 16]), gates[k][:, t0:t1], MULT)
@@ -214,7 +262,7 @@ def tile_moe_tk_glu_silu_kernel(tc, xT, w1, w3, w2, gate, offs, pos1, pos2, pos3
             for b in range(4):
                 for k in range(TOP):
                     nc.tensor.matmul(bank[:, b, :], prods[r, k][:, b * BLK : (b + 1) * BLK], ident[:], start=k == 0, stop=k + 1 == TOP, is_transpose=True)
-            turned[r] = tail.tile([P, 4, BLK], F32, name="turned0", offset=pair_at(2, 2) + LAP)[:] if r == 0 else scratch[r][:, 1].rearrange("p (b n) -> p b n", b=4)
+            turned[r] = scratch[r][:, 1].rearrange("p (b n) -> p b n", b=4)
             nc.scalar.copy(turned[r], bank[:])
 
         def turn_back(r):
@@ -222,47 +270,55 @@ def tile_moe_tk_glu_silu_kernel(tc, xT, w1, w3, w2, gate, offs, pos1, pos2, pos3
             for b in range(4):
                 nc.tensor.transpose(bank[:, b, :], turned[r][:, b, :], ident[:])
             nc.scalar.copy(scratch[r][:, 3], bank[:].rearrange("p b t -> p (b t)"))
-            nc.sync.dma_start(out=out[r * BLK : (r + 1) * BLK, :], in_=scratch[r][:, 3])
+            nc.scalar.dma_start(out=out[r * BLK : (r + 1) * BLK, :], in_=scratch[r][:, 3])
 
-        for e in range(E - 1):
-            group(e, 0)
-            first_layer(e, 0)
-            if e == 0:
-                gather(1)
-            if e > 0:
-                activate(e - 1)
-                hidden(e - 1)
+        group(0, 0)
+        first_layer(0, 0)
+        gather(1)
+        group(0, 1)
+        first_layer(0, 1)
+        group(1, 0)
+        first_layer(1, 0)
+        activate(0)
+        hidden(0)
+        for e in range(1, E - 1):
             group(e, 1)
-            if e > 0 and e % 2 == 0:
-                quantize_h(e // 2 - 1)
+            if e == 1:
+                quantize_h(0)
             first_layer(e, 1)
-        for i in range(2):
-            group(E - 1, i)
-            first_layer(E - 1, i)
-        for e in (E - 2, E - 1):
             activate(e)
-            hidden(e)
-        quantize_h(PAIRS - 1)
-        for q in range(PAIRS):
-            group_w2(0, q)
-            quantize_w2(0, q)
+            group(e + 1, 0)
+            hidden(e, (0,))
+            first_layer(e + 1, 0)
+            if e + 2 < E:
+                hidden(e, (1,))
+                quantize_h(e)
+        quantize_h(E - 2, BLK)
+        group(E - 1, 1)
+        activate(E - 1)
+        first_layer(E - 1, 1)
+        hidden_last_chunk(E - 2)
+        hidden(E - 1)
+        quantize_h(E - 1)
+        for e in range(WHOLE):
+            pack_whole(e)
+        for e in LATE:
+            pack_rows(0, e)
+        for e in range(WHOLE):
+            pack_later(e)
 
         for r in range(ROWS - 1):
-            for q in range(PAIRS):
-                project(r, q)
-            if r == 0:
-                for later in range(1, ROWS):
-                    group_w2(later, 0)
-                    quantize_w2(later, 0)
+            for j in range(len(GROUPS)):
+                project(r, j)
             fetch(r, 0)
-            for q in (1, 2):
-                group_w2(r + 1, q)
-                quantize_w2(r + 1, q)
-                fetch(r, q)
+            for e in LATE:
+                pack_rows(r + 1, e)
+                if e in (E - 3, E - 1):
+                    fetch(r, 1 if e == E - 3 else 2)
 
         last = ROWS - 1
-        for q in range(PAIRS):
-            project(last, q)
+        for j in range(len(GROUPS)):
+            project(last, j)
         add_turned(0)
         add_turned(1)
         turn_back(0)

@@ -27,12 +27,13 @@ WINDOW = 2 * T
 
 WHOLE = 3
 LATE = range(WHOLE, E)
+GATE1_BEFORE = 4
 
 X_SCALAR = 44
-W1_SCALAR = (128, 128, 32, 32, 16, 16)
-W3_SCALAR = (128, 64, 128, 128, 128, 80)
-W2_SCALAR = (96, 0, 96)
-ROWS0_SCALAR = (32, 0, 0)
+W1_SCALAR = (128, 128, 0, 0, 0, 0)
+W3_SCALAR = (128, 96, 128, 128, 128, 128)
+W2_SCALAR = (0, 96, 64)
+ROWS0_SCALAR = (32, 32, 0)
 TIED = (0,)
 
 RAW_BYTES = 4 * H * 4
@@ -108,10 +109,10 @@ def tile_moe_tk_glu_silu_kernel(tc, xT, w1, w3, w2, gate, offs, pos1, pos2, pos3
         for e in LATE:
             load_rows(0, e)
         load_gate(0)
-        load_rows(1, 3)
-        load_gate(1)
-        load_rows(1, 4)
-        load_rows(1, 5)
+        for e in LATE:
+            if e == GATE1_BEFORE:
+                load_gate(1)
+            load_rows(1, e)
         load_gate(2)
         for e in LATE:
             load_rows(2, e)
@@ -174,11 +175,6 @@ def tile_moe_tk_glu_silu_kernel(tc, xT, w1, w3, w2, gate, offs, pos1, pos2, pos3
                 sil[e, c] = room[:, c]
                 nc.scalar.activation(sil[e, c], banks[e, 0, c][:].rearrange("p t s -> p s t"), SILU)
 
-        def hidden_last_chunk(e):
-            late = slab.tile([P, BLK, 4], BF16, name="hb_late", align_bytes=64, offset=place(e + 1, 1) + RAW_BYTES - 8 * BLK)
-            nc.vector.tensor_tensor(late[:], banks[e, 1, 1][:].rearrange("p t s -> p s t"), sil[e, 1], MULT)
-            nc.vector.quantize_mx(out=hw[e][:, BLK:C].bitcast(FP8X4), scales=hs[e][:, BLK:C], in_=late[:].rearrange("p s t -> p (s t)"))
-
         def hidden(e, cs=(0, 1)):
             if e in hb:
                 pass
@@ -190,7 +186,7 @@ def tile_moe_tk_glu_silu_kernel(tc, xT, w1, w3, w2, gate, offs, pos1, pos2, pos3
                 nc.vector.tensor_tensor(hb[e][:, c * BLK : (c + 1) * BLK, :], banks[e, 1, c][:].rearrange("p t s -> p s t"), sil[e, c], MULT)
 
         def quantize_h(e, n=C):
-            at = place(max(e, 1), 1) + RAW_BYTES // 2 + (e == 0) * 5 * C
+            at = place(e + 1 if e < E - 2 else e, 1) + RAW_BYTES // 2 + (e == E - 2) * 5 * C
             hw[e] = slab.tile([P, C], U32, name=f"hw{e}", align_bytes=64, offset=at)
             hs[e] = slab.tile([P, C], U8, name=f"hs{e}", align_bytes=64, offset=at + 4 * C)
             nc.vector.quantize_mx(out=hw[e][:, 0:n].bitcast(FP8X4), scales=hs[e][:, 0:n], in_=hb[e][:, 0:n].rearrange("p s t -> p (s t)"))
@@ -224,7 +220,7 @@ def tile_moe_tk_glu_silu_kernel(tc, xT, w1, w3, w2, gate, offs, pos1, pos2, pos3
             codes[0, e] = (cw[:], cs[:])
 
         def pack_later(e):
-            cw, cs = quantize_w2(f"later{e}", whole_g[e][:, BLK:N], rows_at(0, WHOLE + e))
+            cw, cs = quantize_w2(f"later{e}", whole_g[e][:, BLK:N], rows_at(0, E - 1) + LAP + (e - 1) * 8 * BLK)
             for r in range(1, ROWS):
                 codes[r, e] = (cw[:, (r - 1) * BLK : r * BLK], cs[:, (r - 1) * BLK : r * BLK])
 
@@ -283,21 +279,17 @@ def tile_moe_tk_glu_silu_kernel(tc, xT, w1, w3, w2, gate, offs, pos1, pos2, pos3
         hidden(0)
         for e in range(1, E - 1):
             group(e, 1)
-            if e == 1:
-                quantize_h(0)
             first_layer(e, 1)
+            quantize_h(e - 1)
             activate(e)
             group(e + 1, 0)
             hidden(e, (0,))
             first_layer(e + 1, 0)
-            if e + 2 < E:
-                hidden(e, (1,))
-                quantize_h(e)
-        quantize_h(E - 2, BLK)
+            hidden(e, (1,))
+        quantize_h(E - 2)
         group(E - 1, 1)
         activate(E - 1)
         first_layer(E - 1, 1)
-        hidden_last_chunk(E - 2)
         hidden(E - 1)
         quantize_h(E - 1)
         for e in range(WHOLE):

@@ -22,29 +22,28 @@ P = 128
 BLK = 128
 S = E * C
 ROWS = N // BLK
-PAIRS = E // 2
+LAST = E - 1
 WINDOW = 2 * T
 
 WHOLE = 3
 LATE = range(WHOLE, E)
-GATE1_BEFORE = 4
 
 X_SCALAR = 44
-W1_SCALAR = (128, 128, 0, 0, 0, 0)
-W3_SCALAR = (128, 96, 128, 128, 128, 128)
-W2_SCALAR = (0, 96, 64)
-ROWS0_SCALAR = (32, 32, 0)
-TIED = (0,)
+W3_SECOND_SCALAR = 96
+W2_THIRD_SCALAR = 64
+VECTOR_PIECE = 64
 
 RAW_BYTES = 4 * H * 4
 ROW_BYTES = T * 4
 Y_BYTES = S * 4
+GROUPED_BYTES = 4 * BLK * 2
+WORDS_BYTES = BLK * 4
 BANK_BYTES = 2048
-LAP = 64
-SPAN = len(LATE) * (ROW_BYTES + LAP) + 12 * BLK + Y_BYTES
 
-GROUPS = ((0, 1), (2, 3), (4,), (5,))
-Y_BANKS = ((0, 1, 2, 3), (4, 5, 6, 7), (0, 1, 2, 3))
+LAP = 64
+SPAN = GROUPED_BYTES + WORDS_BYTES + len(LATE) * (ROW_BYTES + LAP) + Y_BYTES
+
+PARTS = ((0, 1), (2, 3), (4,), (5,))
 SUM_BANKS = (4, 6)
 BACK_BANKS = (5, 7)
 
@@ -62,9 +61,6 @@ def tile_moe_tk_glu_silu_kernel(tc, xT, w1, w3, w2, gate, offs, pos1, pos2, pos3
         offs_sb = lists.tile([P, S // 16], U16, name="offs_sb")
         pos_sb = [lists.tile([P, T // 16], U16, name=f"pos_sb{k}") for k in range(TOP)]
 
-        warm = keep.tile([P, 2], F32, name="warm")
-        nc.vector.memset(warm[:, 0:1], 0.0)
-        nc.scalar.activation(warm[:, 1:2], warm[:, 0:1], SILU)
         ident = keep.tile([P, P], F32, name="ident")
         make_identity(nc, ident[:])
         xs = keep.tile([P, WINDOW], U8, name="xs", align_bytes=64)
@@ -75,25 +71,20 @@ def tile_moe_tk_glu_silu_kernel(tc, xT, w1, w3, w2, gate, offs, pos1, pos2, pos3
         x_raw = slab.tile([P, 4, T], F32, name="x_raw", offset=0)
         nc.sync.dma_start(out=x_raw[:], in_=xT.rearrange("(p j) t -> p j t", j=4))
         nc.sync.dma_start(offs_sb[:], offs)
-        raw, raw2, gates = {}, {}, {}
+        raw, whole, rows, gates = {}, {}, {}, {}
 
-        def place(e, i):
+        def raw_at(e, i):
             return ((2 * e + i + 1) % (2 * E)) * RAW_BYTES
 
-        def load_first(e, i):
-            raw[e, i] = slab.tile([P, 4, H], F32, name=f"raw{e}_{i}", align_bytes=64, offset=place(e, i))
-            nc.sync.dma_start(out=raw[e, i][:], in_=(w1, w3)[i][e].rearrange("(p j) i -> p j i", j=4))
-
-        def load_whole(e):
-            raw2[e] = tail.tile([P, 4, N], F32, name=f"whole{e}", offset=ROWS * SPAN + e * Y_BYTES)
-            nc.sync.dma_start(out=raw2[e][:], in_=w2[e].rearrange("(p j) n -> p j n", j=4))
+        def whole_at(e):
+            return ROWS * SPAN + e * Y_BYTES
 
         def rows_at(r, e):
-            return r * SPAN + 12 * BLK + (e - WHOLE) * (ROW_BYTES + LAP)
+            return r * SPAN + GROUPED_BYTES + WORDS_BYTES + (e - WHOLE) * (ROW_BYTES + LAP)
 
         def load_rows(r, e):
-            raw2[r, e] = tail.tile([P, 4, BLK], F32, name=f"raw2_{r}_{e}", offset=rows_at(r, e))
-            nc.sync.dma_start(out=raw2[r, e][:], in_=w2[e].rearrange("(p j) n -> p j n", j=4)[:, :, r * BLK : (r + 1) * BLK])
+            rows[r, e] = tail.tile([P, 4, BLK], F32, name=f"raw2_{r}_{e}", offset=rows_at(r, e))
+            nc.sync.dma_start(out=rows[r, e][:], in_=w2[e].rearrange("(p j) n -> p j n", j=4)[:, :, r * BLK : (r + 1) * BLK])
 
         def load_gate(k):
             nc.sync.dma_start(pos_sb[k][:], (pos1, pos2, pos3)[k])
@@ -101,17 +92,18 @@ def tile_moe_tk_glu_silu_kernel(tc, xT, w1, w3, w2, gate, offs, pos1, pos2, pos3
             nc.sync.dma_start(out=gates[k][:], in_=gate[k, 0:P, :])
 
         for e in range(E):
-            for i in range(2):
-                load_first(e, i)
-
+            for i, w in enumerate((w1, w3)):
+                raw[e, i] = slab.tile([P, 4, H], F32, name=f"raw{e}_{i}", align_bytes=64, offset=raw_at(e, i))
+                nc.sync.dma_start(out=raw[e, i][:], in_=w[e].rearrange("(p j) i -> p j i", j=4))
         for e in range(WHOLE):
-            load_whole(e)
+            whole[e] = tail.tile([P, 4, N], F32, name=f"whole{e}", offset=whole_at(e))
+            nc.sync.dma_start(out=whole[e][:], in_=w2[e].rearrange("(p j) n -> p j n", j=4))
         for e in LATE:
             load_rows(0, e)
         load_gate(0)
-        for e in LATE:
-            if e == GATE1_BEFORE:
-                load_gate(1)
+        load_rows(1, WHOLE)
+        load_gate(1)
+        for e in LATE[1:]:
             load_rows(1, e)
         load_gate(2)
         for e in LATE:
@@ -125,9 +117,10 @@ def tile_moe_tk_glu_silu_kernel(tc, xT, w1, w3, w2, gate, offs, pos1, pos2, pos3
         nc.vector.quantize_mx(out=xw[:, 0:T].bitcast(FP8X4), scales=xs[:, 0:T], in_=xg[:].rearrange("p t j -> p (t j)"))
 
         gw, gs = {}, {}
+        first_at = 2 * E * RAW_BYTES
 
         def gather(half):
-            pool, at = (keep, None) if half == 0 else (slab, 2 * E * RAW_BYTES)
+            pool, at = (keep, None) if half == 0 else (slab, first_at)
             gw[half] = pool.tile([P, S // 2], U32, name=f"gw{half}", align_bytes=64, offset=at)
             gs[half] = pool.tile([P, S // 2], U8, name=f"gs{half}", align_bytes=64, offset=at and at + 2 * S)
             entries = offs_sb[:, half * S // 32 : (half + 1) * S // 32]
@@ -140,22 +133,20 @@ def tile_moe_tk_glu_silu_kernel(tc, xT, w1, w3, w2, gate, offs, pos1, pos2, pos3
             cut = dst.shape[1] - share
             if share > 0:
                 nc.scalar.copy(dst[:, cut:], src[:, cut:])
-            if cut > BLK // 2:
-                nc.vector.tensor_copy(dst[:, 0 : BLK // 2], src[:, 0 : BLK // 2])
-                nc.vector.tensor_copy(dst[:, BLK // 2 : cut], src[:, BLK // 2 : cut])
-            elif cut > 0:
-                nc.vector.tensor_copy(dst[:, 0:cut], src[:, 0:cut])
+            for g0 in range(0, cut, VECTOR_PIECE):
+                g1 = min(g0 + VECTOR_PIECE, cut)
+                nc.vector.tensor_copy(dst[:, g0:g1], src[:, g0:g1])
 
         grouped, banks, sil, hb, hw, hs = {}, {}, {}, {}, {}, {}
 
-        def group(e, i):
+        def group(e, i, share):
             if e + i == 0:
-                grouped[e, i] = slab.tile([P, 4 * H], BF16, name="grp_first", align_bytes=64, offset=2 * E * RAW_BYTES)
+                grouped[e, i] = slab.tile([P, 4 * H], BF16, name="grp_first", align_bytes=64, offset=first_at)
             else:
                 grouped[e, i] = work.tile([P, 4 * H], BF16, name=f"grp{e}_{i}", tag="grp", align_bytes=64, bufs=4)
             dst = grouped[e, i][:].rearrange("p (t m g j) -> p m g t j", t=4, g=2, j=2)
             src = raw[e, i][:].rearrange("p (g j) (m t) -> p m g t j", t=4, j=2)
-            shared_copy(dst, src, (W1_SCALAR, W3_SCALAR)[i][e])
+            shared_copy(dst, src, share)
 
         def first_layer(e, i):
             cw = work.tile([P, H], U32, name=f"cw{e}_{i}", tag="cw", align_bytes=64, bufs=3)
@@ -170,85 +161,77 @@ def tile_moe_tk_glu_silu_kernel(tc, xT, w1, w3, w2, gate, offs, pos1, pos2, pos3
                     nc.tensor.matmul_mx(out=banks[e, i, c][:, t, :], lhsT=cw[:, cols].bitcast(FP8X4), lhsT_scale=cs[:, cols], rhs=gw[half][:, slots].bitcast(FP8X4), rhs_scale=gs[half][:, slots], start=True, stop=True)
 
         def activate(e):
-            room = slab.tile([P, 2, BLK, 4], F32, name=f"sil{e}", offset=place(e + 1, 0) if e in TIED else place(e, 1))
+            room = slab.tile([P, 2, BLK, 4], F32, name=f"sil{e}", offset=raw_at(e, 1) if e > 0 else raw_at(1, 0))
             for c in range(2):
                 sil[e, c] = room[:, c]
                 nc.scalar.activation(sil[e, c], banks[e, 0, c][:].rearrange("p t s -> p s t"), SILU)
 
-        def hidden(e, cs=(0, 1)):
-            if e in hb:
-                pass
-            elif 0 < e < E - 1:
+        def hidden_tile(e):
+            if 0 < e < LAST:
                 hb[e] = raw[e + 1, 0][:, 0, :].bitcast(BF16).rearrange("p (s t) -> p s t", t=4)
             else:
                 hb[e] = work.tile([P, C, 4], BF16, name=f"hb{e}", tag="hb", align_bytes=64)
-            for c in cs:
-                nc.vector.tensor_tensor(hb[e][:, c * BLK : (c + 1) * BLK, :], banks[e, 1, c][:].rearrange("p t s -> p s t"), sil[e, c], MULT)
 
-        def quantize_h(e, n=C):
-            at = place(e + 1 if e < E - 2 else e, 1) + RAW_BYTES // 2 + (e == E - 2) * 5 * C
+        def hidden(e, c):
+            nc.vector.tensor_tensor(hb[e][:, c * BLK : (c + 1) * BLK, :], banks[e, 1, c][:].rearrange("p t s -> p s t"), sil[e, c], MULT)
+
+        def quantize_h(e):
+            at = raw_at(e + 1 if e < LAST - 1 else e, 1) + RAW_BYTES // 2
+            if e == LAST - 1:
+                at = at + 5 * C
             hw[e] = slab.tile([P, C], U32, name=f"hw{e}", align_bytes=64, offset=at)
             hs[e] = slab.tile([P, C], U8, name=f"hs{e}", align_bytes=64, offset=at + 4 * C)
-            nc.vector.quantize_mx(out=hw[e][:, 0:n].bitcast(FP8X4), scales=hs[e][:, 0:n], in_=hb[e][:, 0:n].rearrange("p s t -> p (s t)"))
+            nc.vector.quantize_mx(out=hw[e][:].bitcast(FP8X4), scales=hs[e][:], in_=hb[e][:].rearrange("p s t -> p (s t)"))
 
-        ys, codes = {}, {}
+        ys, codes, whole_grouped = {}, {}, {}
 
-        def last_codes_at(r):
-            return r * SPAN + 8 * BLK - LAP
-
-        def group_w2(name, src, n, cut, at=None):
+        def group_w2(name, src, n, share, at=None):
             if at is None:
                 g = work.tile([P, n, 4], BF16, name=f"grp2_{name}", tag=f"grp2_{n}", align_bytes=64, bufs=3)
             else:
                 g = tail.tile([P, n, 4], BF16, name=f"grp2_{name}", align_bytes=64, offset=at)
-            shared_copy(g[:].rearrange("p (c i) j -> p c j i", i=4), src.rearrange("p j (c i) -> p c j i", i=4), cut)
+            shared_copy(g[:].rearrange("p (c i) j -> p c j i", i=4), src.rearrange("p j (c i) -> p c j i", i=4), share)
             return g
 
         def quantize_w2(name, g, at=None):
             n = g.shape[1]
-            pool = keep if at is None else tail
-            cw = pool.tile([P, n], U32, name=f"w2w{name}", align_bytes=64, offset=at)
+            cw = (keep if at is None else tail).tile([P, n], U32, name=f"w2w{name}", align_bytes=64, offset=at)
             cs = keep.tile([P, n], U8, name=f"w2s{name}", align_bytes=64)
             nc.vector.quantize_mx(out=cw[:].bitcast(FP8X4), scales=cs[:], in_=g.rearrange("p n j -> p (n j)"))
             return cw, cs
 
-        whole_g = {}
-
-        def pack_whole(e):
-            whole_g[e] = group_w2(f"{e}", raw2[e][:], N, W2_SCALAR[e])
-            cw, cs = quantize_w2(f"0_{e}", whole_g[e][:, 0:BLK])
+        def pack_whole(e, share):
+            whole_grouped[e] = group_w2(f"{e}", whole[e][:], N, share)
+            cw, cs = quantize_w2(f"0_{e}", whole_grouped[e][:, 0:BLK])
             codes[0, e] = (cw[:], cs[:])
 
         def pack_later(e):
-            cw, cs = quantize_w2(f"later{e}", whole_g[e][:, BLK:N], rows_at(0, E - 1) + LAP + (e - 1) * 8 * BLK)
+            cw, cs = quantize_w2(f"later{e}", whole_grouped[e][:, BLK:N], rows_at(0, LAST) + LAP + (e - 1) * GROUPED_BYTES)
             for r in range(1, ROWS):
                 codes[r, e] = (cw[:, (r - 1) * BLK : r * BLK], cs[:, (r - 1) * BLK : r * BLK])
 
         def pack_rows(r, e):
-            g = group_w2(f"{r}_{e}", raw2[r, e][:], BLK, ROWS0_SCALAR[e - WHOLE] if r == 0 else BLK // 4, (r - 1) * SPAN if r > 0 and e == WHOLE else None)
-            cw, cs = quantize_w2(f"{r}_{e}", g[:], last_codes_at(r) if e == E - 1 else None)
+            share = 0 if (r, e) == (0, LAST) else BLK // 4
+            g = group_w2(f"{r}_{e}", rows[r, e][:], BLK, share, (r - 1) * SPAN if r > 0 and e == WHOLE else None)
+            cw, cs = quantize_w2(f"{r}_{e}", g[:], r * SPAN + GROUPED_BYTES - LAP if e == LAST else None)
             codes[r, e] = (cw[:], cs[:])
 
-        def project(r, j):
-            experts = GROUPS[j]
-            if j == 0:
-                if r == 0:
-                    ys[r] = tail.tile([P, S], F32, name="y0", offset=ROWS * SPAN + (WHOLE - 1) * Y_BYTES)
-                else:
-                    ys[r] = tail.tile([P, S], F32, name=f"y{r}", offset=rows_at(r, E - 1) + ROW_BYTES - LAP)
-            bank = psum.tile([P, len(experts), C], F32, name=f"bank_y{r}_{j}", offset=Y_BANKS[r][j] * BANK_BYTES)
-            for u, e in enumerate(experts):
-                cw, cs = codes[r, e]
-                nc.tensor.matmul_mx(out=bank[:, u, :], lhsT=cw.bitcast(FP8X4), lhsT_scale=cs, rhs=hw[e][:].bitcast(FP8X4), rhs_scale=hs[e][:], start=True, stop=True)
-            nc.scalar.copy(ys[r][:, experts[0] * C : (experts[-1] + 1) * C], bank[:].rearrange("p u s -> p (u s)"))
+        def project(r):
+            ys[r] = tail.tile([P, S], F32, name=f"y{r}", offset=whole_at(WHOLE - 1) if r == 0 else rows_at(r, LAST) + ROW_BYTES - LAP)
+            for j, experts in enumerate(PARTS):
+                bank = psum.tile([P, len(experts), C], F32, name=f"bank_y{r}_{j}", offset=(4 * (r % 2) + j) * BANK_BYTES)
+                for u, e in enumerate(experts):
+                    cw, cs = codes[r, e]
+                    nc.tensor.matmul_mx(out=bank[:, u, :], lhsT=cw.bitcast(FP8X4), lhsT_scale=cs, rhs=hw[e][:].bitcast(FP8X4), rhs_scale=hs[e][:], start=True, stop=True)
+                nc.scalar.copy(ys[r][:, experts[0] * C : (experts[-1] + 1) * C], bank[:].rearrange("p u s -> p (u s)"))
 
         prods, turned = {}, {}
-        scratch = [slab.tile([P, 4, T], F32, name=f"scratch{r}", offset=(3, 5, 7)[r] * RAW_BYTES) for r in range(ROWS)]
+        scratch = [slab.tile([P, 4, T], F32, name=f"scratch{r}", offset=raw_at(r + 1, 0)) for r in range(ROWS)]
 
         def fetch(r, k, t0=0, t1=T):
             if (r, k) not in prods:
                 if k > 0 and r + 1 < ROWS:
-                    prods[r, k] = tail.tile([P, T], F32, name=f"prod{r}_{k}", offset=rows_at(r + 1, (E - 3, E - 1)[k - 1]) - LAP)
+                    prods[r, k] = tail.tile([P, T], F32, name=f"prod{r}_{k}", offset=rows_at(r + 1, WHOLE if k == 1 else LAST) - LAP)
                 else:
                     prods[r, k] = scratch[r][:, k]
             nc.vector.tensor_tensor(prods[r, k][:, t0:t1], ys[r][:].indirect(pos_sb[k][:, t0 // 16 : t1 // 16]), gates[k][:, t0:t1], MULT)
@@ -268,53 +251,59 @@ def tile_moe_tk_glu_silu_kernel(tc, xT, w1, w3, w2, gate, offs, pos1, pos2, pos3
             nc.scalar.copy(scratch[r][:, 3], bank[:].rearrange("p b t -> p (b t)"))
             nc.scalar.dma_start(out=out[r * BLK : (r + 1) * BLK, :], in_=scratch[r][:, 3])
 
-        group(0, 0)
+        all_groups = H // 4
+        group(0, 0, all_groups)
         first_layer(0, 0)
         gather(1)
-        group(0, 1)
+        group(0, 1, all_groups)
         first_layer(0, 1)
-        group(1, 0)
+        group(1, 0, all_groups)
         first_layer(1, 0)
         activate(0)
-        hidden(0)
-        for e in range(1, E - 1):
-            group(e, 1)
+        hidden_tile(0)
+        for c in range(2):
+            hidden(0, c)
+        for e in range(1, LAST):
+            group(e, 1, W3_SECOND_SCALAR if e == 1 else all_groups)
             first_layer(e, 1)
             quantize_h(e - 1)
             activate(e)
-            group(e + 1, 0)
-            hidden(e, (0,))
+            group(e + 1, 0, 0)
+            hidden_tile(e)
+            hidden(e, 0)
             first_layer(e + 1, 0)
-            hidden(e, (1,))
-        quantize_h(E - 2)
-        group(E - 1, 1)
-        activate(E - 1)
-        first_layer(E - 1, 1)
-        hidden(E - 1)
-        quantize_h(E - 1)
-        for e in range(WHOLE):
-            pack_whole(e)
+            hidden(e, 1)
+        quantize_h(LAST - 1)
+        group(LAST, 1, all_groups)
+        activate(LAST)
+        first_layer(LAST, 1)
+        hidden_tile(LAST)
+        for c in range(2):
+            hidden(LAST, c)
+        quantize_h(LAST)
+
+        for e, share in enumerate((0, N // 4, W2_THIRD_SCALAR)):
+            pack_whole(e, share)
         for e in LATE:
             pack_rows(0, e)
         for e in range(WHOLE):
             pack_later(e)
 
         for r in range(ROWS - 1):
-            for j in range(len(GROUPS)):
-                project(r, j)
+            project(r)
             fetch(r, 0)
-            for e in LATE:
+            pack_rows(r + 1, WHOLE)
+            fetch(r, 1)
+            for e in LATE[1:]:
                 pack_rows(r + 1, e)
-                if e in (E - 3, E - 1):
-                    fetch(r, 1 if e == E - 3 else 2)
+            fetch(r, 2)
 
         last = ROWS - 1
-        for j in range(len(GROUPS)):
-            project(last, j)
-        add_turned(0)
-        add_turned(1)
-        turn_back(0)
-        turn_back(1)
+        project(last)
+        for r in range(last):
+            add_turned(r)
+        for r in range(last):
+            turn_back(r)
         part = scratch[last][:, 3]
         res = work.tile([P, T], F32, name="res", bufs=1)
         fetch(last, 0)

@@ -1,7 +1,6 @@
 from contextlib import ExitStack
 
 import concourse.mybir as mybir
-from concourse.masks import make_identity
 
 K, T, E, C, H, N = 512, 512, 6, 256, 512, 384
 TOP = 3
@@ -16,6 +15,7 @@ U8 = mybir.dt.uint8
 FP8X4 = mybir.dt.float8_e4m3fn_x4
 MULT = mybir.AluOpType.mult
 ADD = mybir.AluOpType.add
+EQUAL = mybir.AluOpType.is_equal
 SILU = mybir.ActivationFunctionType.Silu
 
 P = 128
@@ -62,19 +62,31 @@ def tile_moe_tk_glu_silu_kernel(tc, xT, w1, w3, w2, gate, offs, pos1, pos2, pos3
         pos_sb = [lists.tile([P, T // 16], U16, name=f"pos_sb{k}") for k in range(TOP)]
 
         ident = keep.tile([P, P], F32, name="ident")
-        make_identity(nc, ident[:])
+        nc.vector.memset(ident[:], 0.0)
+        ones = keep.tile([P, 32], F32, name="ones", align_bytes=64)
+        nc.vector.memset(ones[:], 1.0)
+        count = keep.tile([P, 32], F32, name="count", align_bytes=64)
+        nc.vector.tensor_tensor_scan(count[:], ones[:], ones[:], 0.0, MULT, ADD)
+        lane = keep.tile([P, 32], F32, name="lane", align_bytes=64)
+        nc.vector.transpose(lane[:], count[:])
+        for q in range(0, P, 32):
+            nc.vector.tensor_tensor(ident[q : q + 32, q : q + 32], count[q : q + 32, :], lane[q : q + 32, :], EQUAL)
+        warm = keep.tile([P, 1], F32, name="warm")
+        nc.scalar.activation(warm[:], ones[:, 0:1], SILU)
         xs = keep.tile([P, WINDOW], U8, name="xs", align_bytes=64)
         nc.vector.memset(xs[:].bitcast(I32), 0)
         xw = keep.tile([P, WINDOW], U32, name="xw", align_bytes=64)
         nc.vector.memset(xw[:, T:].bitcast(I32), 0)
 
+        gate_cols = keep.tile([P, TOP, 4], F32, name="gate_cols")
+        nc.sync.dma_start(out=gate_cols[:], in_=gate[:, 0, :].rearrange("k (p j) -> p k j", j=4))
         x_raw = slab.tile([P, 4, T], F32, name="x_raw", offset=0)
         nc.sync.dma_start(out=x_raw[:], in_=xT.rearrange("(p j) t -> p j t", j=4))
         nc.sync.dma_start(offs_sb[:], offs)
         raw, whole, rows, gates = {}, {}, {}, {}
 
         def raw_at(e, i):
-            return ((2 * e + i + 1) % (2 * E)) * RAW_BYTES
+            return (2 * e + i + 1) * RAW_BYTES
 
         def whole_at(e):
             return ROWS * SPAN + e * Y_BYTES
@@ -86,10 +98,8 @@ def tile_moe_tk_glu_silu_kernel(tc, xT, w1, w3, w2, gate, offs, pos1, pos2, pos3
             rows[r, e] = tail.tile([P, 4, BLK], F32, name=f"raw2_{r}_{e}", offset=rows_at(r, e))
             nc.sync.dma_start(out=rows[r, e][:], in_=w2[e].rearrange("(p j) n -> p j n", j=4)[:, :, r * BLK : (r + 1) * BLK])
 
-        def load_gate(k):
+        def load_pos(k):
             nc.sync.dma_start(pos_sb[k][:], (pos1, pos2, pos3)[k])
-            gates[k] = keep.tile([P, T], F32, name=f"gate{k}")
-            nc.sync.dma_start(out=gates[k][:], in_=gate[k, 0:P, :])
 
         for e in range(E):
             for i, w in enumerate((w1, w3)):
@@ -100,12 +110,9 @@ def tile_moe_tk_glu_silu_kernel(tc, xT, w1, w3, w2, gate, offs, pos1, pos2, pos3
             nc.sync.dma_start(out=whole[e][:], in_=w2[e].rearrange("(p j) n -> p j n", j=4))
         for e in LATE:
             load_rows(0, e)
-        load_gate(0)
-        load_rows(1, WHOLE)
-        load_gate(1)
-        for e in LATE[1:]:
+        for k, e in enumerate(LATE):
+            load_pos(k)
             load_rows(1, e)
-        load_gate(2)
         for e in LATE:
             load_rows(2, e)
 
@@ -116,8 +123,15 @@ def tile_moe_tk_glu_silu_kernel(tc, xT, w1, w3, w2, gate, offs, pos1, pos2, pos3
         nc.vector.tensor_copy(xv[:, X_SCALAR:], xr[:, X_SCALAR:])
         nc.vector.quantize_mx(out=xw[:, 0:T].bitcast(FP8X4), scales=xs[:, 0:T], in_=xg[:].rearrange("p t j -> p (t j)"))
 
+        for k in range(TOP):
+            bank = psum.tile([P, 4, P], F32, name=f"bank_gate{k}", offset=(5 + k) * BANK_BYTES)
+            for j in range(4):
+                nc.tensor.transpose(bank[:, j, :], gate_cols[:, k, j : j + 1].to_broadcast([P, P]), ident[:])
+            gates[k] = (keep if k == 0 else slab).tile([P, T], F32, name=f"gate{k}", offset=None if k == 0 else k * ROW_BYTES)
+            nc.scalar.copy(gates[k][:].rearrange("p (q j) -> p q j", j=4), bank[:].rearrange("p j q -> p q j"))
+
         gw, gs = {}, {}
-        first_at = 2 * E * RAW_BYTES
+        first_at = (2 * E + 1) * RAW_BYTES
 
         def gather(half):
             pool, at = (keep, None) if half == 0 else (slab, first_at)

@@ -27,6 +27,8 @@ WINDOW = 2 * T
 
 WHOLE = 3
 LATE = range(WHOLE, E)
+EARLY = 3
+STEPWISE = range(EARLY, E)
 
 X_SCALAR = 44
 W3_SECOND_SCALAR = 96
@@ -41,7 +43,11 @@ WORDS_BYTES = BLK * 4
 BANK_BYTES = 2048
 
 LAP = 64
-SPAN = GROUPED_BYTES + WORDS_BYTES + len(LATE) * (ROW_BYTES + LAP) + Y_BYTES
+WORDS_AT = GROUPED_BYTES - LAP
+SCALES_AT = 2 * GROUPED_BYTES + WORDS_BYTES - 2 * LAP
+GROUPED_AT = (0, WORDS_AT + WORDS_BYTES - LAP, SCALES_AT + BLK - LAP)
+ROWS_AT = 3 * GROUPED_BYTES + WORDS_BYTES + BLK
+SPAN = ROWS_AT + len(LATE) * (ROW_BYTES + LAP) + Y_BYTES
 
 PARTS = ((0, 1), (2, 3), (4,), (5,))
 SUM_BANKS = (4, 6)
@@ -71,8 +77,6 @@ def tile_moe_tk_glu_silu_kernel(tc, xT, w1, w3, w2, gate, offs, pos1, pos2, pos3
         nc.vector.transpose(lane[:], count[:])
         for q in range(0, P, 32):
             nc.vector.tensor_tensor(ident[q : q + 32, q : q + 32], count[q : q + 32, :], lane[q : q + 32, :], EQUAL)
-        warm = keep.tile([P, 1], F32, name="warm")
-        nc.scalar.activation(warm[:], ones[:, 0:1], SILU)
         xs = keep.tile([P, WINDOW], U8, name="xs", align_bytes=64)
         nc.vector.memset(xs[:].bitcast(I32), 0)
         xw = keep.tile([P, WINDOW], U32, name="xw", align_bytes=64)
@@ -92,7 +96,8 @@ def tile_moe_tk_glu_silu_kernel(tc, xT, w1, w3, w2, gate, offs, pos1, pos2, pos3
             return ROWS * SPAN + e * Y_BYTES
 
         def rows_at(r, e):
-            return r * SPAN + GROUPED_BYTES + WORDS_BYTES + (e - WHOLE) * (ROW_BYTES + LAP)
+            place = e - WHOLE if r > 0 else (e - LAST) % len(LATE)
+            return r * SPAN + ROWS_AT + place * (ROW_BYTES + LAP)
 
         def load_rows(r, e):
             rows[r, e] = tail.tile([P, 4, BLK], F32, name=f"raw2_{r}_{e}", offset=rows_at(r, e))
@@ -183,55 +188,57 @@ def tile_moe_tk_glu_silu_kernel(tc, xT, w1, w3, w2, gate, offs, pos1, pos2, pos3
         def hidden_tile(e):
             if 0 < e < LAST:
                 hb[e] = raw[e + 1, 0][:, 0, :].bitcast(BF16).rearrange("p (s t) -> p s t", t=4)
+            elif e == 0:
+                hb[e] = keep.tile([P, C, 4], BF16, name="hb0", align_bytes=64)
             else:
-                hb[e] = work.tile([P, C, 4], BF16, name=f"hb{e}", tag="hb", align_bytes=64)
+                flat = whole[0][:].rearrange("p j n -> p (j n)")
+                hb[e] = flat[:, BLK : BLK + 2 * C].bitcast(BF16).rearrange("p (s t) -> p s t", t=4)
 
         def hidden(e, c):
             nc.vector.tensor_tensor(hb[e][:, c * BLK : (c + 1) * BLK, :], banks[e, 1, c][:].rearrange("p t s -> p s t"), sil[e, c], MULT)
 
         def quantize_h(e):
-            at = raw_at(e + 1 if e < LAST - 1 else e, 1) + RAW_BYTES // 2
-            if e == LAST - 1:
+            at = raw_at(min(e + 1, LAST), 1) + RAW_BYTES // 2
+            if e == LAST:
                 at = at + 5 * C
             hw[e] = slab.tile([P, C], U32, name=f"hw{e}", align_bytes=64, offset=at)
             hs[e] = slab.tile([P, C], U8, name=f"hs{e}", align_bytes=64, offset=at + 4 * C)
             nc.vector.quantize_mx(out=hw[e][:].bitcast(FP8X4), scales=hs[e][:], in_=hb[e][:].rearrange("p s t -> p (s t)"))
 
-        ys, codes, whole_grouped = {}, {}, {}
+        ys, codes, whole_grouped, later = {}, {}, {}, {}
 
         def group_w2(name, src, n, share, at=None):
             if at is None:
-                g = work.tile([P, n, 4], BF16, name=f"grp2_{name}", tag=f"grp2_{n}", align_bytes=64, bufs=3)
+                g = work.tile([P, n, 4], BF16, name=f"grp2_{name}", tag=f"grp2_{n}", align_bytes=64, bufs=4 if n == BLK else 2)
             else:
                 g = tail.tile([P, n, 4], BF16, name=f"grp2_{name}", align_bytes=64, offset=at)
             shared_copy(g[:].rearrange("p (c i) j -> p c j i", i=4), src.rearrange("p j (c i) -> p c j i", i=4), share)
             return g
 
-        def quantize_w2(name, g, at=None):
+        def quantize_w2(name, g, at=None, scales_at=None):
             n = g.shape[1]
             cw = (keep if at is None else tail).tile([P, n], U32, name=f"w2w{name}", align_bytes=64, offset=at)
-            cs = keep.tile([P, n], U8, name=f"w2s{name}", align_bytes=64)
+            cs = (keep if scales_at is None else tail).tile([P, n], U8, name=f"w2s{name}", align_bytes=64, offset=scales_at)
             nc.vector.quantize_mx(out=cw[:].bitcast(FP8X4), scales=cs[:], in_=g.rearrange("p n j -> p (n j)"))
             return cw, cs
 
-        def pack_whole(e, share):
-            whole_grouped[e] = group_w2(f"{e}", whole[e][:], N, share)
-            cw, cs = quantize_w2(f"0_{e}", whole_grouped[e][:, 0:BLK])
-            codes[0, e] = (cw[:], cs[:])
+        def group_later(e):
+            at = rows_at(0, LAST) - LAP + GROUPED_BYTES if e == EARLY - 1 else None
+            later[e] = group_w2(f"later{e}", whole[e][:, :, BLK:N], N - BLK, 0, at)
 
         def pack_later(e):
-            cw, cs = quantize_w2(f"later{e}", whole_grouped[e][:, BLK:N], rows_at(0, LAST) + LAP + (e - 1) * GROUPED_BYTES)
+            cw, cs = quantize_w2(f"later{e}", later[e][:], rows_at(0, LAST) - LAP if e == 1 else None)
             for r in range(1, ROWS):
                 codes[r, e] = (cw[:, (r - 1) * BLK : r * BLK], cs[:, (r - 1) * BLK : r * BLK])
 
         def pack_rows(r, e):
             share = 0 if (r, e) == (0, LAST) else BLK // 4
-            g = group_w2(f"{r}_{e}", rows[r, e][:], BLK, share, (r - 1) * SPAN if r > 0 and e == WHOLE else None)
-            cw, cs = quantize_w2(f"{r}_{e}", g[:], r * SPAN + GROUPED_BYTES - LAP if e == LAST else None)
+            g = group_w2(f"{r}_{e}", rows[r, e][:] if e in LATE else whole[e][:, :, r * BLK : (r + 1) * BLK], BLK, share, (r - 1) * SPAN + GROUPED_AT[e - EARLY] if r > 0 else None)
+            cw, cs = quantize_w2(f"{r}_{e}", g[:], *((r * SPAN + WORDS_AT, r * SPAN + SCALES_AT) if e == LAST else ()))
             codes[r, e] = (cw[:], cs[:])
 
         def project(r):
-            ys[r] = tail.tile([P, S], F32, name=f"y{r}", offset=whole_at(WHOLE - 1) if r == 0 else rows_at(r, LAST) + ROW_BYTES - LAP)
+            ys[r] = tail.tile([P, S], F32, name=f"y{r}", offset=rows_at(r, LAST if r > 0 else LAST - 1) + ROW_BYTES - LAP)
             for j, experts in enumerate(PARTS):
                 bank = psum.tile([P, len(experts), C], F32, name=f"bank_y{r}_{j}", offset=(4 * (r % 2) + j) * BANK_BYTES)
                 for u, e in enumerate(experts):
@@ -245,7 +252,7 @@ def tile_moe_tk_glu_silu_kernel(tc, xT, w1, w3, w2, gate, offs, pos1, pos2, pos3
         def fetch(r, k, t0=0, t1=T):
             if (r, k) not in prods:
                 if k > 0 and r + 1 < ROWS:
-                    prods[r, k] = tail.tile([P, T], F32, name=f"prod{r}_{k}", offset=rows_at(r + 1, WHOLE if k == 1 else LAST) - LAP)
+                    prods[r, k] = tail.tile([P, T], F32, name=f"prod{r}_{k}", offset=rows_at(r + 1, LAST - 1 if k == 1 else LAST) - LAP)
                 else:
                     prods[r, k] = scratch[r][:, k]
             nc.vector.tensor_tensor(prods[r, k][:, t0:t1], ys[r][:].indirect(pos_sb[k][:, t0 // 16 : t1 // 16]), gates[k][:, t0:t1], MULT)
@@ -272,44 +279,50 @@ def tile_moe_tk_glu_silu_kernel(tc, xT, w1, w3, w2, gate, offs, pos1, pos2, pos3
         group(0, 1, all_groups)
         first_layer(0, 1)
         group(1, 0, all_groups)
-        first_layer(1, 0)
         activate(0)
+        group(1, 1, W3_SECOND_SCALAR)
+        first_layer(1, 0)
         hidden_tile(0)
         for c in range(2):
             hidden(0, c)
         for e in range(1, LAST):
-            group(e, 1, W3_SECOND_SCALAR if e == 1 else all_groups)
-            first_layer(e, 1)
-            quantize_h(e - 1)
-            activate(e)
             group(e + 1, 0, 0)
-            hidden_tile(e)
-            hidden(e, 0)
+            if e > 1:
+                group(e, 1, all_groups)
+            activate(e)
+            first_layer(e, 1)
             first_layer(e + 1, 0)
-            hidden(e, 1)
-        quantize_h(LAST - 1)
+            quantize_h(e - 1)
+            hidden_tile(e)
+            for c in range(2):
+                hidden(e, c)
         group(LAST, 1, all_groups)
         activate(LAST)
         first_layer(LAST, 1)
+        group_later(0)
+        quantize_h(LAST - 1)
+        pack_rows(0, 0)
         hidden_tile(LAST)
         for c in range(2):
             hidden(LAST, c)
+        pack_rows(0, 1)
         quantize_h(LAST)
-
-        for e, share in enumerate((0, N // 4, W2_THIRD_SCALAR)):
-            pack_whole(e, share)
-        for e in LATE:
+        group_later(1)
+        pack_rows(0, 2)
+        pack_later(0)
+        for e in STEPWISE:
             pack_rows(0, e)
-        for e in range(WHOLE):
-            pack_later(e)
+        group_later(2)
+        pack_later(1)
+        pack_later(2)
 
         for r in range(ROWS - 1):
             project(r)
             fetch(r, 0)
-            pack_rows(r + 1, WHOLE)
-            fetch(r, 1)
-            for e in LATE[1:]:
+            for e in STEPWISE[:-1]:
                 pack_rows(r + 1, e)
+            fetch(r, 1)
+            pack_rows(r + 1, LAST)
             fetch(r, 2)
 
         last = ROWS - 1

@@ -31,7 +31,7 @@ EARLY = 3
 STEPWISE = range(EARLY, E)
 
 X_SCALAR = 44
-W3_SECOND_SCALAR = 96
+W3_SECOND_SCALAR = 80
 W2_THIRD_SCALAR = 64
 VECTOR_PIECE = 64
 
@@ -67,6 +67,9 @@ def tile_moe_tk_glu_silu_kernel(tc, xT, w1, w3, w2, gate, offs, pos1, pos2, pos3
         offs_sb = lists.tile([P, S // 16], U16, name="offs_sb")
         pos_sb = [lists.tile([P, T // 16], U16, name=f"pos_sb{k}") for k in range(TOP)]
 
+        gate_rows = keep.tile([P, BLK], F32, name="gate_rows")
+        nc.vector.memset(gate_rows[:], 0.0)
+        pieces = gate.rearrange("k n (b c) -> (k n b) c", c=BLK)
         ident = keep.tile([P, P], F32, name="ident")
         nc.vector.memset(ident[:], 0.0)
         ones = keep.tile([P, 32], F32, name="ones", align_bytes=64)
@@ -77,15 +80,16 @@ def tile_moe_tk_glu_silu_kernel(tc, xT, w1, w3, w2, gate, offs, pos1, pos2, pos3
         nc.vector.transpose(lane[:], count[:])
         for q in range(0, P, 32):
             nc.vector.tensor_tensor(ident[q : q + 32, q : q + 32], count[q : q + 32, :], lane[q : q + 32, :], EQUAL)
+        warm = keep.tile([P, 1], F32, name="warm")
+        nc.scalar.activation(warm[:], ones[:, 0:1], SILU)
         xs = keep.tile([P, WINDOW], U8, name="xs", align_bytes=64)
         nc.vector.memset(xs[:].bitcast(I32), 0)
         xw = keep.tile([P, WINDOW], U32, name="xw", align_bytes=64)
         nc.vector.memset(xw[:, T:].bitcast(I32), 0)
 
-        gate_cols = keep.tile([P, TOP, 4], F32, name="gate_cols")
-        nc.sync.dma_start(out=gate_cols[:], in_=gate[:, 0, :].rearrange("k (p j) -> p k j", j=4))
         x_raw = slab.tile([P, 4, T], F32, name="x_raw", offset=0)
         nc.sync.dma_start(out=x_raw[:], in_=xT.rearrange("(p j) t -> p j t", j=4))
+        nc.sync.dma_start(out=gate_rows[0 : 4 * TOP, :], in_=pieces[0 : (4 * TOP - 1) * (N + 1) + 1 : N + 1, :])
         nc.sync.dma_start(offs_sb[:], offs)
         raw, whole, rows, gates = {}, {}, {}, {}
 
@@ -128,13 +132,18 @@ def tile_moe_tk_glu_silu_kernel(tc, xT, w1, w3, w2, gate, offs, pos1, pos2, pos3
         nc.vector.tensor_copy(xv[:, X_SCALAR:], xr[:, X_SCALAR:])
         nc.vector.quantize_mx(out=xw[:, 0:T].bitcast(FP8X4), scales=xs[:, 0:T], in_=xg[:].rearrange("p t j -> p (t j)"))
 
-        for k in range(TOP):
+        turned_rows = psum.tile([P, P], F32, name="bank_gate", offset=4 * BANK_BYTES)
+        nc.tensor.transpose(turned_rows[:], gate_rows[:], ident[:])
+        gate_cols = keep.tile([P, 4 * TOP], F32, name="gate_cols")
+        nc.scalar.copy(gate_cols[:], turned_rows[:, 0 : 4 * TOP])
+        def spread_gate(k):
             bank = psum.tile([P, 4, P], F32, name=f"bank_gate{k}", offset=(5 + k) * BANK_BYTES)
-            for j in range(4):
-                nc.tensor.transpose(bank[:, j, :], gate_cols[:, k, j : j + 1].to_broadcast([P, P]), ident[:])
-            gates[k] = (keep if k == 0 else slab).tile([P, T], F32, name=f"gate{k}", offset=None if k == 0 else k * ROW_BYTES)
-            nc.scalar.copy(gates[k][:].rearrange("p (q j) -> p q j", j=4), bank[:].rearrange("p j q -> p q j"))
+            for b in range(4):
+                nc.tensor.transpose(bank[:, b, :], gate_cols[:, 4 * k + b : 4 * k + b + 1].to_broadcast([P, P]), ident[:])
+            gates[k] = (keep if k == 0 else slab).tile([P, T], F32, name=f"gate{k}", offset=None if k == 0 else raw_at(0, 0) + k * ROW_BYTES)
+            nc.scalar.copy(gates[k][:], bank[:].rearrange("p b t -> p (b t)"))
 
+        spread_gate(0)
         gw, gs = {}, {}
         first_at = (2 * E + 1) * RAW_BYTES
 
@@ -274,6 +283,8 @@ def tile_moe_tk_glu_silu_kernel(tc, xT, w1, w3, w2, gate, offs, pos1, pos2, pos3
 
         all_groups = H // 4
         group(0, 0, all_groups)
+        for k in range(1, TOP):
+            spread_gate(k)
         first_layer(0, 0)
         gather(1)
         group(0, 1, all_groups)

@@ -17,6 +17,7 @@ MULT = mybir.AluOpType.mult
 ADD = mybir.AluOpType.add
 EQUAL = mybir.AluOpType.is_equal
 SILU = mybir.ActivationFunctionType.Silu
+COPY = mybir.ActivationFunctionType.Copy
 
 P = 128
 BLK = 128
@@ -50,8 +51,6 @@ ROWS_AT = 3 * GROUPED_BYTES + WORDS_BYTES + BLK
 SPAN = ROWS_AT + len(LATE) * (ROW_BYTES + LAP) + Y_BYTES
 
 PARTS = ((0, 1), (2, 3), (4,), (5,))
-SUM_BANKS = (4, 6)
-BACK_BANKS = (5, 7)
 
 
 def tile_moe_tk_glu_silu_kernel(tc, xT, w1, w3, w2, gate, offs, pos1, pos2, pos3, out):
@@ -258,28 +257,29 @@ def tile_moe_tk_glu_silu_kernel(tc, xT, w1, w3, w2, gate, offs, pos1, pos2, pos3
         prods, turned = {}, {}
         scratch = [slab.tile([P, 4, T], F32, name=f"scratch{r}", offset=raw_at(r + 1, 0)) for r in range(ROWS)]
 
-        def fetch(r, k, t0=0, t1=T):
-            if (r, k) not in prods:
-                if k > 0 and r + 1 < ROWS:
-                    prods[r, k] = tail.tile([P, T], F32, name=f"prod{r}_{k}", offset=rows_at(r + 1, LAST - 1 if k == 1 else LAST) - LAP)
-                else:
-                    prods[r, k] = scratch[r][:, k]
-            nc.vector.tensor_tensor(prods[r, k][:, t0:t1], ys[r][:].indirect(pos_sb[k][:, t0 // 16 : t1 // 16]), gates[k][:, t0:t1], MULT)
+        def fetch(r, k):
+            if k > 0:
+                prods[r, k] = tail.tile([P, T], F32, name=f"prod{r}_{k}", offset=rows_at(r + 1, LAST - 1 if k == 1 else LAST) - LAP)[:]
+            else:
+                prods[r, k] = scratch[r][:, k]
+            width = T // 2 if (r, k) == (1, TOP - 1) else T
+            for t0 in range(0, T, width):
+                nc.vector.tensor_tensor(prods[r, k][:, t0 : t0 + width], ys[r][:].indirect(pos_sb[k][:, t0 // 16 : (t0 + width) // 16]), gates[k][:, t0 : t0 + width], MULT)
 
-        def add_turned(r):
-            bank = psum.tile([P, 4, BLK], F32, name=f"bank_sum{r}", offset=SUM_BANKS[r] * BANK_BYTES)
-            for b in range(4):
+        def add_turned(r, blocks, at):
+            bank = psum.tile([P, len(blocks), BLK], F32, name=f"bank_sum{r}_{blocks[0]}", offset=at * BANK_BYTES)
+            for u, b in enumerate(blocks):
                 for k in range(TOP):
-                    nc.tensor.matmul(bank[:, b, :], prods[r, k][:, b * BLK : (b + 1) * BLK], ident[:], start=k == 0, stop=k + 1 == TOP, is_transpose=True)
-            turned[r] = scratch[r][:, 1].rearrange("p (b n) -> p b n", b=4)
-            nc.scalar.copy(turned[r], bank[:])
+                    nc.tensor.matmul(bank[:, u, :], prods[r, k][:, b * BLK : (b + 1) * BLK], ident[:], start=k == 0, stop=k + 1 == TOP, is_transpose=True)
+            nc.scalar.copy(scratch[r][:, 1, blocks[0] * BLK : (blocks[-1] + 1) * BLK], bank[:].rearrange("p b n -> p (b n)"))
 
-        def turn_back(r):
-            bank = psum.tile([P, 4, BLK], F32, name=f"bank_back{r}", offset=BACK_BANKS[r] * BANK_BYTES)
-            for b in range(4):
-                nc.tensor.transpose(bank[:, b, :], turned[r][:, b, :], ident[:])
-            nc.scalar.copy(scratch[r][:, 3], bank[:].rearrange("p b t -> p (b t)"))
-            nc.scalar.dma_start(out=out[r * BLK : (r + 1) * BLK, :], in_=scratch[r][:, 3])
+        def turn_back(r, blocks, at):
+            bank = psum.tile([P, len(blocks), BLK], F32, name=f"bank_back{r}_{blocks[0]}", offset=at * BANK_BYTES)
+            for u, b in enumerate(blocks):
+                nc.tensor.transpose(bank[:, u, :], scratch[r][:, 1, b * BLK : (b + 1) * BLK], ident[:])
+            cols = slice(blocks[0] * BLK, (blocks[-1] + 1) * BLK)
+            nc.scalar.copy(scratch[r][:, 3, cols], bank[:].rearrange("p b t -> p (b t)"))
+            nc.scalar.dma_start(out=out[r * BLK : (r + 1) * BLK, cols], in_=scratch[r][:, 3, cols])
 
         all_groups = H // 4
         group(0, 0, all_groups)
@@ -338,18 +338,28 @@ def tile_moe_tk_glu_silu_kernel(tc, xT, w1, w3, w2, gate, offs, pos1, pos2, pos3
 
         last = ROWS - 1
         project(last)
-        for r in range(last):
-            add_turned(r)
-        for r in range(last):
-            turn_back(r)
-        part = scratch[last][:, 3]
+        low, high = slice(0, T // 2), slice(T // 2, T)
+        prod = scratch[last]
+        picked = work.tile([P, 2, T], F32, name="picked", bufs=1)
+
+        def window(k, cols):
+            return ys[last][:].indirect(pos_sb[k][:, cols.start // 16 : cols.stop // 16])
+
+        nc.scalar.activation(picked[:, 0], window(2, slice(0, T)), COPY)
+        add_turned(0, (0, 1, 2, 3), 4)
+        add_turned(1, (0, 1), 6)
+        nc.scalar.activation(picked[:, 1, high], window(1, high), COPY)
+        add_turned(1, (2, 3), 7)
+        turn_back(0, (0, 1, 2, 3), 5)
+        turn_back(1, (0, 1), 4)
+        turn_back(1, (2, 3), 0)
         res = work.tile([P, T], F32, name="res", bufs=1)
-        fetch(last, 0)
-        fetch(last, 1)
-        fetch(last, 2, 0, T // 2)
-        nc.vector.tensor_tensor(part, prods[last, 0], prods[last, 1], ADD)
-        fetch(last, 2, T // 2, T)
-        for half in range(2):
-            cols = slice(half * T // 2, (half + 1) * T // 2)
-            nc.vector.tensor_tensor(res[:, cols], part[:, cols], prods[last, 2][:, cols], ADD)
+        nc.vector.tensor_tensor(prod[:, 0], window(0, slice(0, T)), gates[0][:], MULT)
+        nc.vector.tensor_tensor(prod[:, 1, low], window(1, low), gates[1][:, low], MULT)
+        nc.vector.tensor_tensor(prod[:, 2], picked[:, 0], gates[2][:], MULT)
+        nc.vector.tensor_tensor(prod[:, 1, high], picked[:, 1, high], gates[1][:, high], MULT)
+        for cols in (low, high):
+            nc.vector.tensor_tensor(prod[:, 3, cols], prod[:, 0, cols], prod[:, 2, cols], ADD)
+        for cols in (low, high):
+            nc.vector.tensor_tensor(res[:, cols], prod[:, 3, cols], prod[:, 1, cols], ADD)
             nc.sync.dma_start(out=out[last * BLK : (last + 1) * BLK, cols], in_=res[:, cols])

@@ -17,7 +17,6 @@ MULT = mybir.AluOpType.mult
 ADD = mybir.AluOpType.add
 EQUAL = mybir.AluOpType.is_equal
 SILU = mybir.ActivationFunctionType.Silu
-COPY = mybir.ActivationFunctionType.Copy
 
 P = 128
 BLK = 128
@@ -338,28 +337,24 @@ def tile_moe_tk_glu_silu_kernel(tc, xT, w1, w3, w2, gate, offs, pos1, pos2, pos3
 
         last = ROWS - 1
         project(last)
-        low, high = slice(0, T // 2), slice(T // 2, T)
-        prod = scratch[last]
-        picked = work.tile([P, 2, T], F32, name="picked", bufs=1)
-
-        def window(k, cols):
-            return ys[last][:].indirect(pos_sb[k][:, cols.start // 16 : cols.stop // 16])
-
-        nc.scalar.activation(picked[:, 0], window(2, slice(0, T)), COPY)
         add_turned(0, (0, 1, 2, 3), 4)
         add_turned(1, (0, 1), 6)
-        nc.scalar.activation(picked[:, 1, high], window(1, high), COPY)
         add_turned(1, (2, 3), 7)
         turn_back(0, (0, 1, 2, 3), 5)
         turn_back(1, (0, 1), 4)
         turn_back(1, (2, 3), 0)
+        low, high = slice(0, T // 2), slice(T // 2, T)
+        prod = scratch[last]
         res = work.tile([P, T], F32, name="res", bufs=1)
-        nc.vector.tensor_tensor(prod[:, 0], window(0, slice(0, T)), gates[0][:], MULT)
-        nc.vector.tensor_tensor(prod[:, 1, low], window(1, low), gates[1][:, low], MULT)
-        nc.vector.tensor_tensor(prod[:, 2], picked[:, 0], gates[2][:], MULT)
-        nc.vector.tensor_tensor(prod[:, 1, high], picked[:, 1, high], gates[1][:, high], MULT)
+
+        def fetch_last(k, cols):
+            nc.vector.tensor_tensor(prod[:, k, cols], ys[last][:].indirect(pos_sb[k][:, cols.start // 16 : cols.stop // 16]), gates[k][:, cols], MULT)
+
+        fetch_last(0, slice(0, T))
+        fetch_last(1, slice(0, T))
+        fetch_last(2, low)
+        nc.vector.tensor_tensor(prod[:, 3], prod[:, 0], prod[:, 1], ADD)
+        fetch_last(2, high)
         for cols in (low, high):
-            nc.vector.tensor_tensor(prod[:, 3, cols], prod[:, 0, cols], prod[:, 2, cols], ADD)
-        for cols in (low, high):
-            nc.vector.tensor_tensor(res[:, cols], prod[:, 3, cols], prod[:, 1, cols], ADD)
+            nc.vector.tensor_tensor(res[:, cols], prod[:, 3, cols], prod[:, 2, cols], ADD)
             nc.sync.dma_start(out=out[last * BLK : (last + 1) * BLK, cols], in_=res[:, cols])

@@ -256,20 +256,18 @@ def tile_moe_tk_glu_silu_kernel(tc, xT, w1, w3, w2, gate, offs, pos1, pos2, pos3
         prods, turned = {}, {}
         scratch = [slab.tile([P, 4, T], F32, name=f"scratch{r}", offset=raw_at(r + 1, 0)) for r in range(ROWS)]
 
-        def fetch(r, k):
-            if k > 0:
-                prods[r, k] = tail.tile([P, T], F32, name=f"prod{r}_{k}", offset=rows_at(r + 1, LAST - 1 if k == 1 else LAST) - LAP)[:]
-            else:
-                prods[r, k] = scratch[r][:, k]
-            width = T // 2 if (r, k) == (1, TOP - 1) else T
-            for t0 in range(0, T, width):
-                nc.vector.tensor_tensor(prods[r, k][:, t0 : t0 + width], ys[r][:].indirect(pos_sb[k][:, t0 // 16 : (t0 + width) // 16]), gates[k][:, t0 : t0 + width], MULT)
+        low, high, every = slice(0, T // 2), slice(T // 2, T), slice(0, T)
+
+        def fetch(dst, r, k, cols):
+            nc.vector.tensor_tensor(dst, ys[r][:].indirect(pos_sb[k][:, cols.start // 16 : cols.stop // 16]), gates[k][:, cols], MULT)
+            for u, b in enumerate(range(cols.start // BLK, cols.stop // BLK)):
+                prods[r, k, b] = dst[:, u * BLK : (u + 1) * BLK]
 
         def add_turned(r, blocks, at):
             bank = psum.tile([P, len(blocks), BLK], F32, name=f"bank_sum{r}_{blocks[0]}", offset=at * BANK_BYTES)
             for u, b in enumerate(blocks):
                 for k in range(TOP):
-                    nc.tensor.matmul(bank[:, u, :], prods[r, k][:, b * BLK : (b + 1) * BLK], ident[:], start=k == 0, stop=k + 1 == TOP, is_transpose=True)
+                    nc.tensor.matmul(bank[:, u, :], prods[r, k, b], ident[:], start=k == 0, stop=k + 1 == TOP, is_transpose=True)
             nc.scalar.copy(scratch[r][:, 1, blocks[0] * BLK : (blocks[-1] + 1) * BLK], bank[:].rearrange("p b n -> p (b n)"))
 
         def turn_back(r, blocks, at):
@@ -328,12 +326,16 @@ def tile_moe_tk_glu_silu_kernel(tc, xT, w1, w3, w2, gate, offs, pos1, pos2, pos3
 
         for r in range(ROWS - 1):
             project(r)
-            fetch(r, 0)
+            fetch(scratch[r][:, 0], r, 0, every)
             for e in STEPWISE[:-1]:
                 pack_rows(r + 1, e)
-            fetch(r, 1)
+            early = tail.tile([P, T // 2], F32, name=f"early{r}", offset=rows_at(r + 1, LAST - 1) - LAP)
+            fetch(early[:], r, 1, low)
             pack_rows(r + 1, LAST)
-            fetch(r, 2)
+            rest = tail.tile([P, 3, T // 2], F32, name=f"rest{r}", offset=rows_at(r + 1, LAST - 1) + ROW_BYTES // 2)
+            fetch(rest[:, 0], r, 1, high)
+            fetch(rest[:, 1], r, 2, low)
+            fetch(rest[:, 2], r, 2, high)
 
         last = ROWS - 1
         project(last)
@@ -343,18 +345,13 @@ def tile_moe_tk_glu_silu_kernel(tc, xT, w1, w3, w2, gate, offs, pos1, pos2, pos3
         turn_back(0, (0, 1, 2, 3), 5)
         turn_back(1, (0, 1), 4)
         turn_back(1, (2, 3), 0)
-        low, high = slice(0, T // 2), slice(T // 2, T)
         prod = scratch[last]
         res = work.tile([P, T], F32, name="res", bufs=1)
-
-        def fetch_last(k, cols):
-            nc.vector.tensor_tensor(prod[:, k, cols], ys[last][:].indirect(pos_sb[k][:, cols.start // 16 : cols.stop // 16]), gates[k][:, cols], MULT)
-
-        fetch_last(0, slice(0, T))
-        fetch_last(1, slice(0, T))
-        fetch_last(2, low)
+        fetch(prod[:, 0], last, 0, every)
+        fetch(prod[:, 1], last, 1, every)
+        fetch(prod[:, 2, low], last, 2, low)
         nc.vector.tensor_tensor(prod[:, 3], prod[:, 0], prod[:, 1], ADD)
-        fetch_last(2, high)
+        fetch(prod[:, 2, high], last, 2, high)
         for cols in (low, high):
             nc.vector.tensor_tensor(res[:, cols], prod[:, 3, cols], prod[:, 2, cols], ADD)
             nc.sync.dma_start(out=out[last * BLK : (last + 1) * BLK, cols], in_=res[:, cols])

@@ -327,11 +327,11 @@ def tile_moe_tk_glu_silu_kernel(tc, xT, w1, w3, w2, gate, offs, pos1, pos2, pos3
         for r in range(ROWS - 1):
             project(r)
             fetch(scratch[r][:, 0], r, 0, every)
-            for e in STEPWISE[:-1]:
-                pack_rows(r + 1, e)
-            early = tail.tile([P, T // 2], F32, name=f"early{r}", offset=rows_at(r + 1, LAST - 1) - LAP)
+            pack_rows(r + 1, EARLY)
+            early = tail.tile([P, T // 2], F32, name=f"early{r}", offset=rows_at(r + 1, EARLY))
             fetch(early[:], r, 1, low)
-            pack_rows(r + 1, LAST)
+            for e in STEPWISE[1:]:
+                pack_rows(r + 1, e)
             rest = tail.tile([P, 3, T // 2], F32, name=f"rest{r}", offset=rows_at(r + 1, LAST - 1) + ROW_BYTES // 2)
             fetch(rest[:, 0], r, 1, high)
             fetch(rest[:, 1], r, 2, low)

@@ -268,15 +268,16 @@ def tile_moe_tk_glu_silu_kernel(tc, xT, w1, w3, w2, gate, offs, pos1, pos2, pos3
             for u, b in enumerate(blocks):
                 for k in range(TOP):
                     nc.tensor.matmul(bank[:, u, :], prods[r, k, b], ident[:], start=k == 0, stop=k + 1 == TOP, is_transpose=True)
-            nc.scalar.copy(scratch[r][:, 1, blocks[0] * BLK : (blocks[-1] + 1) * BLK], bank[:].rearrange("p b n -> p (b n)"))
+            nc.scalar.copy(turned[r][:, blocks[0] * BLK : (blocks[-1] + 1) * BLK], bank[:].rearrange("p b n -> p (b n)"))
 
         def turn_back(r, blocks, at):
             bank = psum.tile([P, len(blocks), BLK], F32, name=f"bank_back{r}_{blocks[0]}", offset=at * BANK_BYTES)
             for u, b in enumerate(blocks):
-                nc.tensor.transpose(bank[:, u, :], scratch[r][:, 1, b * BLK : (b + 1) * BLK], ident[:])
+                nc.tensor.transpose(bank[:, u, :], turned[r][:, b * BLK : (b + 1) * BLK], ident[:])
             cols = slice(blocks[0] * BLK, (blocks[-1] + 1) * BLK)
             nc.scalar.copy(scratch[r][:, 3, cols], bank[:].rearrange("p b t -> p (b t)"))
-            nc.scalar.dma_start(out=out[r * BLK : (r + 1) * BLK, cols], in_=scratch[r][:, 3, cols])
+            if cols.stop == T:
+                nc.scalar.dma_start(out=out[r * BLK : (r + 1) * BLK, :], in_=scratch[r][:, 3])
 
         all_groups = H // 4
         group(0, 0, all_groups)
@@ -339,6 +340,8 @@ def tile_moe_tk_glu_silu_kernel(tc, xT, w1, w3, w2, gate, offs, pos1, pos2, pos3
 
         last = ROWS - 1
         project(last)
+        turned[0] = slab.tile([P, T], F32, name="turned0", offset=raw_at(LAST, 1) + RAW_BYTES // 2 + 5 * C)[:]
+        turned[1] = scratch[1][:, 1]
         add_turned(0, (0, 1, 2, 3), 4)
         add_turned(1, (0, 1), 6)
         add_turned(1, (2, 3), 7)
@@ -354,4 +357,4 @@ def tile_moe_tk_glu_silu_kernel(tc, xT, w1, w3, w2, gate, offs, pos1, pos2, pos3
         fetch(prod[:, 2, high], last, 2, high)
         for cols in (low, high):
             nc.vector.tensor_tensor(res[:, cols], prod[:, 3, cols], prod[:, 2, cols], ADD)
-            nc.sync.dma_start(out=out[last * BLK : (last + 1) * BLK, cols], in_=res[:, cols])
+        nc.sync.dma_start(out=out[last * BLK : (last + 1) * BLK, :], in_=res[:])

@@ -17,6 +17,7 @@ MULT = mybir.AluOpType.mult
 ADD = mybir.AluOpType.add
 EQUAL = mybir.AluOpType.is_equal
 SILU = mybir.ActivationFunctionType.Silu
+COPY = mybir.ActivationFunctionType.Copy
 
 P = 128
 BLK = 128
@@ -27,12 +28,9 @@ WINDOW = 2 * T
 
 WHOLE = 3
 LATE = range(WHOLE, E)
-EARLY = 3
-STEPWISE = range(EARLY, E)
 
 X_SCALAR = 44
 W3_SECOND_SCALAR = 80
-W2_THIRD_SCALAR = 64
 VECTOR_PIECE = 64
 
 RAW_BYTES = 4 * H * 4
@@ -50,6 +48,8 @@ ROWS_AT = 3 * GROUPED_BYTES + WORDS_BYTES + BLK
 SPAN = ROWS_AT + len(LATE) * (ROW_BYTES + LAP) + Y_BYTES
 
 PARTS = ((0, 1), (2, 3), (4,), (5,))
+SUMS = ((0, (0, 1, 2, 3), 4), (1, (0, 1), 6), (1, (2, 3), 7))
+BACKS = ((0, (0, 1, 2, 3), 5), (1, (0, 1), 4), (1, (2, 3), 0))
 
 
 def tile_moe_tk_glu_silu_kernel(tc, xT, w1, w3, w2, gate, offs, pos1, pos2, pos3, out):
@@ -134,6 +134,7 @@ def tile_moe_tk_glu_silu_kernel(tc, xT, w1, w3, w2, gate, offs, pos1, pos2, pos3
         nc.tensor.transpose(turned_rows[:], gate_rows[:], ident[:])
         gate_cols = keep.tile([P, 4 * TOP], F32, name="gate_cols")
         nc.scalar.copy(gate_cols[:], turned_rows[:, 0 : 4 * TOP])
+
         def spread_gate(k):
             bank = psum.tile([P, 4, P], F32, name=f"bank_gate{k}", offset=(5 + k) * BANK_BYTES)
             for b in range(4):
@@ -212,7 +213,7 @@ def tile_moe_tk_glu_silu_kernel(tc, xT, w1, w3, w2, gate, offs, pos1, pos2, pos3
             hs[e] = slab.tile([P, C], U8, name=f"hs{e}", align_bytes=64, offset=at + 4 * C)
             nc.vector.quantize_mx(out=hw[e][:].bitcast(FP8X4), scales=hs[e][:], in_=hb[e][:].rearrange("p s t -> p (s t)"))
 
-        ys, codes, whole_grouped, later = {}, {}, {}, {}
+        ys, codes, later = {}, {}, {}
 
         def group_w2(name, src, n, share, at=None):
             if at is None:
@@ -230,17 +231,18 @@ def tile_moe_tk_glu_silu_kernel(tc, xT, w1, w3, w2, gate, offs, pos1, pos2, pos3
             return cw, cs
 
         def group_later(e):
-            at = rows_at(0, LAST) - LAP + GROUPED_BYTES if e == EARLY - 1 else None
+            at = rows_at(0, LAST) - LAP + GROUPED_BYTES if e == WHOLE - 1 else None
             later[e] = group_w2(f"later{e}", whole[e][:, :, BLK:N], N - BLK, 0, at)
 
         def pack_later(e):
-            cw, cs = quantize_w2(f"later{e}", later[e][:], rows_at(0, LAST) - LAP if e == 1 else None)
+            cw, cs = quantize_w2(f"later{e}", later[e][:], rows_at(0, LAST) - LAP if e == WHOLE - 2 else None)
             for r in range(1, ROWS):
                 codes[r, e] = (cw[:, (r - 1) * BLK : r * BLK], cs[:, (r - 1) * BLK : r * BLK])
 
         def pack_rows(r, e):
             share = 0 if (r, e) == (0, LAST) else BLK // 4
-            g = group_w2(f"{r}_{e}", rows[r, e][:] if e in LATE else whole[e][:, :, r * BLK : (r + 1) * BLK], BLK, share, (r - 1) * SPAN + GROUPED_AT[e - EARLY] if r > 0 else None)
+            src = rows[r, e][:] if e in LATE else whole[e][:, :, r * BLK : (r + 1) * BLK]
+            g = group_w2(f"{r}_{e}", src, BLK, share, (r - 1) * SPAN + GROUPED_AT[e - WHOLE] if r > 0 else None)
             cw, cs = quantize_w2(f"{r}_{e}", g[:], *((r * SPAN + WORDS_AT, r * SPAN + SCALES_AT) if e == LAST else ()))
             codes[r, e] = (cw[:], cs[:])
 
@@ -319,7 +321,7 @@ def tile_moe_tk_glu_silu_kernel(tc, xT, w1, w3, w2, gate, offs, pos1, pos2, pos3
         group_later(1)
         pack_rows(0, 2)
         pack_later(0)
-        for e in STEPWISE:
+        for e in LATE:
             pack_rows(0, e)
         group_later(2)
         pack_later(1)
@@ -328,10 +330,10 @@ def tile_moe_tk_glu_silu_kernel(tc, xT, w1, w3, w2, gate, offs, pos1, pos2, pos3
         for r in range(ROWS - 1):
             project(r)
             fetch(scratch[r][:, 0], r, 0, every)
-            pack_rows(r + 1, EARLY)
-            early = tail.tile([P, T // 2], F32, name=f"early{r}", offset=rows_at(r + 1, EARLY))
+            pack_rows(r + 1, LATE[0])
+            early = tail.tile([P, T // 2], F32, name=f"early{r}", offset=rows_at(r + 1, LATE[0]))
             fetch(early[:], r, 1, low)
-            for e in STEPWISE[1:]:
+            for e in LATE[1:]:
                 pack_rows(r + 1, e)
             rest = tail.tile([P, 3, T // 2], F32, name=f"rest{r}", offset=rows_at(r + 1, LAST - 1) + ROW_BYTES // 2)
             fetch(rest[:, 0], r, 1, high)
@@ -342,19 +344,20 @@ def tile_moe_tk_glu_silu_kernel(tc, xT, w1, w3, w2, gate, offs, pos1, pos2, pos3
         project(last)
         turned[0] = slab.tile([P, T], F32, name="turned0", offset=raw_at(LAST, 1) + RAW_BYTES // 2 + 5 * C)[:]
         turned[1] = scratch[1][:, 1]
-        add_turned(0, (0, 1, 2, 3), 4)
-        add_turned(1, (0, 1), 6)
-        add_turned(1, (2, 3), 7)
-        turn_back(0, (0, 1, 2, 3), 5)
-        turn_back(1, (0, 1), 4)
-        turn_back(1, (2, 3), 0)
+        add_turned(*SUMS[0])
+        picked = work.tile([P, T], F32, name="picked", bufs=1)
+        nc.scalar.activation(picked[:], ys[last][:].indirect(pos_sb[TOP - 1][:]), COPY)
+        for r, blocks, at in SUMS[1:]:
+            add_turned(r, blocks, at)
+        for r, blocks, at in BACKS:
+            turn_back(r, blocks, at)
         prod = scratch[last]
         res = work.tile([P, T], F32, name="res", bufs=1)
         fetch(prod[:, 0], last, 0, every)
         fetch(prod[:, 1], last, 1, every)
-        fetch(prod[:, 2, low], last, 2, low)
-        nc.vector.tensor_tensor(prod[:, 3], prod[:, 0], prod[:, 1], ADD)
-        fetch(prod[:, 2, high], last, 2, high)
+        nc.vector.tensor_tensor(prod[:, 2], picked[:], gates[TOP - 1][:], MULT)
+        for cols in (low, high):
+            nc.vector.tensor_tensor(prod[:, 3, cols], prod[:, 0, cols], prod[:, 1, cols], ADD)
         for cols in (low, high):
             nc.vector.tensor_tensor(res[:, cols], prod[:, 3, cols], prod[:, 2, cols], ADD)
         nc.sync.dma_start(out=out[last * BLK : (last + 1) * BLK, :], in_=res[:])

from contextlib import ExitStack

import concourse.mybir as mybir

K, T, E, C, H, N = 512, 512, 6, 256, 512, 384
TOP = 3
FLOPS = 2 * TOP * T * (2 * K * H + H * N)

F32 = mybir.dt.float32
BF16 = mybir.dt.bfloat16
I32 = mybir.dt.int32
U32 = mybir.dt.uint32
U16 = mybir.dt.uint16
U8 = mybir.dt.uint8
FP8X4 = mybir.dt.float8_e4m3fn_x4
MULT = mybir.AluOpType.mult
ADD = mybir.AluOpType.add
EQUAL = mybir.AluOpType.is_equal
SILU = mybir.ActivationFunctionType.Silu
COPY = mybir.ActivationFunctionType.Copy

P = 128
BLK = 128
S = E * C
ROWS = N // BLK
LAST = E - 1
WINDOW = 2 * T

WHOLE = 3
LATE = range(WHOLE, E)

X_SCALAR = 44
W3_SECOND_SCALAR = 80
VECTOR_PIECE = 64

RAW_BYTES = 4 * H * 4
ROW_BYTES = T * 4
Y_BYTES = S * 4
GROUPED_BYTES = 4 * BLK * 2
WORDS_BYTES = BLK * 4
BANK_BYTES = 2048

LAP = 64
WORDS_AT = GROUPED_BYTES - LAP
SCALES_AT = 2 * GROUPED_BYTES + WORDS_BYTES - 2 * LAP
GROUPED_AT = (0, WORDS_AT + WORDS_BYTES - LAP, SCALES_AT + BLK - LAP)
ROWS_AT = 3 * GROUPED_BYTES + WORDS_BYTES + BLK
SPAN = ROWS_AT + len(LATE) * (ROW_BYTES + LAP) + Y_BYTES

PARTS = ((0, 1), (2, 3), (4,), (5,))
SUMS = ((0, (0, 1, 2, 3), 4), (1, (0, 1), 6), (1, (2, 3), 7))
BACKS = ((0, (0, 1, 2, 3), 5), (1, (0, 1), 4), (1, (2, 3), 0))


def tile_moe_tk_glu_silu_kernel(tc, xT, w1, w3, w2, gate, offs, pos1, pos2, pos3, out):
    nc = tc.nc
    with ExitStack() as ctx:
        lists = ctx.enter_context(tc.tile_pool(name="lists", bufs=1))
        keep = ctx.enter_context(tc.tile_pool(name="keep", bufs=1))
        slab = ctx.enter_context(tc.tile_pool(name="slab", bufs=1))
        work = ctx.enter_context(tc.tile_pool(name="work", bufs=2))
        tail = ctx.enter_context(tc.tile_pool(name="tail", bufs=1))
        psum = ctx.enter_context(tc.psum_pool(name="psum", bufs=1))

        offs_sb = lists.tile([P, S // 16], U16, name="offs_sb")
        pos_sb = [lists.tile([P, T // 16], U16, name=f"pos_sb{k}") for k in range(TOP)]

        gate_rows = keep.tile([P, BLK], F32, name="gate_rows")
        nc.vector.memset(gate_rows[:], 0.0)
        pieces = gate.rearrange("k n (b c) -> (k n b) c", c=BLK)
        ident = keep.tile([P, P], F32, name="ident")
        nc.vector.memset(ident[:], 0.0)
        ones = keep.tile([P, 32], F32, name="ones", align_bytes=64)
        nc.vector.memset(ones[:], 1.0)
        count = keep.tile([P, 32], F32, name="count", align_bytes=64)
        nc.vector.tensor_tensor_scan(count[:], ones[:], ones[:], 0.0, MULT, ADD)
        lane = keep.tile([P, 32], F32, name="lane", align_bytes=64)
        nc.vector.transpose(lane[:], count[:])
        for q in range(0, P, 32):
            nc.vector.tensor_tensor(ident[q : q + 32, q : q + 32], count[q : q + 32, :], lane[q : q + 32, :], EQUAL)
        warm = keep.tile([P, 1], F32, name="warm")
        nc.scalar.activation(warm[:], ones[:, 0:1], SILU)
        xs = keep.tile([P, WINDOW], U8, name="xs", align_bytes=64)
        nc.vector.memset(xs[:].bitcast(I32), 0)
        xw = keep.tile([P, WINDOW], U32, name="xw", align_bytes=64)
        nc.vector.memset(xw[:, T:].bitcast(I32), 0)

        x_raw = slab.tile([P, 4, T], F32, name="x_raw", offset=0)
        nc.sync.dma_start(out=x_raw[:], in_=xT.rearrange("(p j) t -> p j t", j=4))
        nc.sync.dma_start(out=gate_rows[0 : 4 * TOP, :], in_=pieces[0 : (4 * TOP - 1) * (N + 1) + 1 : N + 1, :])
        nc.sync.dma_start(offs_sb[:], offs)
        raw, whole, rows, gates = {}, {}, {}, {}

        def raw_at(e, i):
            return (2 * e + i + 1) * RAW_BYTES

        def whole_at(e):
            return ROWS * SPAN + e * Y_BYTES

        def rows_at(r, e):
            place = e - WHOLE if r > 0 else (e - LAST) % len(LATE)
            return r * SPAN + ROWS_AT + place * (ROW_BYTES + LAP)

        def load_rows(r, e):
            rows[r, e] = tail.tile([P, 4, BLK], F32, name=f"raw2_{r}_{e}", offset=rows_at(r, e))
            nc.sync.dma_start(out=rows[r, e][:], in_=w2[e].rearrange("(p j) n -> p j n", j=4)[:, :, r * BLK : (r + 1) * BLK])

        def load_pos(k):
            nc.sync.dma_start(pos_sb[k][:], (pos1, pos2, pos3)[k])

        for e in range(E):
            for i, w in enumerate((w1, w3)):
                raw[e, i] = slab.tile([P, 4, H], F32, name=f"raw{e}_{i}", align_bytes=64, offset=raw_at(e, i))
                nc.sync.dma_start(out=raw[e, i][:], in_=w[e].rearrange("(p j) i -> p j i", j=4))
        for e in range(WHOLE):
            whole[e] = tail.tile([P, 4, N], F32, name=f"whole{e}", offset=whole_at(e))
            nc.sync.dma_start(out=whole[e][:], in_=w2[e].rearrange("(p j) n -> p j n", j=4))
        for e in LATE:
            load_rows(0, e)
        for k, e in enumerate(LATE):
            load_pos(k)
            load_rows(1, e)
        for e in LATE:
            load_rows(2, e)

        xg = keep.tile([P, T, 4], BF16, name="xg", align_bytes=64)
        xv = xg[:].rearrange("p (c i) j -> p c j i", i=4)
        xr = x_raw[:].rearrange("p j (c i) -> p c j i", i=4)
        nc.scalar.copy(xv[:, 0:X_SCALAR], xr[:, 0:X_SCALAR])
        nc.vector.tensor_copy(xv[:, X_SCALAR:], xr[:, X_SCALAR:])
        nc.vector.quantize_mx(out=xw[:, 0:T].bitcast(FP8X4), scales=xs[:, 0:T], in_=xg[:].rearrange("p t j -> p (t j)"))

        turned_rows = psum.tile([P, P], F32, name="bank_gate", offset=4 * BANK_BYTES)
        nc.tensor.transpose(turned_rows[:], gate_rows[:], ident[:])
        gate_cols = keep.tile([P, 4 * TOP], F32, name="gate_cols")
        nc.scalar.copy(gate_cols[:], turned_rows[:, 0 : 4 * TOP])

        def spread_gate(k):
            bank = psum.tile([P, 4, P], F32, name=f"bank_gate{k}", offset=(5 + k) * BANK_BYTES)
            for b in range(4):
                nc.tensor.transpose(bank[:, b, :], gate_cols[:, 4 * k + b : 4 * k + b + 1].to_broadcast([P, P]), ident[:])
            gates[k] = (keep if k == 0 else slab).tile([P, T], F32, name=f"gate{k}", offset=None if k == 0 else raw_at(0, 0) + k * ROW_BYTES)
            nc.scalar.copy(gates[k][:], bank[:].rearrange("p b t -> p (b t)"))

        spread_gate(0)
        gw, gs = {}, {}
        first_at = (2 * E + 1) * RAW_BYTES

        def gather(half):
            pool, at = (keep, None) if half == 0 else (slab, first_at)
            gw[half] = pool.tile([P, S // 2], U32, name=f"gw{half}", align_bytes=64, offset=at)
            gs[half] = pool.tile([P, S // 2], U8, name=f"gs{half}", align_bytes=64, offset=at and at + 2 * S)
            entries = offs_sb[:, half * S // 32 : (half + 1) * S // 32]
            nc.vector.tensor_copy(gw[half][:], xw[:].indirect(entries))
            nc.vector.tensor_copy(gs[half][:], xs[:].indirect(entries))

        gather(0)

        def shared_copy(dst, src, share):
            cut = dst.shape[1] - share
            if share > 0:
                nc.scalar.copy(dst[:, cut:], src[:, cut:])
            for g0 in range(0, cut, VECTOR_PIECE):
                g1 = min(g0 + VECTOR_PIECE, cut)
                nc.vector.tensor_copy(dst[:, g0:g1], src[:, g0:g1])

        grouped, banks, sil, hb, hw, hs = {}, {}, {}, {}, {}, {}

        def group(e, i, share):
            if e + i == 0:
                grouped[e, i] = slab.tile([P, 4 * H], BF16, name="grp_first", align_bytes=64, offset=first_at)
            else:
                grouped[e, i] = work.tile([P, 4 * H], BF16, name=f"grp{e}_{i}", tag="grp", align_bytes=64, bufs=4)
            dst = grouped[e, i][:].rearrange("p (t m g j) -> p m g t j", t=4, g=2, j=2)
            src = raw[e, i][:].rearrange("p (g j) (m t) -> p m g t j", t=4, j=2)
            shared_copy(dst, src, share)

        def first_layer(e, i):
            cw = work.tile([P, H], U32, name=f"cw{e}_{i}", tag="cw", align_bytes=64, bufs=3)
            cs = work.tile([P, H], U8, name=f"cs{e}_{i}", tag="cs", align_bytes=64, bufs=3)
            nc.vector.quantize_mx(out=cw[:].bitcast(FP8X4), scales=cs[:], in_=grouped[e, i][:])
            for c in range(2):
                half, at = divmod(e * C + c * BLK, S // 2)
                slots = slice(at, at + BLK)
                banks[e, i, c] = psum.tile([P, 4, BLK], F32, name=f"bank{e}_{i}_{c}", offset=(4 * (e % 2) + 2 * i + c) * BANK_BYTES)
                for t in range(4):
                    cols = slice(t * BLK, (t + 1) * BLK)
                    nc.tensor.matmul_mx(out=banks[e, i, c][:, t, :], lhsT=cw[:, cols].bitcast(FP8X4), lhsT_scale=cs[:, cols], rhs=gw[half][:, slots].bitcast(FP8X4), rhs_scale=gs[half][:, slots], start=True, stop=True)

        def activate(e):
            room = slab.tile([P, 2, BLK, 4], F32, name=f"sil{e}", offset=raw_at(e, 1) if e > 0 else raw_at(1, 0))
            for c in range(2):
                sil[e, c] = room[:, c]
                nc.scalar.activation(sil[e, c], banks[e, 0, c][:].rearrange("p t s -> p s t"), SILU)

        def hidden_tile(e):
            if 0 < e < LAST:
                hb[e] = raw[e + 1, 0][:, 0, :].bitcast(BF16).rearrange("p (s t) -> p s t", t=4)
            elif e == 0:
                hb[e] = keep.tile([P, C, 4], BF16, name="hb0", align_bytes=64)
            else:
                flat = whole[0][:].rearrange("p j n -> p (j n)")
                hb[e] = flat[:, BLK : BLK + 2 * C].bitcast(BF16).rearrange("p (s t) -> p s t", t=4)

        def hidden(e, c):
            nc.vector.tensor_tensor(hb[e][:, c * BLK : (c + 1) * BLK, :], banks[e, 1, c][:].rearrange("p t s -> p s t"), sil[e, c], MULT)

        def quantize_h(e):
            at = raw_at(min(e + 1, LAST), 1) + RAW_BYTES // 2
            if e == LAST:
                at = at + 5 * C
            hw[e] = slab.tile([P, C], U32, name=f"hw{e}", align_bytes=64, offset=at)
            hs[e] = slab.tile([P, C], U8, name=f"hs{e}", align_bytes=64, offset=at + 4 * C)
            nc.vector.quantize_mx(out=hw[e][:].bitcast(FP8X4), scales=hs[e][:], in_=hb[e][:].rearrange("p s t -> p (s t)"))

        ys, codes, later = {}, {}, {}

        def group_w2(name, src, n, share, at=None):
            if at is None:
                g = work.tile([P, n, 4], BF16, name=f"grp2_{name}", tag=f"grp2_{n}", align_bytes=64, bufs=4 if n == BLK else 2)
            else:
                g = tail.tile([P, n, 4], BF16, name=f"grp2_{name}", align_bytes=64, offset=at)
            shared_copy(g[:].rearrange("p (c i) j -> p c j i", i=4), src.rearrange("p j (c i) -> p c j i", i=4), share)
            return g

        def quantize_w2(name, g, at=None, scales_at=None):
            n = g.shape[1]
            cw = (keep if at is None else tail).tile([P, n], U32, name=f"w2w{name}", align_bytes=64, offset=at)
            cs = (keep if scales_at is None else tail).tile([P, n], U8, name=f"w2s{name}", align_bytes=64, offset=scales_at)
            nc.vector.quantize_mx(out=cw[:].bitcast(FP8X4), scales=cs[:], in_=g.rearrange("p n j -> p (n j)"))
            return cw, cs

        def group_later(e):
            at = rows_at(0, LAST) - LAP + GROUPED_BYTES if e == WHOLE - 1 else None
            later[e] = group_w2(f"later{e}", whole[e][:, :, BLK:N], N - BLK, 0, at)

        def pack_later(e):
            cw, cs = quantize_w2(f"later{e}", later[e][:], rows_at(0, LAST) - LAP if e == WHOLE - 2 else None)
            for r in range(1, ROWS):
                codes[r, e] = (cw[:, (r - 1) * BLK : r * BLK], cs[:, (r - 1) * BLK : r * BLK])

        def pack_rows(r, e):
            share = 0 if (r, e) == (0, LAST) else BLK // 4
            src = rows[r, e][:] if e in LATE else whole[e][:, :, r * BLK : (r + 1) * BLK]
            g = group_w2(f"{r}_{e}", src, BLK, share, (r - 1) * SPAN + GROUPED_AT[e - WHOLE] if r > 0 else None)
            cw, cs = quantize_w2(f"{r}_{e}", g[:], *((r * SPAN + WORDS_AT, r * SPAN + SCALES_AT) if e == LAST else ()))
            codes[r, e] = (cw[:], cs[:])

        def project(r):
            ys[r] = tail.tile([P, S], F32, name=f"y{r}", offset=rows_at(r, LAST if r > 0 else LAST - 1) + ROW_BYTES - LAP)
            for j, experts in enumerate(PARTS):
                bank = psum.tile([P, len(experts), C], F32, name=f"bank_y{r}_{j}", offset=(4 * (r % 2) + j) * BANK_BYTES)
                for u, e in enumerate(experts):
                    cw, cs = codes[r, e]
                    nc.tensor.matmul_mx(out=bank[:, u, :], lhsT=cw.bitcast(FP8X4), lhsT_scale=cs, rhs=hw[e][:].bitcast(FP8X4), rhs_scale=hs[e][:], start=True, stop=True)
                nc.scalar.copy(ys[r][:, experts[0] * C : (experts[-1] + 1) * C], bank[:].rearrange("p u s -> p (u s)"))

        prods, turned = {}, {}
        scratch = [slab.tile([P, 4, T], F32, name=f"scratch{r}", offset=raw_at(r + 1, 0)) for r in range(ROWS)]

        low, high, every = slice(0, T // 2), slice(T // 2, T), slice(0, T)

        def fetch(dst, r, k, cols):
            nc.vector.tensor_tensor(dst, ys[r][:].indirect(pos_sb[k][:, cols.start // 16 : cols.stop // 16]), gates[k][:, cols], MULT)
            for u, b in enumerate(range(cols.start // BLK, cols.stop // BLK)):
                prods[r, k, b] = dst[:, u * BLK : (u + 1) * BLK]

        def add_turned(r, blocks, at):
            bank = psum.tile([P, len(blocks), BLK], F32, name=f"bank_sum{r}_{blocks[0]}", offset=at * BANK_BYTES)
            for u, b in enumerate(blocks):
                for k in range(TOP):
                    nc.tensor.matmul(bank[:, u, :], prods[r, k, b], ident[:], start=k == 0, stop=k + 1 == TOP, is_transpose=True)
            nc.scalar.copy(turned[r][:, blocks[0] * BLK : (blocks[-1] + 1) * BLK], bank[:].rearrange("p b n -> p (b n)"))

        def turn_back(r, blocks, at):
            bank = psum.tile([P, len(blocks), BLK], F32, name=f"bank_back{r}_{blocks[0]}", offset=at * BANK_BYTES)
            for u, b in enumerate(blocks):
                nc.tensor.transpose(bank[:, u, :], turned[r][:, b * BLK : (b + 1) * BLK], ident[:])
            cols = slice(blocks[0] * BLK, (blocks[-1] + 1) * BLK)
            nc.scalar.copy(scratch[r][:, 3, cols], bank[:].rearrange("p b t -> p (b t)"))
            if cols.stop == T:
                nc.scalar.dma_start(out=out[r * BLK : (r + 1) * BLK, :], in_=scratch[r][:, 3])

        all_groups = H // 4
        group(0, 0, all_groups)
        for k in range(1, TOP):
            spread_gate(k)
        first_layer(0, 0)
        gather(1)
        group(0, 1, all_groups)
        first_layer(0, 1)
        group(1, 0, all_groups)
        activate(0)
        group(1, 1, W3_SECOND_SCALAR)
        first_layer(1, 0)
        hidden_tile(0)
        for c in range(2):
            hidden(0, c)
        for e in range(1, LAST):
            group(e + 1, 0, 0)
            if e > 1:
                group(e, 1, all_groups)
            activate(e)
            first_layer(e, 1)
            first_layer(e + 1, 0)
            quantize_h(e - 1)
            hidden_tile(e)
            for c in range(2):
                hidden(e, c)
        group(LAST, 1, all_groups)
        activate(LAST)
        first_layer(LAST, 1)
        group_later(0)
        quantize_h(LAST - 1)
        pack_rows(0, 0)
        hidden_tile(LAST)
        for c in range(2):
            hidden(LAST, c)
        pack_rows(0, 1)
        quantize_h(LAST)
        group_later(1)
        pack_rows(0, 2)
        pack_later(0)
        for e in LATE:
            pack_rows(0, e)
        group_later(2)
        pack_later(1)
        pack_later(2)

        for r in range(ROWS - 1):
            project(r)
            fetch(scratch[r][:, 0], r, 0, every)
            pack_rows(r + 1, LATE[0])
            early = tail.tile([P, T // 2], F32, name=f"early{r}", offset=rows_at(r + 1, LATE[0]))
            fetch(early[:], r, 1, low)
            for e in LATE[1:]:
                pack_rows(r + 1, e)
            rest = tail.tile([P, 3, T // 2], F32, name=f"rest{r}", offset=rows_at(r + 1, LAST - 1) + ROW_BYTES // 2)
            fetch(rest[:, 0], r, 1, high)
            fetch(rest[:, 1], r, 2, low)
            fetch(rest[:, 2], r, 2, high)

        last = ROWS - 1
        project(last)
        turned[0] = slab.tile([P, T], F32, name="turned0", offset=raw_at(LAST, 1) + RAW_BYTES // 2 + 5 * C)[:]
        turned[1] = scratch[1][:, 1]
        add_turned(*SUMS[0])
        picked = work.tile([P, T], F32, name="picked", bufs=1)
        nc.scalar.activation(picked[:], ys[last][:].indirect(pos_sb[TOP - 1][:]), COPY)
        for r, blocks, at in SUMS[1:]:
            add_turned(r, blocks, at)
        for r, blocks, at in BACKS:
            turn_back(r, blocks, at)
        prod = scratch[last]
        res = work.tile([P, T], F32, name="res", bufs=1)
        fetch(prod[:, 0], last, 0, every)
        fetch(prod[:, 1], last, 1, every)
        nc.vector.tensor_tensor(prod[:, 2], picked[:], gates[TOP - 1][:], MULT)
        for cols in (low, high):
            nc.vector.tensor_tensor(prod[:, 3, cols], prod[:, 0, cols], prod[:, 1, cols], ADD)
        for cols in (low, high):
            nc.vector.tensor_tensor(res[:, cols], prod[:, 3, cols], prod[:, 2, cols], ADD)
        nc.sync.dma_start(out=out[last * BLK : (last + 1) * BLK, :], in_=res[:])
